import numpy as np
import ml_dtypes


def mxq(x, axis, fmt="e4m3"):
    dtype, down = {"e4m3": (ml_dtypes.float8_e4m3fn, 7), "e5m2": (ml_dtypes.float8_e5m2, 14)}[fmt]
    v = np.moveaxis(np.asarray(x, np.float32).astype(ml_dtypes.bfloat16).astype(np.float64), axis, -1)
    blocks = v.reshape(v.shape[:-1] + (-1, 32))
    amax = np.abs(blocks).max(-1, keepdims=True)
    byte = np.maximum(np.where(amax > 0, np.frexp(amax)[1] - 1 + 127, 0) - down, 1)
    scale = np.exp2(byte - 127.0)
    codes = (blocks / scale).astype(np.float32).astype(dtype).astype(np.float64)
    return np.moveaxis((codes * scale).reshape(v.shape), -1, axis)


WIDE = False


def mx_kscale(k):
    if not WIDE:
        return np.ones(k)
    levels = np.array([10, -10, 5, -5, 0])
    if k % 512:
        return np.exp2(np.random.permutation(np.resize(levels, k // 32))).repeat(32)
    a = np.empty((k // 512, 16))
    for p in range(k // 512):
        a[p, :8] = np.random.permutation(np.resize(levels, 8))
        for g in range(8):
            far = levels[np.abs(levels - a[p, g]) >= 10]
            a[p, g + 8] = far[np.random.randint(len(far))]
    return np.exp2(a.ravel()).repeat(32)


def f64(x):
    return np.asarray(x).astype(np.float64)


def striped(idx):
    return np.tile(idx.reshape(-1, 16).T, (8, 1)).astype(np.uint16)


def unstriped(offs):
    return offs[:16].T.reshape(-1).astype(np.int64)


E2M1 = np.array([0.0, 0.5, 1.0, 1.5, 2.0, 3.0, 4.0, 6.0, -0.0, -0.5, -1.0, -1.5, -2.0, -3.0, -4.0, -6.0])


def pack_weight(w, fmt):
    k, n = w.shape
    w = f64(np.asarray(w, np.float32).astype(ml_dtypes.bfloat16)).reshape(k // 32, 32, n)
    amax = np.abs(w).max(1)
    if fmt == "e4m3":
        byte = np.frexp(amax)[1] - 1 + 127 - 7
    else:
        mant, ex = np.frexp(amax / 6.0)
        byte = np.where(mant > 0.5, ex, ex - 1) + 127
    byte = np.clip(np.where(amax > 0, byte, 1), 1, 254)
    scaled = (w * np.exp2(127.0 - byte)[:, None, :]).reshape(k, n).astype(np.float32)
    by_word = np.ascontiguousarray(scaled.reshape(k // 512, 128, 4, n).transpose(0, 1, 3, 2))
    if fmt == "e4m3":
        words = by_word.astype(ml_dtypes.float8_e4m3fn).view(np.uint8)
    else:
        c = by_word.astype(ml_dtypes.float4_e2m1fn).view(np.uint8) & 0xF
        words = (c[..., 0::2] | (c[..., 1::2] << 4)).reshape(k // 512, 128, 2 * n)
    return np.ascontiguousarray(words), np.ascontiguousarray(byte.astype(np.uint8).reshape(k // 512, 16, n))


def unpack_weight(words, scales, fmt):
    g, _, n = scales.shape
    words = np.ascontiguousarray(words).reshape(g, 128, n, -1)
    if fmt == "e4m3":
        vals = words.view(ml_dtypes.float8_e4m3fn).astype(np.float64)
    else:
        nib = np.empty((g, 128, n, 4), np.uint8)
        nib[..., 0::2] = words & 0xF
        nib[..., 1::2] = words >> 4
        vals = E2M1[nib]
    vals = vals * np.repeat(np.exp2(scales.astype(np.float64) - 127.0), 8, axis=1)[..., None]
    return vals.transpose(0, 1, 3, 2).reshape(g * 512, n)


def gelu(v):
    return 0.5 * v * (1.0 + np.tanh(np.sqrt(2.0 / np.pi) * (v + 0.044715 * v**3)))


def bf(x):
    return np.asarray(x, np.float32).astype(ml_dtypes.bfloat16)

def planes(Y):
    n, m = Y.shape
    b = f64(bf(Y)).reshape(n // 32, 32, m)
    amax = np.abs(b).max(1)
    byte = np.clip(np.where(amax > 0, np.frexp(amax)[1] - 1 + 127 - 7, 1), 1, 254)
    codes = (b * np.exp2(127.0 - byte)[:, None, :]).reshape(n, m).astype(np.float32).astype(ml_dtypes.float8_e4m3fn).view(np.uint8)
    words = codes.reshape(n // 512, 128, 4, m).transpose(0, 1, 3, 2)
    return np.ascontiguousarray(words), np.ascontiguousarray(byte.astype(np.uint8).reshape(n // 512, 16, m))


K, H, T, S, T2, S2 = 1536, 512, 4096, 1024, 4096, 1536

def setup_inputs():
    n = np.random.standard_normal
    s = mx_kscale(K)[:, None]
    u = mx_kscale(H)[:, None]
    tab_words, tab_scales = pack_weight(n((K, T)) * s, "e4m3")
    tab2_words, tab2_scales = pack_weight(1.2 * n((H, T2)) / u / np.sqrt(H), "e4m3")
    w4_words, w4_scales = pack_weight(n((K, H)) / s * u.T / np.sqrt(K), "e2m1")
    wg = (n((K, H)) / s / np.sqrt(K)).astype(np.float32)
    src_scale = np.exp(0.3 * n(S)).astype(np.float32)
    tgt_scale = np.exp(0.8 * n(S2)).astype(np.float32)
    offs = striped(np.random.permutation(T)[:S])
    offs2 = striped(np.random.permutation(T2)[:S2])
    return {"tab_words": tab_words, "tab_scales": tab_scales, "tab2_words": tab2_words, "tab2_scales": tab2_scales,
            "w4_words": w4_words, "w4_scales": w4_scales, "wg": wg, "src_scale": src_scale, "tgt_scale": tgt_scale,
            "offs": offs, "offs2": offs2}

def reference(tab_words, tab_scales, tab2_words, tab2_scales, w4_words, w4_scales, wg, src_scale, tgt_scale, offs, offs2):
    v = unpack_weight(tab_words, tab_scales, "e4m3")[:, unstriped(offs)]
    v2 = unpack_weight(tab2_words, tab2_scales, "e4m3")[:, unstriped(offs2)]
    w4 = unpack_weight(w4_words, w4_scales, "e2m1")
    p = w4.T @ v
    g = mxq(f64(wg), 0, "e4m3").T @ v
    h = p * (1.0 / (1.0 + np.exp(-g)))
    kern = np.exp(v2.T @ mxq(h, 0, "e4m3"))
    y = kern * f64(src_scale)[None, :] * f64(tgt_scale)[:, None]
    words, scales = planes(y)
    return y, words, scales

@@ -1,0 +1,251 @@
+from contextlib import ExitStack
+
+import concourse.mybir as mybir
+from concourse.masks import make_identity
+
+K, H, T, S, T2, S2 = 1536, 512, 4096, 1024, 4096, 1536
+FLOPS = 2 * (2 * K * H * S + H * S2 * S)
+
+F32 = mybir.dt.float32
+BF16 = mybir.dt.bfloat16
+I32 = mybir.dt.int32
+U32 = mybir.dt.uint32
+U16 = mybir.dt.uint16
+U8 = mybir.dt.uint8
+FP8X4 = mybir.dt.float8_e4m3fn_x4
+FP4X4 = mybir.dt.float4_e2m1fn_x4
+ACT = mybir.ActivationFunctionType
+ALU = mybir.AluOpType
+
+P = 128
+PACK = 4
+PASS = P * PACK
+PASSES = K // PASS
+GROUPS = S2 // PASS
+HALF = 512
+HALVES = S // HALF
+CHUNK = 128
+CHUNKS = HALF // CHUNK
+LIST_COLS = HALF // 16
+QUADS = 4
+SHIFT_ROWS = 112
+SCALAR_CAST = [384, 384, 384, 256, 256, 256]
+
+
+def tile_list_transport_plan_lookup_kernel(tc, tab_words, tab_scales, tab2_words, tab2_scales, w4_words,
+                                                    w4_scales, wg, src_scale, tgt_scale, offs, offs2,
+                                                    out_0, out_1, out_2):
+    nc = tc.nc
+    with ExitStack() as ctx:
+        lists = ctx.enter_context(tc.tile_pool(name="lists", bufs=1))
+        keep = ctx.enter_context(tc.tile_pool(name="keep", bufs=1))
+        ring = ctx.enter_context(tc.tile_pool(name="ring", bufs=2))
+        psum = ctx.enter_context(tc.psum_pool(name="psum", bufs=8))
+
+        def kept(name, shape, dtype):
+            return keep.tile(shape, dtype, name=name, align_bytes=64)
+
+        def bank(shape):
+            return psum.tile(shape, F32, name="bank")
+
+        src_list = lists.tile([P, S // 16], U16, name="src_list")
+        tgt_list = lists.tile([P, S2 // 16], U16, name="tgt_list")
+        w4_raw = kept("w4_raw", [P, PASSES, 2 * H // 4], I32)
+        tab = [kept("tab%d" % a, [P, T], I32) for a in range(PASSES)]
+        wg_raw = [kept("wg_raw%d" % a, [P, PACK, H], F32) for a in range(PASSES)]
+        tab2 = kept("tabtwo", [P, T2], I32)
+
+        def load_tab(a):
+            nc.sync.dma_start(out=tab[a][:], in_=tab_words[a].rearrange("p t i -> p (t i)").bitcast(I32))
+
+        def load_wg(a):
+            nc.sync.dma_start(out=wg_raw[a][:],
+                              in_=wg[a * PASS:(a + 1) * PASS, :].rearrange("(p j) c -> p j c", j=PACK))
+
+        nc.sync.dma_start(src_list[:], offs)
+        nc.sync.dma_start(out=w4_raw[:], in_=w4_words.bitcast(I32).rearrange("a p b -> p a b"))
+        load_tab(0)
+        nc.sync.dma_start(tgt_list[:], offs2)
+        load_wg(0)
+        load_tab(1)
+        load_wg(1)
+        load_wg(2)
+        load_tab(2)
+        nc.sync.dma_start(out=tab2[:], in_=tab2_words[0].rearrange("p t i -> p (t i)").bitcast(I32))
+
+        src_rows = kept("src_rows", [P, S // P], F32)
+        tgt = kept("tgt", [P, GROUPS, PACK], F32)
+        nc.scalar.dma_start(out=src_rows[:], in_=src_scale.rearrange("(p c) -> p c", p=P))
+        nc.scalar.dma_start(out=tgt[:], in_=tgt_scale.rearrange("(g p t) -> p g t", p=P, t=PACK))
+
+        tab_sc = kept("tab_sc", [P, T // 4], I32)
+        w4_sc_raw = kept("w4_sc_raw", [P, PASSES, H // 4], I32)
+        tab2_sc = kept("tab2_sc", [P, T2 // 4], I32)
+        nc.vector.memset(tab_sc[:], 0)
+        nc.vector.memset(w4_sc_raw[:], 0)
+        nc.vector.memset(tab2_sc[:], 0)
+        for q in range(QUADS):
+            nc.gpsimd.dma_start(out=tab_sc[32 * q:32 * q + 4 * PASSES, :],
+                                in_=tab_scales.bitcast(I32)[:, 4 * q:4 * q + 4, :])
+        for q in range(QUADS):
+            nc.gpsimd.dma_start(out=w4_sc_raw[32 * q:32 * q + 4, :, :],
+                                in_=w4_scales.bitcast(I32)[:, 4 * q:4 * q + 4, :].rearrange("a r c -> r a c"))
+        for q in range(QUADS):
+            nc.gpsimd.dma_start(out=tab2_sc[32 * q:32 * q + 4, :],
+                                in_=tab2_scales.bitcast(I32)[0, 4 * q:4 * q + 4, :])
+
+        ident = kept("ident", [P, P], F32)
+        make_identity(nc, ident[:])
+        src = kept("src", [P, S], F32)
+        for u in range(2):
+            spread = bank([P, 4, P])
+            for m in range(4):
+                col = 4 * u + m
+                nc.tensor.transpose(spread[:, m, :], src_rows[:, col:col + 1].to_broadcast([P, P]), ident[:])
+            nc.scalar.copy(out=src[:].rearrange("p (n u m) -> p u n m", u=2, m=4)[:, u],
+                           in_=spread[:].rearrange("p m n -> p n m"))
+
+        w4 = kept("w4", [P, PASSES, 2 * H], U8)
+        nc.vector.tensor_copy(out=w4[:].bitcast(U16).rearrange("p a (t m) -> p a t m", t=PACK),
+                              in_=w4_raw[:].bitcast(U16).rearrange("p a (m t) -> p a t m", t=PACK))
+
+        v_sc = [kept("v_sc%d" % a, [P, S], U8) for a in range(PASSES)]
+        nc.vector.tensor_copy(v_sc[0][:], tab_sc[:].bitcast(U8).indirect(src_list[:]))
+        for a in range(1, PASSES):
+            nc.vector.memset(v_sc[a][:].bitcast(I32), 0)
+            nc.scalar.dma_start(out=v_sc[a][0:SHIFT_ROWS, :].bitcast(I32),
+                                in_=v_sc[0][4 * a:4 * a + SHIFT_ROWS, :].bitcast(I32))
+
+        w4_sc = kept("w4_sc", [P, PASSES, H], U8)
+        nc.vector.tensor_copy(out=w4_sc[:].rearrange("p a (t m) -> p a t m", t=PACK),
+                              in_=w4_sc_raw[:].bitcast(U8).rearrange("p a (m t) -> p a t m", t=PACK))
+
+        v = [[kept("v%d_%d" % (a, h), [P, HALF], U32) for h in range(HALVES)] for a in range(PASSES)]
+        wg_q = [kept("wg_q%d" % a, [P, H], U32) for a in range(PASSES)]
+        wg_sc = [kept("wg_sc%d" % a, [P, H], U8) for a in range(PASSES)]
+
+        def gather_sources(a, h):
+            nc.vector.tensor_copy(v[a][h][:],
+                                  tab[a][:].bitcast(U32).indirect(src_list[:, h * LIST_COLS:(h + 1) * LIST_COLS]))
+
+        def quantise_wg(a):
+            rounded = ring.tile([P, PACK * H], BF16, name="wg_bf", align_bytes=64)
+            nc.scalar.copy(out=rounded[:].rearrange("p (t m j) -> p m j t", t=PACK, j=PACK),
+                           in_=wg_raw[a][:].rearrange("p j (m t) -> p m j t", t=PACK))
+            nc.vector.quantize_mx(out=wg_q[a][:].bitcast(FP8X4), scales=wg_sc[a][:], in_=rounded[:])
+
+        def project(p_bank, g_bank, a, h, c):
+            cols = slice(c * CHUNK, (c + 1) * CHUNK)
+            sc_cols = slice(h * HALF + c * CHUNK, h * HALF + (c + 1) * CHUNK)
+            for t in range(PACK):
+                nc.tensor.matmul_mx(
+                    out=g_bank[:, t, :],
+                    lhsT=wg_q[a][:, t * P:(t + 1) * P].bitcast(FP8X4), lhsT_scale=wg_sc[a][:, t * P:(t + 1) * P],
+                    rhs=v[a][h][:, cols].bitcast(FP8X4), rhs_scale=v_sc[a][:, sc_cols],
+                    start=(a == 0 and t == 0), stop=(a == PASSES - 1 and t == PACK - 1))
+            for t in range(PACK):
+                nc.tensor.matmul_mx(
+                    out=p_bank[:, t, :],
+                    lhsT=w4[:, a, 2 * t * P:2 * (t + 1) * P].bitcast(FP4X4), lhsT_scale=w4_sc[:, a, t * P:(t + 1) * P],
+                    rhs=v[a][h][:, cols].bitcast(FP8X4), rhs_scale=v_sc[a][:, sc_cols],
+                    start=(a == 0 and t == 0), stop=(a == PASSES - 1 and t == PACK - 1))
+
+        h_bf = [kept("h_bf%d" % h, [P, HALF, PACK], BF16) for h in range(HALVES)]
+        h_q = [kept("h_q%d" % h, [P, HALF], U32) for h in range(HALVES)]
+        h_sc = [kept("h_sc%d" % h, [P, HALF], U8) for h in range(HALVES)]
+
+        def gate(p_bank, g_bank, h, c):
+            th = ring.tile([P, CHUNK, PACK], F32, name="tanh", bufs=3)
+            nc.scalar.activation(out=th[:], in_=g_bank[:].rearrange("p t n -> p n t"), func=ACT.Tanh, scale=0.5)
+            nc.vector.scalar_tensor_tensor(out=h_bf[h][:, c * CHUNK:(c + 1) * CHUNK, :], in0=th[:], scalar=1.0,
+                                           in1=p_bank[:].rearrange("p t n -> p n t"), op0=ALU.add, op1=ALU.mult)
+
+        def quantise_h(h):
+            nc.vector.quantize_mx(out=h_q[h][:].bitcast(FP8X4), scales=h_sc[h][:],
+                                  in_=h_bf[h][:].rearrange("p i t -> p (i t)"))
+
+        v2 = [kept("tgt_words%d" % g, [P, PACK, P], U32) for g in range(GROUPS)]
+        v2_sc = [kept("tgt_sc%d" % g, [P, PACK, P], U8) for g in range(GROUPS)]
+
+        def gather_target_scales(g):
+            picked = ring.tile([P, PASS], U8, name="picked_sc", align_bytes=64)
+            nc.vector.tensor_copy(picked[:],
+                                  tab2_sc[:].bitcast(U8).indirect(tgt_list[:, g * LIST_COLS:(g + 1) * LIST_COLS]))
+            nc.vector.tensor_copy(out=v2_sc[g][:], in_=picked[:].rearrange("p (m t) -> p t m", t=PACK))
+
+        def gather_targets(g):
+            picked = ring.tile([P, PASS], U32, name="picked", align_bytes=64)
+            nc.vector.tensor_copy(picked[:],
+                                  tab2[:].bitcast(U32).indirect(tgt_list[:, g * LIST_COLS:(g + 1) * LIST_COLS]))
+            nc.vector.tensor_copy(out=v2[g][:].rearrange("p t (c m) -> p c t m", m=4),
+                                  in_=picked[:].rearrange("p (c m t) -> p c t m", m=4, t=PACK))
+
+        y_sc = kept("y_sc", [P, GROUPS, S], U8)
+
+        def plan(h, g):
+            cols = slice(h * HALF, (h + 1) * HALF)
+            y = ring.tile([P, PACK, HALF], F32, name="y", bufs=3)
+            for t in range(PACK):
+                s_bank = bank([P, HALF])
+                nc.tensor.matmul_mx(out=s_bank[:], lhsT=v2[g][:, t, :].bitcast(FP8X4), lhsT_scale=v2_sc[g][:, t, :],
+                                    rhs=h_q[h][:].bitcast(FP8X4), rhs_scale=h_sc[h][:], start=True, stop=True)
+                kern = ring.tile([P, HALF], F32, name="kern", bufs=6)
+                nc.scalar.activation(out=kern[:], in_=s_bank[:], func=ACT.Exp, scale=0.5)
+                nc.vector.scalar_tensor_tensor(out=y[:, t, :], in0=kern[:], scalar=tgt[:, g, t:t + 1],
+                                               in1=src[:, cols], op0=ALU.mult, op1=ALU.mult)
+            nc.sync.dma_start(out=out_0[g * PASS:(g + 1) * PASS, cols].rearrange("(p t) i -> p t i", t=PACK), in_=y[:])
+            return y
+
+        def planes(h, g, y):
+            cols = slice(h * HALF, (h + 1) * HALF)
+            y_bf = ring.tile([P, HALF, PACK], BF16, name="y_bf", bufs=3, align_bytes=64)
+            cut = SCALAR_CAST[h * GROUPS + g]
+            nc.scalar.copy(out=y_bf[:, 0:cut, :].rearrange("p (c i) t -> p c t i", i=4),
+                           in_=y[:, :, 0:cut].rearrange("p t (c i) -> p c t i", i=4))
+            nc.vector.tensor_copy(out=y_bf[:, cut:HALF, :].rearrange("p (c i) t -> p c t i", i=4),
+                                  in_=y[:, :, cut:HALF].rearrange("p t (c i) -> p c t i", i=4))
+            y_q = ring.tile([P, HALF], U32, name="y_q", bufs=3, align_bytes=64)
+            nc.vector.quantize_mx(out=y_q[:].bitcast(FP8X4), scales=y_sc[:, g, cols],
+                                  in_=y_bf[:].rearrange("p i t -> p (i t)"))
+            nc.sync.dma_start(out=out_1[g].rearrange("p m t -> p (m t)").bitcast(I32)[:, cols], in_=y_q[:].bitcast(I32))
+
+        banks = [(bank([P, PACK, CHUNK]), bank([P, PACK, CHUNK])) for c in range(CHUNKS)]
+        for a in range(PASSES):
+            gather_sources(a, 0)
+            quantise_wg(a)
+            for c in range(CHUNKS):
+                project(banks[c][0], banks[c][1], a, 0, c)
+                if a == PASSES - 1:
+                    gate(banks[c][0], banks[c][1], 0, c)
+            gather_sources(a, 1)
+            if a == 1:
+                for g in range(GROUPS):
+                    gather_target_scales(g)
+        quantise_h(0)
+
+        def second_half_chunk(c):
+            p_bank, g_bank = bank([P, PACK, CHUNK]), bank([P, PACK, CHUNK])
+            for a in range(PASSES):
+                project(p_bank, g_bank, a, 1, c)
+            gate(p_bank, g_bank, 1, c)
+
+        second_half_chunk(0)
+        second_half_chunk(1)
+        gather_targets(0)
+        y_prev = plan(0, 0)
+        gather_targets(1)
+        second_half_chunk(2)
+        units = [(h, g) for h in range(HALVES) for g in range(GROUPS)]
+        for n in range(1, len(units)):
+            y_now = plan(*units[n])
+            planes(*units[n - 1], y_prev)
+            y_prev = y_now
+            if n == 1:
+                gather_targets(2)
+                second_half_chunk(3)
+                quantise_h(1)
+        planes(*units[-1], y_prev)
+
+        for q in range(QUADS):
+            nc.sync.dma_start(out=out_2.bitcast(I32)[:, 4 * q:4 * q + 4, :].rearrange("g r m -> r g m"),
+                              in_=y_sc[32 * q:32 * q + 4, :, :].bitcast(I32))

@@ -28,8 +28,8 @@ CHUNK = 128
 CHUNKS = HALF // CHUNK
 LIST_COLS = HALF // 16
 QUADS = 4
-SHIFT_ROWS = 112
-SCALAR_CAST = [384, 384, 384, 256, 256, 256]
+ROW0 = P - 16 * PASSES
+CAST_CUTS = [(320, 512)] * 5 + [(128, 288)]
 
 
 def tile_list_transport_plan_lookup_kernel(tc, tab_words, tab_scales, tab2_words, tab2_scales, w4_words,
@@ -51,74 +51,70 @@ def tile_list_transport_plan_lookup_kernel(tc, tab_words, tab_scales, tab2_words
         src_list = lists.tile([P, S // 16], U16, name="src_list")
         tgt_list = lists.tile([P, S2 // 16], U16, name="tgt_list")
         w4_raw = kept("w4_raw", [P, PASSES, 2 * H // 4], I32)
-        tab = [kept("tab%d" % a, [P, T], I32) for a in range(PASSES)]
-        wg_raw = [kept("wg_raw%d" % a, [P, PACK, H], F32) for a in range(PASSES)]
-        tab2 = kept("tabtwo", [P, T2], I32)
+        tab, wg_raw = [], []
 
-        def load_tab(a):
-            nc.sync.dma_start(out=tab[a][:], in_=tab_words[a].rearrange("p t i -> p (t i)").bitcast(I32))
+        def load_words(words, place):
+            window = kept(place, [P, T], I32)
+            nc.sync.dma_start(out=window[:], in_=words.rearrange("p t i -> p (t i)").bitcast(I32))
+            return window
 
-        def load_wg(a):
-            nc.sync.dma_start(out=wg_raw[a][:],
-                              in_=wg[a * PASS:(a + 1) * PASS, :].rearrange("(p j) c -> p j c", j=PACK))
+        def load_wg(a, place):
+            raw = kept(place, [P, PACK, H], F32)
+            nc.sync.dma_start(out=raw[:], in_=wg[a * PASS:(a + 1) * PASS, :].rearrange("(p j) c -> p j c", j=PACK))
+            return raw
 
-        nc.sync.dma_start(src_list[:], offs)
-        nc.sync.dma_start(out=w4_raw[:], in_=w4_words.bitcast(I32).rearrange("a p b -> p a b"))
-        load_tab(0)
-        nc.sync.dma_start(tgt_list[:], offs2)
-        load_wg(0)
-        load_tab(1)
-        load_wg(1)
-        load_wg(2)
-        load_tab(2)
-        nc.sync.dma_start(out=tab2[:], in_=tab2_words[0].rearrange("p t i -> p (t i)").bitcast(I32))
 
-        src_rows = kept("src_rows", [P, S // P], F32)
+        src_cols = kept("src_cols", [P, S // P], F32)
         tgt = kept("tgt", [P, GROUPS, PACK], F32)
-        nc.scalar.dma_start(out=src_rows[:], in_=src_scale.rearrange("(p c) -> p c", p=P))
-        nc.scalar.dma_start(out=tgt[:], in_=tgt_scale.rearrange("(g p t) -> p g t", p=P, t=PACK))
-
-        tab_sc = kept("tab_sc", [P, T // 4], I32)
-        w4_sc_raw = kept("w4_sc_raw", [P, PASSES, H // 4], I32)
+        tab_sc = kept("place_c", [P, T // 4], I32)
+        w4_sc_raw = kept("place_b", [P, H // 4], I32)
         tab2_sc = kept("tab2_sc", [P, T2 // 4], I32)
-        nc.vector.memset(tab_sc[:], 0)
-        nc.vector.memset(w4_sc_raw[:], 0)
+
+        nc.scalar.dma_start(out=tab_sc[ROW0:P, :], in_=tab_scales.bitcast(I32).rearrange("a q c -> q a c"))
+        nc.scalar.dma_start(out=w4_sc_raw[ROW0:P, :], in_=w4_scales.bitcast(I32).rearrange("a q c -> q a c"))
+        with nc.allow_non_contiguous_dma(reason="one value a partition"):
+            nc.scalar.dma_start(out=src_cols[:], in_=src_scale.rearrange("(c p) -> p c", p=P))
+        nc.scalar.dma_start(out=tgt[:], in_=tgt_scale.rearrange("(g p t) -> p g t", p=P, t=PACK))
+        nc.sync.dma_start(src_list[:], offs)
+        nc.sync.dma_start(tgt_list[:], offs2)
+        nc.sync.dma_start(out=w4_raw[:], in_=w4_words.bitcast(I32).rearrange("a p b -> p a b"))
+        wg_raw.append(load_wg(0, "wg_first"))
+        tab.append(load_words(tab_words[0], "place_a"))
+
         nc.vector.memset(tab2_sc[:], 0)
-        for q in range(QUADS):
-            nc.gpsimd.dma_start(out=tab_sc[32 * q:32 * q + 4 * PASSES, :],
-                                in_=tab_scales.bitcast(I32)[:, 4 * q:4 * q + 4, :])
-        for q in range(QUADS):
-            nc.gpsimd.dma_start(out=w4_sc_raw[32 * q:32 * q + 4, :, :],
-                                in_=w4_scales.bitcast(I32)[:, 4 * q:4 * q + 4, :].rearrange("a r c -> r a c"))
+        nc.vector.memset(tab_sc[0:ROW0, :], 0)
+        nc.vector.memset(w4_sc_raw[0:ROW0, :], 0)
         for q in range(QUADS):
             nc.gpsimd.dma_start(out=tab2_sc[32 * q:32 * q + 4, :],
                                 in_=tab2_scales.bitcast(I32)[0, 4 * q:4 * q + 4, :])
+        sc = kept("sc", [P, PASSES, S + H], U8)
+        nc.vector.memset(sc[:].bitcast(I32), 0)
 
         ident = kept("ident", [P, P], F32)
         make_identity(nc, ident[:])
-        src = kept("src", [P, S], F32)
-        for u in range(2):
-            spread = bank([P, 4, P])
-            for m in range(4):
-                col = 4 * u + m
-                nc.tensor.transpose(spread[:, m, :], src_rows[:, col:col + 1].to_broadcast([P, P]), ident[:])
-            nc.scalar.copy(out=src[:].rearrange("p (n u m) -> p u n m", u=2, m=4)[:, u],
-                           in_=spread[:].rearrange("p m n -> p n m"))
 
+        def spread_src(h):
+            spread = bank([P, CHUNKS, CHUNK])
+            for c in range(CHUNKS):
+                col = h * CHUNKS + c
+                nc.tensor.transpose(spread[:, c, :], src_cols[:, col:col + 1].to_broadcast([P, P]), ident[:])
+            return spread
+
+        picked_src_sc = kept("place_d", [P, S], U8)
+        nc.vector.tensor_copy(picked_src_sc[:], tab_sc[:].bitcast(U8).indirect(src_list[:]))
+        rows = kept("rows", [P, S + H], U8)
+        nc.vector.tensor_copy(out=rows[:, S:S + H].rearrange("p (t m) -> p t m", t=PACK),
+                              in_=w4_sc_raw[:].bitcast(U8).rearrange("p (m t) -> p t m", t=PACK))
+        wg_raw.append(load_wg(1, "place_b"))
+        wg_raw.append(load_wg(2, "place_c"))
+        nc.vector.tensor_copy(out=rows[:, 0:S].bitcast(I32), in_=picked_src_sc[:].bitcast(I32))
+        for q in range(QUADS):
+            nc.sync.dma_start(out=sc[32 * q:32 * q + 4, :, :].bitcast(I32),
+                              in_=rows[ROW0 + 12 * q:ROW0 + 12 * (q + 1), :].bitcast(I32))
+        tab.append(load_words(tab_words[1], "place_d"))
         w4 = kept("w4", [P, PASSES, 2 * H], U8)
         nc.vector.tensor_copy(out=w4[:].bitcast(U16).rearrange("p a (t m) -> p a t m", t=PACK),
                               in_=w4_raw[:].bitcast(U16).rearrange("p a (m t) -> p a t m", t=PACK))
-
-        v_sc = [kept("v_sc%d" % a, [P, S], U8) for a in range(PASSES)]
-        nc.vector.tensor_copy(v_sc[0][:], tab_sc[:].bitcast(U8).indirect(src_list[:]))
-        for a in range(1, PASSES):
-            nc.vector.memset(v_sc[a][:].bitcast(I32), 0)
-            nc.scalar.dma_start(out=v_sc[a][0:SHIFT_ROWS, :].bitcast(I32),
-                                in_=v_sc[0][4 * a:4 * a + SHIFT_ROWS, :].bitcast(I32))
-
-        w4_sc = kept("w4_sc", [P, PASSES, H], U8)
-        nc.vector.tensor_copy(out=w4_sc[:].rearrange("p a (t m) -> p a t m", t=PACK),
-                              in_=w4_sc_raw[:].bitcast(U8).rearrange("p a (m t) -> p a t m", t=PACK))
 
         v = [[kept("v%d_%d" % (a, h), [P, HALF], U32) for h in range(HALVES)] for a in range(PASSES)]
         wg_q = [kept("wg_q%d" % a, [P, H], U32) for a in range(PASSES)]
@@ -130,8 +126,8 @@ def tile_list_transport_plan_lookup_kernel(tc, tab_words, tab_scales, tab2_words
 
         def quantise_wg(a):
             rounded = ring.tile([P, PACK * H], BF16, name="wg_bf", align_bytes=64)
-            nc.scalar.copy(out=rounded[:].rearrange("p (t m j) -> p m j t", t=PACK, j=PACK),
-                           in_=wg_raw[a][:].rearrange("p j (m t) -> p m j t", t=PACK))
+            nc.scalar.copy(out=rounded[:].rearrange("p (t m j) -> p t m j", t=PACK, j=PACK),
+                           in_=wg_raw[a][:].rearrange("p j (m t) -> p t m j", t=PACK))
             nc.vector.quantize_mx(out=wg_q[a][:].bitcast(FP8X4), scales=wg_sc[a][:], in_=rounded[:])
 
         def project(p_bank, g_bank, a, h, c):
@@ -141,13 +137,13 @@ def tile_list_transport_plan_lookup_kernel(tc, tab_words, tab_scales, tab2_words
                 nc.tensor.matmul_mx(
                     out=g_bank[:, t, :],
                     lhsT=wg_q[a][:, t * P:(t + 1) * P].bitcast(FP8X4), lhsT_scale=wg_sc[a][:, t * P:(t + 1) * P],
-                    rhs=v[a][h][:, cols].bitcast(FP8X4), rhs_scale=v_sc[a][:, sc_cols],
+                    rhs=v[a][h][:, cols].bitcast(FP8X4), rhs_scale=sc[:, a, sc_cols],
                     start=(a == 0 and t == 0), stop=(a == PASSES - 1 and t == PACK - 1))
             for t in range(PACK):
                 nc.tensor.matmul_mx(
                     out=p_bank[:, t, :],
-                    lhsT=w4[:, a, 2 * t * P:2 * (t + 1) * P].bitcast(FP4X4), lhsT_scale=w4_sc[:, a, t * P:(t + 1) * P],
-                    rhs=v[a][h][:, cols].bitcast(FP8X4), rhs_scale=v_sc[a][:, sc_cols],
+                    lhsT=w4[:, a, 2 * t * P:2 * (t + 1) * P].bitcast(FP4X4), lhsT_scale=sc[:, a, S + t * P:S + (t + 1) * P],
+                    rhs=v[a][h][:, cols].bitcast(FP8X4), rhs_scale=sc[:, a, sc_cols],
                     start=(a == 0 and t == 0), stop=(a == PASSES - 1 and t == PACK - 1))
 
         h_bf = [kept("h_bf%d" % h, [P, HALF, PACK], BF16) for h in range(HALVES)]
@@ -192,35 +188,45 @@ def tile_list_transport_plan_lookup_kernel(tc, tab_words, tab_scales, tab2_words
                 kern = ring.tile([P, HALF], F32, name="kern", bufs=6)
                 nc.scalar.activation(out=kern[:], in_=s_bank[:], func=ACT.Exp, scale=0.5)
                 nc.vector.scalar_tensor_tensor(out=y[:, t, :], in0=kern[:], scalar=tgt[:, g, t:t + 1],
-                                               in1=src[:, cols], op0=ALU.mult, op1=ALU.mult)
-            nc.sync.dma_start(out=out_0[g * PASS:(g + 1) * PASS, cols].rearrange("(p t) i -> p t i", t=PACK), in_=y[:])
+                                               in1=src[h][:].rearrange("p c n -> p (c n)"), op0=ALU.mult, op1=ALU.mult)
+                if t % 2 == 1:
+                    rows_out = out_0[g * PASS:(g + 1) * PASS, cols].rearrange("(p t) i -> p t i", t=PACK)
+                    nc.sync.dma_start(out=rows_out[:, t - 1:t + 1, :], in_=y[:, t - 1:t + 1, :])
             return y
 
         def planes(h, g, y):
             cols = slice(h * HALF, (h + 1) * HALF)
             y_bf = ring.tile([P, HALF, PACK], BF16, name="y_bf", bufs=3, align_bytes=64)
-            cut = SCALAR_CAST[h * GROUPS + g]
-            nc.scalar.copy(out=y_bf[:, 0:cut, :].rearrange("p (c i) t -> p c t i", i=4),
-                           in_=y[:, :, 0:cut].rearrange("p t (c i) -> p c t i", i=4))
-            nc.vector.tensor_copy(out=y_bf[:, cut:HALF, :].rearrange("p (c i) t -> p c t i", i=4),
-                                  in_=y[:, :, cut:HALF].rearrange("p t (c i) -> p c t i", i=4))
+            cut, cut2 = CAST_CUTS[h * GROUPS + g]
+            nc.gpsimd.tensor_scalar(out=y_bf[:, 0:cut, :], in0=y[:, :, 0:cut].rearrange("p t i -> p i t"),
+                                    scalar1=1.0, scalar2=0.0, op0=ALU.mult, op1=ALU.add)
+            nc.scalar.copy(out=y_bf[:, cut:cut2, :].rearrange("p (c i) t -> p c t i", i=4),
+                           in_=y[:, :, cut:cut2].rearrange("p t (c i) -> p c t i", i=4))
+            if cut2 < HALF:
+                nc.vector.tensor_copy(out=y_bf[:, cut2:HALF, :].rearrange("p (c i) t -> p c t i", i=4),
+                                      in_=y[:, :, cut2:HALF].rearrange("p t (c i) -> p c t i", i=4))
             y_q = ring.tile([P, HALF], U32, name="y_q", bufs=3, align_bytes=64)
             nc.vector.quantize_mx(out=y_q[:].bitcast(FP8X4), scales=y_sc[:, g, cols],
                                   in_=y_bf[:].rearrange("p i t -> p (i t)"))
             nc.sync.dma_start(out=out_1[g].rearrange("p m t -> p (m t)").bitcast(I32)[:, cols], in_=y_q[:].bitcast(I32))
 
         banks = [(bank([P, PACK, CHUNK]), bank([P, PACK, CHUNK])) for c in range(CHUNKS)]
+        for g in range(GROUPS):
+            gather_target_scales(g)
         for a in range(PASSES):
+            if a == 0:
+                quantise_wg(0)
             gather_sources(a, 0)
-            quantise_wg(a)
             for c in range(CHUNKS):
                 project(banks[c][0], banks[c][1], a, 0, c)
                 if a == PASSES - 1:
                     gate(banks[c][0], banks[c][1], 0, c)
             gather_sources(a, 1)
-            if a == 1:
-                for g in range(GROUPS):
-                    gather_target_scales(g)
+            if a == 0:
+                tab.append(load_words(tab_words[2], "place_a"))
+                quantise_wg(1)
+                tab2 = load_words(tab2_words[0], "place_b")
+                quantise_wg(2)
         quantise_h(0)
 
         def second_half_chunk(c):
@@ -229,9 +235,10 @@ def tile_list_transport_plan_lookup_kernel(tc, tab_words, tab_scales, tab2_words
                 project(p_bank, g_bank, a, 1, c)
             gate(p_bank, g_bank, 1, c)
 
+        src = [spread_src(0)]
+        gather_targets(0)
         second_half_chunk(0)
         second_half_chunk(1)
-        gather_targets(0)
         y_prev = plan(0, 0)
         gather_targets(1)
         second_half_chunk(2)
@@ -244,6 +251,7 @@ def tile_list_transport_plan_lookup_kernel(tc, tab_words, tab_scales, tab2_words
                 gather_targets(2)
                 second_half_chunk(3)
                 quantise_h(1)
+                src.append(spread_src(1))
         planes(*units[-1], y_prev)
 
         for q in range(QUADS):

@@ -29,7 +29,9 @@ CHUNKS = HALF // CHUNK
 LIST_COLS = HALF // 16
 QUADS = 4
 ROW0 = P - 16 * PASSES
-CAST_CUTS = [(320, 512)] * 5 + [(128, 288)]
+CAST_CUTS = [(352, 512)] * 5 + [(128, 288)]
+WG_CUT = 48
+PLAN_BANKS = (1, 6, 7)
 
 
 def tile_list_transport_plan_lookup_kernel(tc, tab_words, tab_scales, tab2_words, tab2_scales, w4_words,
@@ -40,13 +42,13 @@ def tile_list_transport_plan_lookup_kernel(tc, tab_words, tab_scales, tab2_words
         lists = ctx.enter_context(tc.tile_pool(name="lists", bufs=1))
         keep = ctx.enter_context(tc.tile_pool(name="keep", bufs=1))
         ring = ctx.enter_context(tc.tile_pool(name="ring", bufs=2))
-        psum = ctx.enter_context(tc.psum_pool(name="psum", bufs=8))
+        psum = ctx.enter_context(tc.psum_pool(name="psum", bufs=1))
 
         def kept(name, shape, dtype):
             return keep.tile(shape, dtype, name=name, align_bytes=64)
 
-        def bank(shape):
-            return psum.tile(shape, F32, name="bank")
+        def bank(b, shape):
+            return psum.tile(shape, F32, name="bank%d" % b)
 
         src_list = lists.tile([P, S // 16], U16, name="src_list")
         tgt_list = lists.tile([P, S2 // 16], U16, name="tgt_list")
@@ -64,49 +66,46 @@ def tile_list_transport_plan_lookup_kernel(tc, tab_words, tab_scales, tab2_words
             return raw
 
 
-        src_cols = kept("src_cols", [P, S // P], F32)
+        src_cols = kept("src_cols", [P, HALVES, CHUNKS], F32)
         tgt = kept("tgt", [P, GROUPS, PACK], F32)
         tab_sc = kept("place_c", [P, T // 4], I32)
         w4_sc_raw = kept("place_b", [P, H // 4], I32)
         tab2_sc = kept("tab2_sc", [P, T2 // 4], I32)
 
-        nc.scalar.dma_start(out=tab_sc[ROW0:P, :], in_=tab_scales.bitcast(I32).rearrange("a q c -> q a c"))
-        nc.scalar.dma_start(out=w4_sc_raw[ROW0:P, :], in_=w4_scales.bitcast(I32).rearrange("a q c -> q a c"))
-        with nc.allow_non_contiguous_dma(reason="one value a partition"):
-            nc.scalar.dma_start(out=src_cols[:], in_=src_scale.rearrange("(c p) -> p c", p=P))
-        nc.scalar.dma_start(out=tgt[:], in_=tgt_scale.rearrange("(g p t) -> p g t", p=P, t=PACK))
         nc.sync.dma_start(src_list[:], offs)
+        nc.sync.dma_start(out=tab_sc[ROW0:P, :], in_=tab_scales.bitcast(I32).rearrange("a q c -> q a c"))
         nc.sync.dma_start(tgt_list[:], offs2)
-        nc.sync.dma_start(out=w4_raw[:], in_=w4_words.bitcast(I32).rearrange("a p b -> p a b"))
         wg_raw.append(load_wg(0, "wg_first"))
+        nc.sync.dma_start(out=w4_sc_raw[ROW0:P, :], in_=w4_scales.bitcast(I32).rearrange("a q c -> q a c"))
         tab.append(load_words(tab_words[0], "place_a"))
+        nc.sync.dma_start(out=w4_raw[:], in_=w4_words.bitcast(I32).rearrange("a p b -> p a b"))
 
         nc.vector.memset(tab2_sc[:], 0)
         nc.vector.memset(tab_sc[0:ROW0, :], 0)
         nc.vector.memset(w4_sc_raw[0:ROW0, :], 0)
         for q in range(QUADS):
-            nc.gpsimd.dma_start(out=tab2_sc[32 * q:32 * q + 4, :],
+            nc.scalar.dma_start(out=tab2_sc[32 * q:32 * q + 4, :],
                                 in_=tab2_scales.bitcast(I32)[0, 4 * q:4 * q + 4, :])
+        nc.gpsimd.dma_start(out=src_cols[:], in_=src_scale.rearrange("(h p c) -> p h c", p=P, c=CHUNKS))
+        nc.gpsimd.dma_start(out=tgt[:], in_=tgt_scale.rearrange("(g p t) -> p g t", p=P, t=PACK))
         sc = kept("sc", [P, PASSES, S + H], U8)
         nc.vector.memset(sc[:].bitcast(I32), 0)
 
         ident = kept("ident", [P, P], F32)
         make_identity(nc, ident[:])
 
-        def spread_src(h):
-            spread = bank([P, CHUNKS, CHUNK])
+        def spread_src(h, b):
+            spread = bank(b, [P, P, CHUNKS])
             for c in range(CHUNKS):
-                col = h * CHUNKS + c
-                nc.tensor.transpose(spread[:, c, :], src_cols[:, col:col + 1].to_broadcast([P, P]), ident[:])
+                nc.tensor.transpose(spread[:, :, c], src_cols[:, h, c:c + 1].to_broadcast([P, P]), ident[:])
             return spread
 
         picked_src_sc = kept("place_d", [P, S], U8)
         nc.vector.tensor_copy(picked_src_sc[:], tab_sc[:].bitcast(U8).indirect(src_list[:]))
-        rows = kept("rows", [P, S + H], U8)
+        rows = kept("place_e", [P, S + H], U8)
         nc.vector.tensor_copy(out=rows[:, S:S + H].rearrange("p (t m) -> p t m", t=PACK),
                               in_=w4_sc_raw[:].bitcast(U8).rearrange("p (m t) -> p t m", t=PACK))
         wg_raw.append(load_wg(1, "place_b"))
-        wg_raw.append(load_wg(2, "place_c"))
         nc.vector.tensor_copy(out=rows[:, 0:S].bitcast(I32), in_=picked_src_sc[:].bitcast(I32))
         for q in range(QUADS):
             nc.sync.dma_start(out=sc[32 * q:32 * q + 4, :, :].bitcast(I32),
@@ -116,34 +115,39 @@ def tile_list_transport_plan_lookup_kernel(tc, tab_words, tab_scales, tab2_words
         nc.vector.tensor_copy(out=w4[:].bitcast(U16).rearrange("p a (t m) -> p a t m", t=PACK),
                               in_=w4_raw[:].bitcast(U16).rearrange("p a (m t) -> p a t m", t=PACK))
 
-        v = [[kept("v%d_%d" % (a, h), [P, HALF], U32) for h in range(HALVES)] for a in range(PASSES)]
+        v = [kept("v%d" % a, [P, S], U32) for a in range(PASSES)]
         wg_q = [kept("wg_q%d" % a, [P, H], U32) for a in range(PASSES)]
         wg_sc = [kept("wg_sc%d" % a, [P, H], U8) for a in range(PASSES)]
 
-        def gather_sources(a, h):
-            nc.vector.tensor_copy(v[a][h][:],
-                                  tab[a][:].bitcast(U32).indirect(src_list[:, h * LIST_COLS:(h + 1) * LIST_COLS]))
+        def gather_sources(a, h0, h1):
+            nc.vector.tensor_copy(v[a][:, h0 * HALF:h1 * HALF],
+                                  tab[a][:].bitcast(U32).indirect(src_list[:, h0 * LIST_COLS:h1 * LIST_COLS]))
 
-        def quantise_wg(a):
+        def quantise_wg(a, cut):
             rounded = ring.tile([P, PACK * H], BF16, name="wg_bf", align_bytes=64)
-            nc.scalar.copy(out=rounded[:].rearrange("p (t m j) -> p t m j", t=PACK, j=PACK),
-                           in_=wg_raw[a][:].rearrange("p j (m t) -> p t m j", t=PACK))
+            dst = rounded[:].rearrange("p (t m j) -> p m j t", t=PACK, j=PACK)
+            raw = wg_raw[a][:].rearrange("p j (m t) -> p m j t", t=PACK)
+            nc.scalar.copy(out=dst[:, 0:cut], in_=raw[:, 0:cut])
+            if cut < P:
+                nc.vector.tensor_copy(out=dst[:, cut:P], in_=raw[:, cut:P])
             nc.vector.quantize_mx(out=wg_q[a][:].bitcast(FP8X4), scales=wg_sc[a][:], in_=rounded[:])
 
-        def project(p_bank, g_bank, a, h, c):
-            cols = slice(c * CHUNK, (c + 1) * CHUNK)
+        def project_g(g_bank, a, h, c):
             sc_cols = slice(h * HALF + c * CHUNK, h * HALF + (c + 1) * CHUNK)
             for t in range(PACK):
                 nc.tensor.matmul_mx(
                     out=g_bank[:, t, :],
                     lhsT=wg_q[a][:, t * P:(t + 1) * P].bitcast(FP8X4), lhsT_scale=wg_sc[a][:, t * P:(t + 1) * P],
-                    rhs=v[a][h][:, cols].bitcast(FP8X4), rhs_scale=sc[:, a, sc_cols],
+                    rhs=v[a][:, sc_cols].bitcast(FP8X4), rhs_scale=sc[:, a, sc_cols],
                     start=(a == 0 and t == 0), stop=(a == PASSES - 1 and t == PACK - 1))
+
+        def project_p(p_bank, a, h, c):
+            sc_cols = slice(h * HALF + c * CHUNK, h * HALF + (c + 1) * CHUNK)
             for t in range(PACK):
                 nc.tensor.matmul_mx(
                     out=p_bank[:, t, :],
                     lhsT=w4[:, a, 2 * t * P:2 * (t + 1) * P].bitcast(FP4X4), lhsT_scale=sc[:, a, S + t * P:S + (t + 1) * P],
-                    rhs=v[a][h][:, cols].bitcast(FP8X4), rhs_scale=sc[:, a, sc_cols],
+                    rhs=v[a][:, sc_cols].bitcast(FP8X4), rhs_scale=sc[:, a, sc_cols],
                     start=(a == 0 and t == 0), stop=(a == PASSES - 1 and t == PACK - 1))
 
         h_bf = [kept("h_bf%d" % h, [P, HALF, PACK], BF16) for h in range(HALVES)]
@@ -160,20 +164,20 @@ def tile_list_transport_plan_lookup_kernel(tc, tab_words, tab_scales, tab2_words
             nc.vector.quantize_mx(out=h_q[h][:].bitcast(FP8X4), scales=h_sc[h][:],
                                   in_=h_bf[h][:].rearrange("p i t -> p (i t)"))
 
-        v2 = [kept("tgt_words%d" % g, [P, PACK, P], U32) for g in range(GROUPS)]
-        v2_sc = [kept("tgt_sc%d" % g, [P, PACK, P], U8) for g in range(GROUPS)]
+        v2 = kept("tgt_words", [P, PACK, GROUPS, P], U32)
+        v2_sc = kept("tgt_sc", [P, PACK, GROUPS, P], U8)
 
-        def gather_target_scales(g):
-            picked = ring.tile([P, PASS], U8, name="picked_sc", align_bytes=64)
-            nc.vector.tensor_copy(picked[:],
-                                  tab2_sc[:].bitcast(U8).indirect(tgt_list[:, g * LIST_COLS:(g + 1) * LIST_COLS]))
-            nc.vector.tensor_copy(out=v2_sc[g][:], in_=picked[:].rearrange("p (m t) -> p t m", t=PACK))
+        def gather_target_scales():
+            picked = kept("picked_sc", [P, S2], U8)
+            nc.vector.tensor_copy(picked[:], tab2_sc[:].bitcast(U8).indirect(tgt_list[:]))
+            nc.vector.tensor_copy(out=v2_sc[:].rearrange("p t g (c m) -> p (g c) t m", m=16),
+                                  in_=picked[:].rearrange("p (c m t) -> p c t m", m=16, t=PACK))
 
-        def gather_targets(g):
-            picked = ring.tile([P, PASS], U32, name="picked", align_bytes=64)
+        def gather_targets(g0, g1):
+            picked = kept("picked%d" % g0, [P, (g1 - g0) * PASS], U32)
             nc.vector.tensor_copy(picked[:],
-                                  tab2[:].bitcast(U32).indirect(tgt_list[:, g * LIST_COLS:(g + 1) * LIST_COLS]))
-            nc.vector.tensor_copy(out=v2[g][:].rearrange("p t (c m) -> p c t m", m=4),
+                                  tab2[:].bitcast(U32).indirect(tgt_list[:, g0 * LIST_COLS:g1 * LIST_COLS]))
+            nc.vector.tensor_copy(out=v2[:, :, g0:g1, :].rearrange("p t g (c m) -> p (g c) t m", m=4),
                                   in_=picked[:].rearrange("p (c m t) -> p c t m", m=4, t=PACK))
 
         y_sc = kept("y_sc", [P, GROUPS, S], U8)
@@ -182,10 +186,10 @@ def tile_list_transport_plan_lookup_kernel(tc, tab_words, tab_scales, tab2_words
             cols = slice(h * HALF, (h + 1) * HALF)
             y = ring.tile([P, PACK, HALF], F32, name="y", bufs=3)
             for t in range(PACK):
-                s_bank = bank([P, HALF])
-                nc.tensor.matmul_mx(out=s_bank[:], lhsT=v2[g][:, t, :].bitcast(FP8X4), lhsT_scale=v2_sc[g][:, t, :],
+                s_bank = bank(PLAN_BANKS[(PACK * (h * GROUPS + g) + t) % len(PLAN_BANKS)], [P, HALF])
+                nc.tensor.matmul_mx(out=s_bank[:], lhsT=v2[:, t, g, :].bitcast(FP8X4), lhsT_scale=v2_sc[:, t, g, :],
                                     rhs=h_q[h][:].bitcast(FP8X4), rhs_scale=h_sc[h][:], start=True, stop=True)
-                kern = ring.tile([P, HALF], F32, name="kern", bufs=6)
+                kern = ring.tile([P, HALF], F32, name="kern", bufs=8)
                 nc.scalar.activation(out=kern[:], in_=s_bank[:], func=ACT.Exp, scale=0.5)
                 nc.vector.scalar_tensor_tensor(out=y[:, t, :], in0=kern[:], scalar=tgt[:, g, t:t + 1],
                                                in1=src[h][:].rearrange("p c n -> p (c n)"), op0=ALU.mult, op1=ALU.mult)
@@ -196,7 +200,7 @@ def tile_list_transport_plan_lookup_kernel(tc, tab_words, tab_scales, tab2_words
 
         def planes(h, g, y):
             cols = slice(h * HALF, (h + 1) * HALF)
-            y_bf = ring.tile([P, HALF, PACK], BF16, name="y_bf", bufs=3, align_bytes=64)
+            y_bf = ring.tile([P, HALF, PACK], BF16, name="y_bf", bufs=2, align_bytes=64)
             cut, cut2 = CAST_CUTS[h * GROUPS + g]
             nc.gpsimd.tensor_scalar(out=y_bf[:, 0:cut, :], in0=y[:, :, 0:cut].rearrange("p t i -> p i t"),
                                     scalar1=1.0, scalar2=0.0, op0=ALU.mult, op1=ALU.add)
@@ -210,48 +214,56 @@ def tile_list_transport_plan_lookup_kernel(tc, tab_words, tab_scales, tab2_words
                                   in_=y_bf[:].rearrange("p i t -> p (i t)"))
             nc.sync.dma_start(out=out_1[g].rearrange("p m t -> p (m t)").bitcast(I32)[:, cols], in_=y_q[:].bitcast(I32))
 
-        banks = [(bank([P, PACK, CHUNK]), bank([P, PACK, CHUNK])) for c in range(CHUNKS)]
-        for g in range(GROUPS):
-            gather_target_scales(g)
+        banks = [(bank(2 * c, [P, PACK, CHUNK]), bank(2 * c + 1, [P, PACK, CHUNK])) for c in range(CHUNKS)]
+        tab.append(load_words(tab_words[2], "place_e"))
         for a in range(PASSES):
+            if a < PASSES - 1:
+                quantise_wg(a, P)
+            if a == 1:
+                wg_raw.append(load_wg(2, "place_b"))
+            if a < PASSES - 1:
+                gather_sources(a, 0, 2)
+            else:
+                gather_sources(a, 0, 1)
+                gather_sources(a, 1, 2)
             if a == 0:
-                quantise_wg(0)
-            gather_sources(a, 0)
+                gather_target_scales()
+            if a == 1:
+                tab2 = load_words(tab2_words[0], "place_d")
             for c in range(CHUNKS):
-                project(banks[c][0], banks[c][1], a, 0, c)
-                if a == PASSES - 1:
-                    gate(banks[c][0], banks[c][1], 0, c)
-            gather_sources(a, 1)
-            if a == 0:
-                tab.append(load_words(tab_words[2], "place_a"))
-                quantise_wg(1)
-                tab2 = load_words(tab2_words[0], "place_b")
-                quantise_wg(2)
+                project_p(banks[c][0], a, 0, c)
+                if a < PASSES - 1:
+                    project_g(banks[c][1], a, 0, c)
+        quantise_wg(PASSES - 1, WG_CUT)
+        for c in range(CHUNKS):
+            project_g(banks[c][1], PASSES - 1, 0, c)
+            gate(banks[c][0], banks[c][1], 0, c)
+        src = [spread_src(0, 0)]
+        gather_targets(0, 1)
         quantise_h(0)
+        gather_targets(1, 3)
 
         def second_half_chunk(c):
-            p_bank, g_bank = bank([P, PACK, CHUNK]), bank([P, PACK, CHUNK])
+            p_bank, g_bank = bank(2 + 2 * (c % 2), [P, PACK, CHUNK]), bank(3 + 2 * (c % 2), [P, PACK, CHUNK])
             for a in range(PASSES):
-                project(p_bank, g_bank, a, 1, c)
+                project_g(g_bank, a, 1, c)
+            for a in range(PASSES):
+                project_p(p_bank, a, 1, c)
             gate(p_bank, g_bank, 1, c)
 
-        src = [spread_src(0)]
-        gather_targets(0)
+        y_prev = plan(0, 0)
         second_half_chunk(0)
         second_half_chunk(1)
-        y_prev = plan(0, 0)
-        gather_targets(1)
-        second_half_chunk(2)
         units = [(h, g) for h in range(HALVES) for g in range(GROUPS)]
         for n in range(1, len(units)):
             y_now = plan(*units[n])
             planes(*units[n - 1], y_prev)
             y_prev = y_now
             if n == 1:
-                gather_targets(2)
+                second_half_chunk(2)
                 second_half_chunk(3)
                 quantise_h(1)
-                src.append(spread_src(1))
+                src.append(spread_src(1, 2))
         planes(*units[-1], y_prev)
 
         for q in range(QUADS):

@@ -29,7 +29,8 @@ CHUNKS = HALF // CHUNK
 LIST_COLS = HALF // 16
 QUADS = 4
 ROW0 = P - 16 * PASSES
-CAST_CUTS = [(352, 512)] * 5 + [(128, 288)]
+CAST_CUTS = [512, 448, 384, 320, 320, 192]
+TGT_ROW = 12
 WG_CUT = 48
 PLAN_BANKS = (1, 6, 7)
 
@@ -52,7 +53,7 @@ def tile_list_transport_plan_lookup_kernel(tc, tab_words, tab_scales, tab2_words
 
         src_list = lists.tile([P, S // 16], U16, name="src_list")
         tgt_list = lists.tile([P, S2 // 16], U16, name="tgt_list")
-        w4_raw = kept("w4_raw", [P, PASSES, 2 * H // 4], I32)
+        w4_raw = kept("place_f", [P, PASSES, 2 * H // 4], I32)
         tab, wg_raw = [], []
 
         def load_words(words, place):
@@ -66,8 +67,6 @@ def tile_list_transport_plan_lookup_kernel(tc, tab_words, tab_scales, tab2_words
             return raw
 
 
-        src_cols = kept("src_cols", [P, HALVES, CHUNKS], F32)
-        tgt = kept("tgt", [P, GROUPS, PACK], F32)
         tab_sc = kept("place_c", [P, T // 4], I32)
         w4_sc_raw = kept("place_b", [P, H // 4], I32)
         tab2_sc = kept("tab2_sc", [P, T2 // 4], I32)
@@ -83,11 +82,8 @@ def tile_list_transport_plan_lookup_kernel(tc, tab_words, tab_scales, tab2_words
         nc.vector.memset(tab2_sc[:], 0)
         nc.vector.memset(tab_sc[0:ROW0, :], 0)
         nc.vector.memset(w4_sc_raw[0:ROW0, :], 0)
-        for q in range(QUADS):
-            nc.scalar.dma_start(out=tab2_sc[32 * q:32 * q + 4, :],
-                                in_=tab2_scales.bitcast(I32)[0, 4 * q:4 * q + 4, :])
-        nc.gpsimd.dma_start(out=src_cols[:], in_=src_scale.rearrange("(h p c) -> p h c", p=P, c=CHUNKS))
-        nc.gpsimd.dma_start(out=tgt[:], in_=tgt_scale.rearrange("(g p t) -> p g t", p=P, t=PACK))
+        for r in range(4):
+            nc.scalar.dma_start(out=tab2_sc[TGT_ROW + r:P:32, :], in_=tab2_scales.bitcast(I32)[0, r:16:4, :])
         sc = kept("sc", [P, PASSES, S + H], U8)
         nc.vector.memset(sc[:].bitcast(I32), 0)
 
@@ -107,7 +103,7 @@ def tile_list_transport_plan_lookup_kernel(tc, tab_words, tab_scales, tab2_words
                               in_=w4_sc_raw[:].bitcast(U8).rearrange("p (m t) -> p t m", t=PACK))
         wg_raw.append(load_wg(1, "place_b"))
         nc.vector.tensor_copy(out=rows[:, 0:S].bitcast(I32), in_=picked_src_sc[:].bitcast(I32))
-        for q in range(QUADS):
+        for q in (0, 2, 1, 3):
             nc.sync.dma_start(out=sc[32 * q:32 * q + 4, :, :].bitcast(I32),
                               in_=rows[ROW0 + 12 * q:ROW0 + 12 * (q + 1), :].bitcast(I32))
         tab.append(load_words(tab_words[1], "place_d"))
@@ -125,11 +121,11 @@ def tile_list_transport_plan_lookup_kernel(tc, tab_words, tab_scales, tab2_words
 
         def quantise_wg(a, cut):
             rounded = ring.tile([P, PACK * H], BF16, name="wg_bf", align_bytes=64)
-            dst = rounded[:].rearrange("p (t m j) -> p m j t", t=PACK, j=PACK)
-            raw = wg_raw[a][:].rearrange("p j (m t) -> p m j t", t=PACK)
-            nc.scalar.copy(out=dst[:, 0:cut], in_=raw[:, 0:cut])
+            dst = rounded[:].rearrange("p (u t m j) -> p u m j t", u=2, t=2, j=PACK)
+            raw = wg_raw[a][:].rearrange("p j (m u t) -> p u m j t", u=2, t=2)
+            nc.scalar.copy(out=dst[:, :, 0:cut], in_=raw[:, :, 0:cut])
             if cut < P:
-                nc.vector.tensor_copy(out=dst[:, cut:P], in_=raw[:, cut:P])
+                nc.vector.tensor_copy(out=dst[:, :, cut:P], in_=raw[:, :, cut:P])
             nc.vector.quantize_mx(out=wg_q[a][:].bitcast(FP8X4), scales=wg_sc[a][:], in_=rounded[:])
 
         def project_g(g_bank, a, h, c):
@@ -164,30 +160,32 @@ def tile_list_transport_plan_lookup_kernel(tc, tab_words, tab_scales, tab2_words
             nc.vector.quantize_mx(out=h_q[h][:].bitcast(FP8X4), scales=h_sc[h][:],
                                   in_=h_bf[h][:].rearrange("p i t -> p (i t)"))
 
-        v2 = kept("tgt_words", [P, PACK, GROUPS, P], U32)
+        v2 = []
         v2_sc = kept("tgt_sc", [P, PACK, GROUPS, P], U8)
 
         def gather_target_scales():
-            picked = kept("picked_sc", [P, S2], U8)
+            picked = kept("place_g", [P, S2], U8)
             nc.vector.tensor_copy(picked[:], tab2_sc[:].bitcast(U8).indirect(tgt_list[:]))
             nc.vector.tensor_copy(out=v2_sc[:].rearrange("p t g (c m) -> p (g c) t m", m=16),
                                   in_=picked[:].rearrange("p (c m t) -> p c t m", m=16, t=PACK))
 
         def gather_targets(g0, g1):
-            picked = kept("picked%d" % g0, [P, (g1 - g0) * PASS], U32)
+            picked = kept("picked", [P, (g1 - g0) * PASS], U32)
+            dealt = kept("tgt_words%d" % g0, [P, PACK, (g1 - g0) * P], U32)
             nc.vector.tensor_copy(picked[:],
                                   tab2[:].bitcast(U32).indirect(tgt_list[:, g0 * LIST_COLS:g1 * LIST_COLS]))
-            nc.vector.tensor_copy(out=v2[:, :, g0:g1, :].rearrange("p t g (c m) -> p (g c) t m", m=4),
+            nc.vector.tensor_copy(out=dealt[:].rearrange("p t (c m) -> p c t m", m=4),
                                   in_=picked[:].rearrange("p (c m t) -> p c t m", m=4, t=PACK))
+            v2.extend(dealt[:, :, g * P:(g + 1) * P] for g in range(g1 - g0))
 
-        y_sc = kept("y_sc", [P, GROUPS, S], U8)
+        y_sc = [kept("y_sc%d" % h, [P, GROUPS, HALF], U8) for h in range(HALVES)]
 
         def plan(h, g):
             cols = slice(h * HALF, (h + 1) * HALF)
             y = ring.tile([P, PACK, HALF], F32, name="y", bufs=3)
             for t in range(PACK):
                 s_bank = bank(PLAN_BANKS[(PACK * (h * GROUPS + g) + t) % len(PLAN_BANKS)], [P, HALF])
-                nc.tensor.matmul_mx(out=s_bank[:], lhsT=v2[:, t, g, :].bitcast(FP8X4), lhsT_scale=v2_sc[:, t, g, :],
+                nc.tensor.matmul_mx(out=s_bank[:], lhsT=v2[g][:, t, :].bitcast(FP8X4), lhsT_scale=v2_sc[TGT_ROW:P, t, g, :],
                                     rhs=h_q[h][:].bitcast(FP8X4), rhs_scale=h_sc[h][:], start=True, stop=True)
                 kern = ring.tile([P, HALF], F32, name="kern", bufs=8)
                 nc.scalar.activation(out=kern[:], in_=s_bank[:], func=ACT.Exp, scale=0.5)
@@ -201,34 +199,39 @@ def tile_list_transport_plan_lookup_kernel(tc, tab_words, tab_scales, tab2_words
         def planes(h, g, y):
             cols = slice(h * HALF, (h + 1) * HALF)
             y_bf = ring.tile([P, HALF, PACK], BF16, name="y_bf", bufs=2, align_bytes=64)
-            cut, cut2 = CAST_CUTS[h * GROUPS + g]
-            nc.gpsimd.tensor_scalar(out=y_bf[:, 0:cut, :], in0=y[:, :, 0:cut].rearrange("p t i -> p i t"),
-                                    scalar1=1.0, scalar2=0.0, op0=ALU.mult, op1=ALU.add)
-            nc.scalar.copy(out=y_bf[:, cut:cut2, :].rearrange("p (c i) t -> p c t i", i=4),
-                           in_=y[:, :, cut:cut2].rearrange("p t (c i) -> p c t i", i=4))
+            cut2 = CAST_CUTS[h * GROUPS + g]
+            nc.scalar.copy(out=y_bf[:, 0:cut2, :].rearrange("p (c i) t -> p c t i", i=4),
+                           in_=y[:, :, 0:cut2].rearrange("p t (c i) -> p c t i", i=4))
             if cut2 < HALF:
                 nc.vector.tensor_copy(out=y_bf[:, cut2:HALF, :].rearrange("p (c i) t -> p c t i", i=4),
                                       in_=y[:, :, cut2:HALF].rearrange("p t (c i) -> p c t i", i=4))
             y_q = ring.tile([P, HALF], U32, name="y_q", bufs=3, align_bytes=64)
-            nc.vector.quantize_mx(out=y_q[:].bitcast(FP8X4), scales=y_sc[:, g, cols],
+            nc.vector.quantize_mx(out=y_q[:].bitcast(FP8X4), scales=y_sc[h][:, g, :],
                                   in_=y_bf[:].rearrange("p i t -> p (i t)"))
             nc.sync.dma_start(out=out_1[g].rearrange("p m t -> p (m t)").bitcast(I32)[:, cols], in_=y_q[:].bitcast(I32))
+
+        def store_scales(h):
+            for r in range(4):
+                nc.sync.dma_start(out=out_2.bitcast(I32)[:, r:16:4, h * P:(h + 1) * P].rearrange("g q m -> q g m"),
+                                  in_=y_sc[h][r:P:32, :, :].bitcast(I32))
 
         banks = [(bank(2 * c, [P, PACK, CHUNK]), bank(2 * c + 1, [P, PACK, CHUNK])) for c in range(CHUNKS)]
         tab.append(load_words(tab_words[2], "place_e"))
         for a in range(PASSES):
             if a < PASSES - 1:
                 quantise_wg(a, P)
-            if a == 1:
-                wg_raw.append(load_wg(2, "place_b"))
-            if a < PASSES - 1:
                 gather_sources(a, 0, 2)
             else:
                 gather_sources(a, 0, 1)
                 gather_sources(a, 1, 2)
             if a == 0:
                 gather_target_scales()
+                src_cols = kept("place_f", [P, HALVES, CHUNKS], F32)
+                tgt = kept("place_g", [P, GROUPS, PACK], F32)
+                nc.sync.dma_start(out=src_cols[:], in_=src_scale.rearrange("(h p c) -> p h c", p=P, c=CHUNKS))
+                nc.sync.dma_start(out=tgt[:], in_=tgt_scale.rearrange("(g p t) -> p g t", p=P, t=PACK))
             if a == 1:
+                wg_raw.append(load_wg(2, "place_b"))
                 tab2 = load_words(tab2_words[0], "place_d")
             for c in range(CHUNKS):
                 project_p(banks[c][0], a, 0, c)
@@ -259,6 +262,8 @@ def tile_list_transport_plan_lookup_kernel(tc, tab_words, tab_scales, tab2_words
             y_now = plan(*units[n])
             planes(*units[n - 1], y_prev)
             y_prev = y_now
+            if n == GROUPS:
+                store_scales(0)
             if n == 1:
                 second_half_chunk(2)
                 second_half_chunk(3)
@@ -266,6 +271,4 @@ def tile_list_transport_plan_lookup_kernel(tc, tab_words, tab_scales, tab2_words
                 src.append(spread_src(1, 2))
         planes(*units[-1], y_prev)
 
-        for q in range(QUADS):
-            nc.sync.dma_start(out=out_2.bitcast(I32)[:, 4 * q:4 * q + 4, :].rearrange("g r m -> r g m"),
-                              in_=y_sc[32 * q:32 * q + 4, :, :].bitcast(I32))
+        store_scales(1)

@@ -156,9 +156,10 @@ def tile_list_transport_plan_lookup_kernel(tc, tab_words, tab_scales, tab2_words
             nc.vector.scalar_tensor_tensor(out=h_bf[h][:, c * CHUNK:(c + 1) * CHUNK, :], in0=th[:], scalar=1.0,
                                            in1=p_bank[:].rearrange("p t n -> p n t"), op0=ALU.add, op1=ALU.mult)
 
-        def quantise_h(h):
-            nc.vector.quantize_mx(out=h_q[h][:].bitcast(FP8X4), scales=h_sc[h][:],
-                                  in_=h_bf[h][:].rearrange("p i t -> p (i t)"))
+        def quantise_h(h, c0, width):
+            cols = slice(c0, c0 + width)
+            nc.vector.quantize_mx(out=h_q[h][:, cols].bitcast(FP8X4), scales=h_sc[h][:, cols],
+                                  in_=h_bf[h][:, cols, :].rearrange("p i t -> p (i t)"))
 
         v2 = []
         v2_sc = kept("tgt_sc", [P, PACK, GROUPS, P], U8)
@@ -180,33 +181,40 @@ def tile_list_transport_plan_lookup_kernel(tc, tab_words, tab_scales, tab2_words
 
         y_sc = [kept("y_sc%d" % h, [P, GROUPS, HALF], U8) for h in range(HALVES)]
 
-        def plan(h, g):
-            cols = slice(h * HALF, (h + 1) * HALF)
-            y = ring.tile([P, PACK, HALF], F32, name="y", bufs=3)
+        banks_used = []
+
+        def next_bank():
+            banks_used.append(PLAN_BANKS[len(banks_used) % len(PLAN_BANKS)])
+            return banks_used[-1]
+
+        def plan(h, g, c0, width):
+            cols = slice(h * HALF + c0, h * HALF + c0 + width)
+            y = ring.tile([P, PACK, width], F32, name="y", bufs=3)
             for t in range(PACK):
-                s_bank = bank(PLAN_BANKS[(PACK * (h * GROUPS + g) + t) % len(PLAN_BANKS)], [P, HALF])
+                s_bank = bank(next_bank(), [P, width])
                 nc.tensor.matmul_mx(out=s_bank[:], lhsT=v2[g][:, t, :].bitcast(FP8X4), lhsT_scale=v2_sc[TGT_ROW:P, t, g, :],
-                                    rhs=h_q[h][:].bitcast(FP8X4), rhs_scale=h_sc[h][:], start=True, stop=True)
-                kern = ring.tile([P, HALF], F32, name="kern", bufs=8)
+                                    rhs=h_q[h][:, c0:c0 + width].bitcast(FP8X4), rhs_scale=h_sc[h][:, c0:c0 + width],
+                                    start=True, stop=True)
+                kern = ring.tile([P, width], F32, name="kern", bufs=8)
                 nc.scalar.activation(out=kern[:], in_=s_bank[:], func=ACT.Exp, scale=0.5)
                 nc.vector.scalar_tensor_tensor(out=y[:, t, :], in0=kern[:], scalar=tgt[:, g, t:t + 1],
-                                               in1=src[h][:].rearrange("p c n -> p (c n)"), op0=ALU.mult, op1=ALU.mult)
+                                               in1=src[h][:].rearrange("p c n -> p (c n)")[:, c0:c0 + width],
+                                               op0=ALU.mult, op1=ALU.mult)
                 if t % 2 == 1:
                     rows_out = out_0[g * PASS:(g + 1) * PASS, cols].rearrange("(p t) i -> p t i", t=PACK)
                     nc.sync.dma_start(out=rows_out[:, t - 1:t + 1, :], in_=y[:, t - 1:t + 1, :])
             return y
 
-        def planes(h, g, y):
-            cols = slice(h * HALF, (h + 1) * HALF)
-            y_bf = ring.tile([P, HALF, PACK], BF16, name="y_bf", bufs=2, align_bytes=64)
-            cut2 = CAST_CUTS[h * GROUPS + g]
-            nc.scalar.copy(out=y_bf[:, 0:cut2, :].rearrange("p (c i) t -> p c t i", i=4),
-                           in_=y[:, :, 0:cut2].rearrange("p t (c i) -> p c t i", i=4))
-            if cut2 < HALF:
-                nc.vector.tensor_copy(out=y_bf[:, cut2:HALF, :].rearrange("p (c i) t -> p c t i", i=4),
-                                      in_=y[:, :, cut2:HALF].rearrange("p t (c i) -> p c t i", i=4))
-            y_q = ring.tile([P, HALF], U32, name="y_q", bufs=3, align_bytes=64)
-            nc.vector.quantize_mx(out=y_q[:].bitcast(FP8X4), scales=y_sc[h][:, g, :],
+        def planes(h, g, c0, width, y, cut2):
+            cols = slice(h * HALF + c0, h * HALF + c0 + width)
+            y_bf = ring.tile([P, width, PACK], BF16, name="y_bf", bufs=2, align_bytes=64)
+            nc.scalar.copy(out=y_bf[:, 0:cut2, :].rearrange("p (c i) t -> p c t i", i=2),
+                           in_=y[:, :, 0:cut2].rearrange("p t (c i) -> p c t i", i=2))
+            if cut2 < width:
+                nc.vector.tensor_copy(out=y_bf[:, cut2:width, :].rearrange("p (c i) t -> p c t i", i=2),
+                                      in_=y[:, :, cut2:width].rearrange("p t (c i) -> p c t i", i=2))
+            y_q = ring.tile([P, width], U32, name="y_q", bufs=3, align_bytes=64)
+            nc.vector.quantize_mx(out=y_q[:].bitcast(FP8X4), scales=y_sc[h][:, g, c0:c0 + width],
                                   in_=y_bf[:].rearrange("p i t -> p (i t)"))
             nc.sync.dma_start(out=out_1[g].rearrange("p m t -> p (m t)").bitcast(I32)[:, cols], in_=y_q[:].bitcast(I32))
 
@@ -243,8 +251,7 @@ def tile_list_transport_plan_lookup_kernel(tc, tab_words, tab_scales, tab2_words
             gate(banks[c][0], banks[c][1], 0, c)
         src = [spread_src(0, 0)]
         gather_targets(0, 1)
-        quantise_h(0)
-        gather_targets(1, 3)
+        quantise_h(0, 0, HALF)
 
         def second_half_chunk(c):
             p_bank, g_bank = bank(2 + 2 * (c % 2), [P, PACK, CHUNK]), bank(3 + 2 * (c % 2), [P, PACK, CHUNK])
@@ -254,21 +261,23 @@ def tile_list_transport_plan_lookup_kernel(tc, tab_words, tab_scales, tab2_words
                 project_p(p_bank, a, 1, c)
             gate(p_bank, g_bank, 1, c)
 
-        y_prev = plan(0, 0)
+        units = [(h, g, 0, HALF) for h in range(HALVES) for g in range(GROUPS)]
+        gather_targets(1, 2)
+        y_prev = plan(*units[0])
+        gather_targets(2, 3)
         second_half_chunk(0)
         second_half_chunk(1)
-        units = [(h, g) for h in range(HALVES) for g in range(GROUPS)]
         for n in range(1, len(units)):
             y_now = plan(*units[n])
-            planes(*units[n - 1], y_prev)
+            planes(*units[n - 1], y_prev, CAST_CUTS[n - 1])
             y_prev = y_now
             if n == GROUPS:
                 store_scales(0)
             if n == 1:
                 second_half_chunk(2)
                 second_half_chunk(3)
-                quantise_h(1)
+                quantise_h(1, 0, HALF)
                 src.append(spread_src(1, 2))
-        planes(*units[-1], y_prev)
+        planes(*units[-1], y_prev, CAST_CUTS[-1])
 
         store_scales(1)

@@ -30,8 +30,8 @@ LIST_COLS = HALF // 16
 QUADS = 4
 ROW0 = P - 16 * PASSES
 CAST_CUTS = [512, 448, 384, 320, 320, 192]
-TGT_ROW = 12
 WG_CUT = 48
+SRC_ROW = P - S // P
 PLAN_BANKS = (1, 6, 7)
 
 
@@ -43,6 +43,8 @@ def tile_list_transport_plan_lookup_kernel(tc, tab_words, tab_scales, tab2_words
         lists = ctx.enter_context(tc.tile_pool(name="lists", bufs=1))
         keep = ctx.enter_context(tc.tile_pool(name="keep", bufs=1))
         ring = ctx.enter_context(tc.tile_pool(name="ring", bufs=2))
+        mid = ctx.enter_context(tc.tile_pool(name="mid", bufs=1))
+        early = ctx.enter_context(tc.tile_pool(name="early", bufs=1))
         psum = ctx.enter_context(tc.psum_pool(name="psum", bufs=1))
 
         def kept(name, shape, dtype):
@@ -67,46 +69,59 @@ def tile_list_transport_plan_lookup_kernel(tc, tab_words, tab_scales, tab2_words
             return raw
 
 
-        tab_sc = kept("place_c", [P, T // 4], I32)
-        w4_sc_raw = kept("place_b", [P, H // 4], I32)
+        tab_sc = early.tile([P, T // 4], I32, name="tab_sc", align_bytes=64, offset=0)
+        w4_sc_raw = mid.tile([P, H // 4], I32, name="w4_sc_raw", align_bytes=64, offset=S)
         tab2_sc = kept("tab2_sc", [P, T2 // 4], I32)
 
         nc.sync.dma_start(src_list[:], offs)
         nc.sync.dma_start(out=tab_sc[ROW0:P, :], in_=tab_scales.bitcast(I32).rearrange("a q c -> q a c"))
-        nc.sync.dma_start(tgt_list[:], offs2)
-        wg_raw.append(load_wg(0, "wg_first"))
         nc.sync.dma_start(out=w4_sc_raw[ROW0:P, :], in_=w4_scales.bitcast(I32).rearrange("a q c -> q a c"))
+        wg_raw.append(load_wg(0, "wg_first"))
+        nc.sync.dma_start(tgt_list[:], offs2)
         tab.append(load_words(tab_words[0], "place_a"))
         nc.sync.dma_start(out=w4_raw[:], in_=w4_words.bitcast(I32).rearrange("a p b -> p a b"))
 
         nc.vector.memset(tab2_sc[:], 0)
         nc.vector.memset(tab_sc[0:ROW0, :], 0)
         nc.vector.memset(w4_sc_raw[0:ROW0, :], 0)
-        for r in range(4):
-            nc.scalar.dma_start(out=tab2_sc[TGT_ROW + r:P:32, :], in_=tab2_scales.bitcast(I32)[0, r:16:4, :])
+        nc.scalar.dma_start(out=tab2_sc[0:P:8, :], in_=tab2_scales.bitcast(I32)[0])
         sc = kept("sc", [P, PASSES, S + H], U8)
         nc.vector.memset(sc[:].bitcast(I32), 0)
 
         ident = kept("ident", [P, P], F32)
         make_identity(nc, ident[:])
 
+        src_rows = kept("src_rows", [P, P], F32)
+        nc.gpsimd.memset(src_rows[0:96, :], 0.0)
+        nc.gpsimd.memset(src_rows[96:SRC_ROW, :], 0.0)
+        nc.scalar.dma_start(out=src_rows[SRC_ROW:P, :], in_=src_scale.rearrange("(c p) -> c p", p=P))
+        turned = bank(7, [P, P])
+        nc.tensor.transpose(turned[:], src_rows[:], ident[:])
+        src_cols = kept("src_cols", [P, S // P], F32)
+        nc.scalar.copy(out=src_cols[:], in_=turned[:, SRC_ROW:P])
+
         def spread_src(h, b):
-            spread = bank(b, [P, P, CHUNKS])
+            spread = bank(b, [P, CHUNKS, CHUNK])
             for c in range(CHUNKS):
-                nc.tensor.transpose(spread[:, :, c], src_cols[:, h, c:c + 1].to_broadcast([P, P]), ident[:])
+                col = h * CHUNKS + c
+                nc.tensor.transpose(spread[:, c, :], src_cols[:, col:col + 1].to_broadcast([P, P]), ident[:])
             return spread
 
-        picked_src_sc = kept("place_d", [P, S], U8)
+        picked_src_sc = mid.tile([P, S], U8, name="picked_src_sc", align_bytes=64, offset=0)
         nc.vector.tensor_copy(picked_src_sc[:], tab_sc[:].bitcast(U8).indirect(src_list[:]))
         rows = kept("place_e", [P, S + H], U8)
         nc.vector.tensor_copy(out=rows[:, S:S + H].rearrange("p (t m) -> p t m", t=PACK),
                               in_=w4_sc_raw[:].bitcast(U8).rearrange("p (m t) -> p t m", t=PACK))
-        wg_raw.append(load_wg(1, "place_b"))
+        mid_wg = early.tile([P, PACK, H], F32, name="mid_wg", align_bytes=64, offset=T // 2)
+        nc.sync.dma_start(out=mid_wg[:], in_=wg[PASS:2 * PASS, :].rearrange("(p j) c -> p j c", j=PACK))
+        wg_raw.append(mid_wg)
         nc.vector.tensor_copy(out=rows[:, 0:S].bitcast(I32), in_=picked_src_sc[:].bitcast(I32))
         for q in (0, 2, 1, 3):
             nc.sync.dma_start(out=sc[32 * q:32 * q + 4, :, :].bitcast(I32),
                               in_=rows[ROW0 + 12 * q:ROW0 + 12 * (q + 1), :].bitcast(I32))
-        tab.append(load_words(tab_words[1], "place_d"))
+        mid_tab = mid.tile([P, T], I32, name="mid_tab", align_bytes=64, offset=0)
+        nc.sync.dma_start(out=mid_tab[:], in_=tab_words[1].rearrange("p t i -> p (t i)").bitcast(I32))
+        tab.append(mid_tab)
         w4 = kept("w4", [P, PASSES, 2 * H], U8)
         nc.vector.tensor_copy(out=w4[:].bitcast(U16).rearrange("p a (t m) -> p a t m", t=PACK),
                               in_=w4_raw[:].bitcast(U16).rearrange("p a (m t) -> p a t m", t=PACK))
@@ -162,16 +177,19 @@ def tile_list_transport_plan_lookup_kernel(tc, tab_words, tab_scales, tab2_words
                                   in_=h_bf[h][:, cols, :].rearrange("p i t -> p (i t)"))
 
         v2 = []
-        v2_sc = kept("tgt_sc", [P, PACK, GROUPS, P], U8)
+        dealt_sc = kept("dealt_sc", [P, PACK, GROUPS, P], U8)
 
         def gather_target_scales():
-            picked = kept("place_g", [P, S2], U8)
+            picked = early.tile([P, S2], U8, name="picked_tgt_sc", align_bytes=64, offset=0)
             nc.vector.tensor_copy(picked[:], tab2_sc[:].bitcast(U8).indirect(tgt_list[:]))
-            nc.vector.tensor_copy(out=v2_sc[:].rearrange("p t g (c m) -> p (g c) t m", m=16),
+            nc.vector.tensor_copy(out=dealt_sc[:].rearrange("p t g (c m) -> p (g c) t m", m=16),
                                   in_=picked[:].rearrange("p (c m t) -> p c t m", m=16, t=PACK))
 
         def gather_targets(g0, g1):
-            picked = kept("picked", [P, (g1 - g0) * PASS], U32)
+            if g0 < GROUPS - 1:
+                picked = kept("picked", [P, PASS], U32)
+            else:
+                picked = ring.tile([P, PASS], U32, name="kern", bufs=8, align_bytes=64)
             dealt = kept("tgt_words%d" % g0, [P, PACK, (g1 - g0) * P], U32)
             nc.vector.tensor_copy(picked[:],
                                   tab2[:].bitcast(U32).indirect(tgt_list[:, g0 * LIST_COLS:g1 * LIST_COLS]))
@@ -192,10 +210,10 @@ def tile_list_transport_plan_lookup_kernel(tc, tab_words, tab_scales, tab2_words
             y = ring.tile([P, PACK, width], F32, name="y", bufs=3)
             for t in range(PACK):
                 s_bank = bank(next_bank(), [P, width])
-                nc.tensor.matmul_mx(out=s_bank[:], lhsT=v2[g][:, t, :].bitcast(FP8X4), lhsT_scale=v2_sc[TGT_ROW:P, t, g, :],
+                nc.tensor.matmul_mx(out=s_bank[:], lhsT=v2[g][:, t, :].bitcast(FP8X4), lhsT_scale=v2_sc[:, t, g, :],
                                     rhs=h_q[h][:, c0:c0 + width].bitcast(FP8X4), rhs_scale=h_sc[h][:, c0:c0 + width],
                                     start=True, stop=True)
-                kern = ring.tile([P, width], F32, name="kern", bufs=8)
+                kern = ring.tile([P, width], F32, name="kern", bufs=8, align_bytes=64)
                 nc.scalar.activation(out=kern[:], in_=s_bank[:], func=ACT.Exp, scale=0.5)
                 nc.vector.scalar_tensor_tensor(out=y[:, t, :], in0=kern[:], scalar=tgt[:, g, t:t + 1],
                                                in1=src[h][:].rearrange("p c n -> p (c n)")[:, c0:c0 + width],
@@ -234,13 +252,17 @@ def tile_list_transport_plan_lookup_kernel(tc, tab_words, tab_scales, tab2_words
                 gather_sources(a, 1, 2)
             if a == 0:
                 gather_target_scales()
-                src_cols = kept("place_f", [P, HALVES, CHUNKS], F32)
-                tgt = kept("place_g", [P, GROUPS, PACK], F32)
-                nc.sync.dma_start(out=src_cols[:], in_=src_scale.rearrange("(h p c) -> p h c", p=P, c=CHUNKS))
-                nc.sync.dma_start(out=tgt[:], in_=tgt_scale.rearrange("(g p t) -> p g t", p=P, t=PACK))
             if a == 1:
-                wg_raw.append(load_wg(2, "place_b"))
-                tab2 = load_words(tab2_words[0], "place_d")
+                last_wg = early.tile([P, PACK, H], F32, name="last_wg", align_bytes=64, offset=T // 2)
+                nc.sync.dma_start(out=last_wg[:], in_=wg[2 * PASS:3 * PASS, :].rearrange("(p j) c -> p j c", j=PACK))
+                wg_raw.append(last_wg)
+                tab2 = mid.tile([P, T2], I32, name="tab2", align_bytes=64, offset=2048)
+                nc.sync.dma_start(out=tab2[:], in_=tab2_words[0].rearrange("p t i -> p (t i)").bitcast(I32))
+                v2_sc = mid.tile([P, PACK, GROUPS, P], U8, name="v2_sc", align_bytes=64, offset=0)
+                for r in range(4):
+                    nc.sync.dma_start(out=v2_sc[r:P:32].bitcast(I32), in_=dealt_sc[8 * r:P:32].bitcast(I32))
+                tgt = mid.tile([P, GROUPS, PACK], F32, name="tgt", align_bytes=64, offset=S2 + 64)
+                nc.sync.dma_start(out=tgt[:], in_=tgt_scale.rearrange("(g p t) -> p g t", p=P, t=PACK))
             for c in range(CHUNKS):
                 project_p(banks[c][0], a, 0, c)
                 if a < PASSES - 1:
@@ -264,11 +286,12 @@ def tile_list_transport_plan_lookup_kernel(tc, tab_words, tab_scales, tab2_words
         units = [(h, g, 0, HALF) for h in range(HALVES) for g in range(GROUPS)]
         gather_targets(1, 2)
         y_prev = plan(*units[0])
-        gather_targets(2, 3)
         second_half_chunk(0)
         second_half_chunk(1)
         for n in range(1, len(units)):
             y_now = plan(*units[n])
+            if n == 1:
+                gather_targets(2, 3)
             planes(*units[n - 1], y_prev, CAST_CUTS[n - 1])
             y_prev = y_now
             if n == GROUPS:

@@ -29,7 +29,7 @@ CHUNKS = HALF // CHUNK
 LIST_COLS = HALF // 16
 QUADS = 4
 ROW0 = P - 16 * PASSES
-CAST_CUTS = [512, 448, 384, 320, 320, 192]
+CAST_CUTS = [448, 384, 352, 320, 288, 192]
 WG_CUT = 48
 SRC_ROW = P - S // P
 PLAN_BANKS = (1, 6, 7)
@@ -74,19 +74,18 @@ def tile_list_transport_plan_lookup_kernel(tc, tab_words, tab_scales, tab2_words
         tab2_sc = kept("tab2_sc", [P, T2 // 4], I32)
 
         nc.sync.dma_start(src_list[:], offs)
+        nc.sync.dma_start(out=w4_raw[:], in_=w4_words.bitcast(I32).rearrange("a p b -> p a b"))
         nc.sync.dma_start(out=tab_sc[ROW0:P, :], in_=tab_scales.bitcast(I32).rearrange("a q c -> q a c"))
         nc.sync.dma_start(out=w4_sc_raw[ROW0:P, :], in_=w4_scales.bitcast(I32).rearrange("a q c -> q a c"))
         wg_raw.append(load_wg(0, "wg_first"))
         nc.sync.dma_start(tgt_list[:], offs2)
         tab.append(load_words(tab_words[0], "place_a"))
-        nc.sync.dma_start(out=w4_raw[:], in_=w4_words.bitcast(I32).rearrange("a p b -> p a b"))
 
         nc.vector.memset(tab2_sc[:], 0)
         nc.vector.memset(tab_sc[0:ROW0, :], 0)
         nc.vector.memset(w4_sc_raw[0:ROW0, :], 0)
         nc.scalar.dma_start(out=tab2_sc[0:P:8, :], in_=tab2_scales.bitcast(I32)[0])
         sc = kept("sc", [P, PASSES, S + H], U8)
-        nc.vector.memset(sc[:].bitcast(I32), 0)
 
         ident = kept("ident", [P, P], F32)
         make_identity(nc, ident[:])
@@ -107,6 +106,9 @@ def tile_list_transport_plan_lookup_kernel(tc, tab_words, tab_scales, tab2_words
                 nc.tensor.transpose(spread[:, c, :], src_cols[:, col:col + 1].to_broadcast([P, P]), ident[:])
             return spread
 
+        w4 = kept("w4", [P, PASSES, 2 * H], U8)
+        nc.vector.tensor_copy(out=w4[:].bitcast(U16).rearrange("p a (t c m) -> p c a t m", t=PACK, c=2),
+                              in_=w4_raw[:].bitcast(U16).rearrange("p a (c m t) -> p c a t m", t=PACK, c=2))
         picked_src_sc = mid.tile([P, S], U8, name="picked_src_sc", align_bytes=64, offset=0)
         nc.vector.tensor_copy(picked_src_sc[:], tab_sc[:].bitcast(U8).indirect(src_list[:]))
         rows = kept("place_e", [P, S + H], U8)
@@ -122,9 +124,6 @@ def tile_list_transport_plan_lookup_kernel(tc, tab_words, tab_scales, tab2_words
         mid_tab = mid.tile([P, T], I32, name="mid_tab", align_bytes=64, offset=0)
         nc.sync.dma_start(out=mid_tab[:], in_=tab_words[1].rearrange("p t i -> p (t i)").bitcast(I32))
         tab.append(mid_tab)
-        w4 = kept("w4", [P, PASSES, 2 * H], U8)
-        nc.vector.tensor_copy(out=w4[:].bitcast(U16).rearrange("p a (t m) -> p a t m", t=PACK),
-                              in_=w4_raw[:].bitcast(U16).rearrange("p a (m t) -> p a t m", t=PACK))
 
         v = [kept("v%d" % a, [P, S], U32) for a in range(PASSES)]
         wg_q = [kept("wg_q%d" % a, [P, H], U32) for a in range(PASSES)]

@@ -21,83 +21,85 @@ P = 128
 PACK = 4
 PASS = P * PACK
 PASSES = K // PASS
+BLOCKS = PASS // 32
+QUAD = 32
 GROUPS = S2 // PASS
 HALF = 512
 HALVES = S // HALF
 CHUNK = 128
 CHUNKS = HALF // CHUNK
 LIST_COLS = HALF // 16
-QUADS = 4
-ROW0 = P - 16 * PASSES
-CAST_CUTS = [448, 384, 352, 320, 288, 192]
+UNITS = [(h, g) for h in range(HALVES) for g in range(GROUPS)]
+
+SC_ROW0 = P - BLOCKS * PASSES
+TGT_SC_STEP = P // BLOCKS
+SRC_ROW0 = P - S // P
+WEAVE_FIRST, WEAVE_STEP = 416, 32
 WG_CUT = 48
-SRC_ROW = P - S // P
 PLAN_BANKS = (1, 6, 7)
+KERN_BUFS = 2 * PACK
 
 
 def tile_list_transport_plan_lookup_kernel(tc, tab_words, tab_scales, tab2_words, tab2_scales, w4_words,
-                                                    w4_scales, wg, src_scale, tgt_scale, offs, offs2,
-                                                    out_0, out_1, out_2):
+                                                       w4_scales, wg, src_scale, tgt_scale, offs, offs2,
+                                                       out_0, out_1, out_2):
     nc = tc.nc
     with ExitStack() as ctx:
         lists = ctx.enter_context(tc.tile_pool(name="lists", bufs=1))
         keep = ctx.enter_context(tc.tile_pool(name="keep", bufs=1))
         ring = ctx.enter_context(tc.tile_pool(name="ring", bufs=2))
-        mid = ctx.enter_context(tc.tile_pool(name="mid", bufs=1))
-        early = ctx.enter_context(tc.tile_pool(name="early", bufs=1))
+        tab1_place = ctx.enter_context(tc.tile_pool(name="tab1_place", bufs=1))
+        wg_place = ctx.enter_context(tc.tile_pool(name="wg_place", bufs=1))
         psum = ctx.enter_context(tc.psum_pool(name="psum", bufs=1))
 
-        def kept(name, shape, dtype):
-            return keep.tile(shape, dtype, name=name, align_bytes=64)
+        def kept(tag, shape, dtype):
+            return keep.tile(shape, dtype, name=tag, align_bytes=64)
+
+        def placed(pool, name, shape, dtype, offset):
+            return pool.tile(shape, dtype, name=name, align_bytes=64, offset=offset)
 
         def bank(b, shape):
             return psum.tile(shape, F32, name="bank%d" % b)
 
-        src_list = lists.tile([P, S // 16], U16, name="src_list")
-        tgt_list = lists.tile([P, S2 // 16], U16, name="tgt_list")
-        w4_raw = kept("place_f", [P, PASSES, 2 * H // 4], I32)
-        tab, wg_raw = [], []
-
-        def load_words(words, place):
-            window = kept(place, [P, T], I32)
+        def load_words(window, words):
             nc.sync.dma_start(out=window[:], in_=words.rearrange("p t i -> p (t i)").bitcast(I32))
             return window
 
-        def load_wg(a, place):
-            raw = kept(place, [P, PACK, H], F32)
+        def load_wg(raw, a):
             nc.sync.dma_start(out=raw[:], in_=wg[a * PASS:(a + 1) * PASS, :].rearrange("(p j) c -> p j c", j=PACK))
             return raw
 
-
-        tab_sc = early.tile([P, T // 4], I32, name="tab_sc", align_bytes=64, offset=0)
-        w4_sc_raw = mid.tile([P, H // 4], I32, name="w4_sc_raw", align_bytes=64, offset=S)
+        src_list = lists.tile([P, S // 16], U16, name="src_list")
+        tgt_list = lists.tile([P, S2 // 16], U16, name="tgt_list")
+        w4_raw = kept("w4_raw", [P, PASSES, 2 * H // 4], I32)
+        tab_sc = placed(wg_place, "tab_sc", [P, T // 4], I32, 0)
+        w4_sc_raw = placed(tab1_place, "w4_sc_raw", [P, H // 4], I32, S)
         tab2_sc = kept("tab2_sc", [P, T2 // 4], I32)
 
         nc.sync.dma_start(src_list[:], offs)
         nc.sync.dma_start(out=w4_raw[:], in_=w4_words.bitcast(I32).rearrange("a p b -> p a b"))
-        nc.sync.dma_start(out=tab_sc[ROW0:P, :], in_=tab_scales.bitcast(I32).rearrange("a q c -> q a c"))
-        nc.sync.dma_start(out=w4_sc_raw[ROW0:P, :], in_=w4_scales.bitcast(I32).rearrange("a q c -> q a c"))
-        wg_raw.append(load_wg(0, "wg_first"))
+        nc.sync.dma_start(out=tab_sc[SC_ROW0:P, :], in_=tab_scales.bitcast(I32).rearrange("a q c -> q a c"))
+        nc.sync.dma_start(out=w4_sc_raw[SC_ROW0:P, :], in_=w4_scales.bitcast(I32).rearrange("a q c -> q a c"))
+        wg_raw = [load_wg(kept("wg_raw0", [P, PACK, H], F32), 0)]
         nc.sync.dma_start(tgt_list[:], offs2)
-        tab.append(load_words(tab_words[0], "place_a"))
+        tab = [load_words(kept("tab0", [P, T], I32), tab_words[0])]
 
         nc.vector.memset(tab2_sc[:], 0)
-        nc.vector.memset(tab_sc[0:ROW0, :], 0)
-        nc.vector.memset(w4_sc_raw[0:ROW0, :], 0)
-        nc.scalar.dma_start(out=tab2_sc[0:P:8, :], in_=tab2_scales.bitcast(I32)[0])
+        nc.vector.memset(tab_sc[0:SC_ROW0, :], 0)
+        nc.vector.memset(w4_sc_raw[0:SC_ROW0, :], 0)
+        nc.scalar.dma_start(out=tab2_sc[0:P:TGT_SC_STEP, :], in_=tab2_scales.bitcast(I32)[0])
         sc = kept("sc", [P, PASSES, S + H], U8)
 
         ident = kept("ident", [P, P], F32)
         make_identity(nc, ident[:])
-
         src_rows = kept("src_rows", [P, P], F32)
-        nc.gpsimd.memset(src_rows[0:96, :], 0.0)
-        nc.gpsimd.memset(src_rows[96:SRC_ROW, :], 0.0)
-        nc.scalar.dma_start(out=src_rows[SRC_ROW:P, :], in_=src_scale.rearrange("(c p) -> c p", p=P))
+        nc.gpsimd.memset(src_rows[0:P - QUAD, :], 0.0)
+        nc.gpsimd.memset(src_rows[P - QUAD:SRC_ROW0, :], 0.0)
+        nc.scalar.dma_start(out=src_rows[SRC_ROW0:P, :], in_=src_scale.rearrange("(c p) -> c p", p=P))
         turned = bank(7, [P, P])
         nc.tensor.transpose(turned[:], src_rows[:], ident[:])
         src_cols = kept("src_cols", [P, S // P], F32)
-        nc.scalar.copy(out=src_cols[:], in_=turned[:, SRC_ROW:P])
+        nc.scalar.copy(out=src_cols[:], in_=turned[:, SRC_ROW0:P])
 
         def spread_src(h, b):
             spread = bank(b, [P, CHUNKS, CHUNK])
@@ -109,32 +111,33 @@ def tile_list_transport_plan_lookup_kernel(tc, tab_words, tab_scales, tab2_words
         w4 = kept("w4", [P, PASSES, 2 * H], U8)
         nc.vector.tensor_copy(out=w4[:].bitcast(U16).rearrange("p a (t c m) -> p c a t m", t=PACK, c=2),
                               in_=w4_raw[:].bitcast(U16).rearrange("p a (c m t) -> p c a t m", t=PACK, c=2))
-        picked_src_sc = mid.tile([P, S], U8, name="picked_src_sc", align_bytes=64, offset=0)
+        picked_src_sc = placed(tab1_place, "picked_src_sc", [P, S], U8, 0)
         nc.vector.tensor_copy(picked_src_sc[:], tab_sc[:].bitcast(U8).indirect(src_list[:]))
-        rows = kept("place_e", [P, S + H], U8)
-        nc.vector.tensor_copy(out=rows[:, S:S + H].rearrange("p (t m) -> p t m", t=PACK),
+        sc_rows = kept("tab_last", [P, S + H], U8)
+        nc.vector.tensor_copy(out=sc_rows[:, S:S + H].rearrange("p (t m) -> p t m", t=PACK),
                               in_=w4_sc_raw[:].bitcast(U8).rearrange("p (m t) -> p t m", t=PACK))
-        mid_wg = early.tile([P, PACK, H], F32, name="mid_wg", align_bytes=64, offset=T // 2)
-        nc.sync.dma_start(out=mid_wg[:], in_=wg[PASS:2 * PASS, :].rearrange("(p j) c -> p j c", j=PACK))
-        wg_raw.append(mid_wg)
-        nc.vector.tensor_copy(out=rows[:, 0:S].bitcast(I32), in_=picked_src_sc[:].bitcast(I32))
-        for q in (0, 2, 1, 3):
-            nc.sync.dma_start(out=sc[32 * q:32 * q + 4, :, :].bitcast(I32),
-                              in_=rows[ROW0 + 12 * q:ROW0 + 12 * (q + 1), :].bitcast(I32))
-        mid_tab = mid.tile([P, T], I32, name="mid_tab", align_bytes=64, offset=0)
-        nc.sync.dma_start(out=mid_tab[:], in_=tab_words[1].rearrange("p t i -> p (t i)").bitcast(I32))
-        tab.append(mid_tab)
+        wg_raw.append(load_wg(placed(wg_place, "wg_raw1", [P, PACK, H], F32, T // 2), 1))
+        nc.vector.tensor_copy(out=sc_rows[:, 0:S].bitcast(I32), in_=picked_src_sc[:].bitcast(I32))
+        rows_a_quad = PACK * PASSES
+        for quad in (0, 2, 1, 3):
+            first = SC_ROW0 + rows_a_quad * quad
+            nc.sync.dma_start(out=sc[QUAD * quad:QUAD * quad + PACK, :, :].bitcast(I32),
+                              in_=sc_rows[first:first + rows_a_quad, :].bitcast(I32))
+        tab.append(load_words(placed(tab1_place, "tab1", [P, T], I32, 0), tab_words[1]))
 
-        v = [kept("v%d" % a, [P, S], U32) for a in range(PASSES)]
+        v = {}
         wg_q = [kept("wg_q%d" % a, [P, H], U32) for a in range(PASSES)]
         wg_sc = [kept("wg_sc%d" % a, [P, H], U8) for a in range(PASSES)]
 
-        def gather_sources(a, h0, h1):
-            nc.vector.tensor_copy(v[a][:, h0 * HALF:h1 * HALF],
+        def gather_sources(a, h0, h1, tag):
+            picked = kept(tag, [P, (h1 - h0) * HALF], U32)
+            nc.vector.tensor_copy(picked[:],
                                   tab[a][:].bitcast(U32).indirect(src_list[:, h0 * LIST_COLS:h1 * LIST_COLS]))
+            for h in range(h0, h1):
+                v[a, h] = picked[:, (h - h0) * HALF:(h - h0 + 1) * HALF]
 
         def quantise_wg(a, cut):
-            rounded = ring.tile([P, PACK * H], BF16, name="wg_bf", align_bytes=64)
+            rounded = kept("wg_bf", [P, PACK * H], BF16)
             dst = rounded[:].rearrange("p (u t m j) -> p u m j t", u=2, t=2, j=PACK)
             raw = wg_raw[a][:].rearrange("p j (m u t) -> p u m j t", u=2, t=2)
             nc.scalar.copy(out=dst[:, :, 0:cut], in_=raw[:, :, 0:cut])
@@ -142,137 +145,130 @@ def tile_list_transport_plan_lookup_kernel(tc, tab_words, tab_scales, tab2_words
                 nc.vector.tensor_copy(out=dst[:, :, cut:P], in_=raw[:, :, cut:P])
             nc.vector.quantize_mx(out=wg_q[a][:].bitcast(FP8X4), scales=wg_sc[a][:], in_=rounded[:])
 
-        def project_g(g_bank, a, h, c):
+        def project(out_bank, words, scales, a, h, c):
             sc_cols = slice(h * HALF + c * CHUNK, h * HALF + (c + 1) * CHUNK)
             for t in range(PACK):
-                nc.tensor.matmul_mx(
-                    out=g_bank[:, t, :],
-                    lhsT=wg_q[a][:, t * P:(t + 1) * P].bitcast(FP8X4), lhsT_scale=wg_sc[a][:, t * P:(t + 1) * P],
-                    rhs=v[a][:, sc_cols].bitcast(FP8X4), rhs_scale=sc[:, a, sc_cols],
-                    start=(a == 0 and t == 0), stop=(a == PASSES - 1 and t == PACK - 1))
+                nc.tensor.matmul_mx(out=out_bank[:, t, :], lhsT=words(a, t), lhsT_scale=scales(a, t),
+                                    rhs=v[a, h][:, c * CHUNK:(c + 1) * CHUNK].bitcast(FP8X4), rhs_scale=sc[:, a, sc_cols],
+                                    start=(a == 0 and t == 0), stop=(a == PASSES - 1 and t == PACK - 1))
+
+        def project_g(g_bank, a, h, c):
+            project(g_bank, lambda a, t: wg_q[a][:, t * P:(t + 1) * P].bitcast(FP8X4),
+                    lambda a, t: wg_sc[a][:, t * P:(t + 1) * P], a, h, c)
 
         def project_p(p_bank, a, h, c):
-            sc_cols = slice(h * HALF + c * CHUNK, h * HALF + (c + 1) * CHUNK)
-            for t in range(PACK):
-                nc.tensor.matmul_mx(
-                    out=p_bank[:, t, :],
-                    lhsT=w4[:, a, 2 * t * P:2 * (t + 1) * P].bitcast(FP4X4), lhsT_scale=sc[:, a, S + t * P:S + (t + 1) * P],
-                    rhs=v[a][:, sc_cols].bitcast(FP8X4), rhs_scale=sc[:, a, sc_cols],
-                    start=(a == 0 and t == 0), stop=(a == PASSES - 1 and t == PACK - 1))
+            project(p_bank, lambda a, t: w4[:, a, 2 * t * P:2 * (t + 1) * P].bitcast(FP4X4),
+                    lambda a, t: sc[:, a, S + t * P:S + (t + 1) * P], a, h, c)
 
         h_bf = [kept("h_bf%d" % h, [P, HALF, PACK], BF16) for h in range(HALVES)]
         h_q = [kept("h_q%d" % h, [P, HALF], U32) for h in range(HALVES)]
         h_sc = [kept("h_sc%d" % h, [P, HALF], U8) for h in range(HALVES)]
 
         def gate(p_bank, g_bank, h, c):
-            th = ring.tile([P, CHUNK, PACK], F32, name="tanh", bufs=3)
-            nc.scalar.activation(out=th[:], in_=g_bank[:].rearrange("p t n -> p n t"), func=ACT.Tanh, scale=0.5)
-            nc.vector.scalar_tensor_tensor(out=h_bf[h][:, c * CHUNK:(c + 1) * CHUNK, :], in0=th[:], scalar=1.0,
+            tanh = ring.tile([P, CHUNK, PACK], F32, name="tanh", bufs=3)
+            nc.scalar.activation(out=tanh[:], in_=g_bank[:].rearrange("p t n -> p n t"), func=ACT.Tanh, scale=0.5)
+            nc.vector.scalar_tensor_tensor(out=h_bf[h][:, c * CHUNK:(c + 1) * CHUNK, :], in0=tanh[:], scalar=1.0,
                                            in1=p_bank[:].rearrange("p t n -> p n t"), op0=ALU.add, op1=ALU.mult)
 
-        def quantise_h(h, c0, width):
-            cols = slice(c0, c0 + width)
-            nc.vector.quantize_mx(out=h_q[h][:, cols].bitcast(FP8X4), scales=h_sc[h][:, cols],
-                                  in_=h_bf[h][:, cols, :].rearrange("p i t -> p (i t)"))
+        def quantise_h(h):
+            nc.vector.quantize_mx(out=h_q[h][:].bitcast(FP8X4), scales=h_sc[h][:],
+                                  in_=h_bf[h][:].rearrange("p i t -> p (i t)"))
 
         v2 = []
         dealt_sc = kept("dealt_sc", [P, PACK, GROUPS, P], U8)
 
         def gather_target_scales():
-            picked = early.tile([P, S2], U8, name="picked_tgt_sc", align_bytes=64, offset=0)
+            picked = placed(wg_place, "picked_tgt_sc", [P, S2], U8, 0)
             nc.vector.tensor_copy(picked[:], tab2_sc[:].bitcast(U8).indirect(tgt_list[:]))
             nc.vector.tensor_copy(out=dealt_sc[:].rearrange("p t g (c m) -> p (g c) t m", m=16),
                                   in_=picked[:].rearrange("p (c m t) -> p c t m", m=16, t=PACK))
 
-        def gather_targets(g0, g1):
-            if g0 < GROUPS - 1:
-                picked = kept("picked", [P, PASS], U32)
-            else:
-                picked = ring.tile([P, PASS], U32, name="kern", bufs=8, align_bytes=64)
-            dealt = kept("tgt_words%d" % g0, [P, PACK, (g1 - g0) * P], U32)
+        def gather_targets(g, picked):
+            dealt = kept("tgt_words%d" % g, [P, PACK, P], U32)
             nc.vector.tensor_copy(picked[:],
-                                  tab2[:].bitcast(U32).indirect(tgt_list[:, g0 * LIST_COLS:g1 * LIST_COLS]))
+                                  tab2[:].bitcast(U32).indirect(tgt_list[:, g * LIST_COLS:(g + 1) * LIST_COLS]))
             nc.vector.tensor_copy(out=dealt[:].rearrange("p t (c m) -> p c t m", m=4),
                                   in_=picked[:].rearrange("p (c m t) -> p c t m", m=4, t=PACK))
-            v2.extend(dealt[:, :, g * P:(g + 1) * P] for g in range(g1 - g0))
+            v2.append(dealt)
+
+        def kern_buffer(dtype):
+            return ring.tile([P, HALF], dtype, name="kern", bufs=KERN_BUFS, align_bytes=64)
 
         y_sc = [kept("y_sc%d" % h, [P, GROUPS, HALF], U8) for h in range(HALVES)]
 
-        banks_used = []
-
-        def next_bank():
-            banks_used.append(PLAN_BANKS[len(banks_used) % len(PLAN_BANKS)])
-            return banks_used[-1]
-
-        def plan(h, g, c0, width):
-            cols = slice(h * HALF + c0, h * HALF + c0 + width)
-            y = ring.tile([P, PACK, width], F32, name="y", bufs=3)
+        def plan(n):
+            h, g = UNITS[n]
+            rows_out = out_0[g * PASS:(g + 1) * PASS, h * HALF:(h + 1) * HALF].rearrange("(p t) i -> p t i", t=PACK)
+            y = ring.tile([P, PACK, HALF], F32, name="y", bufs=4)
             for t in range(PACK):
-                s_bank = bank(next_bank(), [P, width])
+                s_bank = bank(PLAN_BANKS[(PACK * n + t) % len(PLAN_BANKS)], [P, HALF])
                 nc.tensor.matmul_mx(out=s_bank[:], lhsT=v2[g][:, t, :].bitcast(FP8X4), lhsT_scale=v2_sc[:, t, g, :],
-                                    rhs=h_q[h][:, c0:c0 + width].bitcast(FP8X4), rhs_scale=h_sc[h][:, c0:c0 + width],
-                                    start=True, stop=True)
-                kern = ring.tile([P, width], F32, name="kern", bufs=8, align_bytes=64)
+                                    rhs=h_q[h][:].bitcast(FP8X4), rhs_scale=h_sc[h][:], start=True, stop=True)
+                kern = kern_buffer(F32)
                 nc.scalar.activation(out=kern[:], in_=s_bank[:], func=ACT.Exp, scale=0.5)
                 nc.vector.scalar_tensor_tensor(out=y[:, t, :], in0=kern[:], scalar=tgt[:, g, t:t + 1],
-                                               in1=src[h][:].rearrange("p c n -> p (c n)")[:, c0:c0 + width],
-                                               op0=ALU.mult, op1=ALU.mult)
-                if t % 2 == 1:
-                    rows_out = out_0[g * PASS:(g + 1) * PASS, cols].rearrange("(p t) i -> p t i", t=PACK)
-                    nc.sync.dma_start(out=rows_out[:, t - 1:t + 1, :], in_=y[:, t - 1:t + 1, :])
+                                               in1=src[h][:].rearrange("p c n -> p (c n)"), op0=ALU.mult, op1=ALU.mult)
+                nc.sync.dma_start(out=rows_out[:, t, :], in_=y[:, t, :])
             return y
 
-        def planes(h, g, c0, width, y, cut2):
-            cols = slice(h * HALF + c0, h * HALF + c0 + width)
-            y_bf = ring.tile([P, width, PACK], BF16, name="y_bf", bufs=2, align_bytes=64)
-            nc.scalar.copy(out=y_bf[:, 0:cut2, :].rearrange("p (c i) t -> p c t i", i=2),
-                           in_=y[:, :, 0:cut2].rearrange("p t (c i) -> p c t i", i=2))
-            if cut2 < width:
-                nc.vector.tensor_copy(out=y_bf[:, cut2:width, :].rearrange("p (c i) t -> p c t i", i=2),
-                                      in_=y[:, :, cut2:width].rearrange("p t (c i) -> p c t i", i=2))
-            y_q = ring.tile([P, width], U32, name="y_q", bufs=3, align_bytes=64)
-            nc.vector.quantize_mx(out=y_q[:].bitcast(FP8X4), scales=y_sc[h][:, g, c0:c0 + width],
-                                  in_=y_bf[:].rearrange("p i t -> p (i t)"))
-            nc.sync.dma_start(out=out_1[g].rearrange("p m t -> p (m t)").bitcast(I32)[:, cols], in_=y_q[:].bitcast(I32))
+        def planes(n, y, parts):
+            h, g = UNITS[n]
+            cut = WEAVE_FIRST - WEAVE_STEP * n
+            y_bf = ring.tile([P, HALF, PACK], BF16, name="y_bf", bufs=3, align_bytes=64)
+            nc.scalar.copy(out=y_bf[:, 0:cut, :].rearrange("p (c i) t -> p c t i", i=2),
+                           in_=y[:, :, 0:cut].rearrange("p t (c i) -> p c t i", i=2))
+            nc.vector.tensor_copy(out=y_bf[:, cut:HALF, :].rearrange("p (c i) t -> p c t i", i=2),
+                                  in_=y[:, :, cut:HALF].rearrange("p t (c i) -> p c t i", i=2))
+            y_q = ring.tile([P, HALF], U32, name="y_q", bufs=3, align_bytes=64)
+            words_out = out_1[g].rearrange("p m t -> p (m t)").bitcast(I32)[:, h * HALF:(h + 1) * HALF]
+            for part in parts:
+                nc.vector.quantize_mx(out=y_q[:, part].bitcast(FP8X4), scales=y_sc[h][:, g, part],
+                                      in_=y_bf[:, part, :].rearrange("p i t -> p (i t)"))
+                nc.sync.dma_start(out=words_out[:, part], in_=y_q[:, part].bitcast(I32))
 
-        def store_scales(h):
-            for r in range(4):
-                nc.sync.dma_start(out=out_2.bitcast(I32)[:, r:16:4, h * P:(h + 1) * P].rearrange("g q m -> q g m"),
-                                  in_=y_sc[h][r:P:32, :, :].bitcast(I32))
+        def store_scales(h, queue):
+            word_cols = slice(h * HALF // 4, (h + 1) * HALF // 4)
+            for r in range(PACK):
+                queue.dma_start(out=out_2.bitcast(I32)[:, r:BLOCKS:PACK, word_cols].rearrange("g q m -> q g m"),
+                                in_=y_sc[h][r:P:QUAD, :, :].bitcast(I32))
 
         banks = [(bank(2 * c, [P, PACK, CHUNK]), bank(2 * c + 1, [P, PACK, CHUNK])) for c in range(CHUNKS)]
-        tab.append(load_words(tab_words[2], "place_e"))
-        for a in range(PASSES):
-            if a < PASSES - 1:
-                quantise_wg(a, P)
-                gather_sources(a, 0, 2)
-            else:
-                gather_sources(a, 0, 1)
-                gather_sources(a, 1, 2)
-            if a == 0:
-                gather_target_scales()
-            if a == 1:
-                last_wg = early.tile([P, PACK, H], F32, name="last_wg", align_bytes=64, offset=T // 2)
-                nc.sync.dma_start(out=last_wg[:], in_=wg[2 * PASS:3 * PASS, :].rearrange("(p j) c -> p j c", j=PACK))
-                wg_raw.append(last_wg)
-                tab2 = mid.tile([P, T2], I32, name="tab2", align_bytes=64, offset=2048)
-                nc.sync.dma_start(out=tab2[:], in_=tab2_words[0].rearrange("p t i -> p (t i)").bitcast(I32))
-                v2_sc = mid.tile([P, PACK, GROUPS, P], U8, name="v2_sc", align_bytes=64, offset=0)
-                for r in range(4):
-                    nc.sync.dma_start(out=v2_sc[r:P:32].bitcast(I32), in_=dealt_sc[8 * r:P:32].bitcast(I32))
-                tgt = mid.tile([P, GROUPS, PACK], F32, name="tgt", align_bytes=64, offset=S2 + 64)
-                nc.sync.dma_start(out=tgt[:], in_=tgt_scale.rearrange("(g p t) -> p g t", p=P, t=PACK))
-            for c in range(CHUNKS):
-                project_p(banks[c][0], a, 0, c)
-                if a < PASSES - 1:
-                    project_g(banks[c][1], a, 0, c)
-        quantise_wg(PASSES - 1, WG_CUT)
+        last = PASSES - 1
+        tab.append(load_words(kept("tab_last", [P, T], I32), tab_words[last]))
+
+        quantise_wg(0, P)
+        gather_sources(0, 0, HALVES, "v0")
+        gather_target_scales()
         for c in range(CHUNKS):
-            project_g(banks[c][1], PASSES - 1, 0, c)
+            project_p(banks[c][0], 0, 0, c)
+            project_g(banks[c][1], 0, 0, c)
+
+        quantise_wg(1, P)
+        gather_sources(1, 0, HALVES, "v1")
+        wg_raw.append(load_wg(placed(wg_place, "wg_raw2", [P, PACK, H], F32, T // 2), last))
+        tgt_offset = S2 + 64
+        tab2_offset = 2048
+        tab2 = load_words(placed(tab1_place, "tab2", [P, T2], I32, tab2_offset), tab2_words[0])
+        v2_sc = placed(tab1_place, "v2_sc", [P, PACK, GROUPS, P], U8, 0)
+        for r in range(PACK):
+            nc.sync.dma_start(out=v2_sc[r:P:QUAD].bitcast(I32), in_=dealt_sc[TGT_SC_STEP * r:P:QUAD].bitcast(I32))
+        tgt = placed(tab1_place, "tgt", [P, GROUPS, PACK], F32, tgt_offset)
+        nc.sync.dma_start(out=tgt[:], in_=tgt_scale.rearrange("(g p t) -> p g t", p=P, t=PACK))
+        for c in range(CHUNKS):
+            project_p(banks[c][0], 1, 0, c)
+            project_g(banks[c][1], 1, 0, c)
+
+        gather_sources(last, 0, 1, "v2_first")
+        for c in range(CHUNKS):
+            project_p(banks[c][0], last, 0, c)
+        quantise_wg(last, WG_CUT)
+        gather_sources(last, 1, HALVES, "wg_bf")
+        for c in range(CHUNKS):
+            project_g(banks[c][1], last, 0, c)
             gate(banks[c][0], banks[c][1], 0, c)
         src = [spread_src(0, 0)]
-        gather_targets(0, 1)
-        quantise_h(0, 0, HALF)
+        gather_targets(0, kept("picked", [P, PASS], U32))
+        quantise_h(0)
 
         def second_half_chunk(c):
             p_bank, g_bank = bank(2 + 2 * (c % 2), [P, PACK, CHUNK]), bank(3 + 2 * (c % 2), [P, PACK, CHUNK])
@@ -282,24 +278,22 @@ def tile_list_transport_plan_lookup_kernel(tc, tab_words, tab_scales, tab2_words
                 project_p(p_bank, a, 1, c)
             gate(p_bank, g_bank, 1, c)
 
-        units = [(h, g, 0, HALF) for h in range(HALVES) for g in range(GROUPS)]
-        gather_targets(1, 2)
-        y_prev = plan(*units[0])
+        whole = [slice(0, HALF)]
+        gather_targets(1, kept("picked", [P, PASS], U32))
+        y_prev = plan(0)
         second_half_chunk(0)
         second_half_chunk(1)
-        for n in range(1, len(units)):
-            y_now = plan(*units[n])
-            if n == 1:
-                gather_targets(2, 3)
-            planes(*units[n - 1], y_prev, CAST_CUTS[n - 1])
-            y_prev = y_now
+        y_now = plan(1)
+        gather_targets(2, kern_buffer(U32))
+        planes(0, y_prev, whole)
+        second_half_chunk(2)
+        second_half_chunk(3)
+        quantise_h(1)
+        src.append(spread_src(1, 2))
+        for n in range(2, len(UNITS)):
+            y_prev, y_now = y_now, plan(n)
+            planes(n - 1, y_prev, whole)
             if n == GROUPS:
-                store_scales(0)
-            if n == 1:
-                second_half_chunk(2)
-                second_half_chunk(3)
-                quantise_h(1, 0, HALF)
-                src.append(spread_src(1, 2))
-        planes(*units[-1], y_prev, CAST_CUTS[-1])
-
-        store_scales(1)
+                store_scales(0, nc.sync)
+        planes(len(UNITS) - 1, y_now, [slice(HALF // 2, HALF), slice(0, HALF // 2)])
+        store_scales(1, nc.scalar)

@@ -84,6 +84,14 @@ def tile_list_transport_plan_lookup_kernel(tc, tab_words, tab_scales, tab2_words
         nc.sync.dma_start(tgt_list[:], offs2)
         tab = [load_words(kept("tab0", [P, T], I32), tab_words[0])]
 
+        tgt = kept("tgt", [P, GROUPS * PACK], F32)
+        nc.scalar.dma_start(out=tgt[:].rearrange("p (g t) -> p g t", t=PACK),
+                            in_=tgt_scale.rearrange("(g p t) -> p g t", p=P, t=PACK))
+        ln_tgt = kept("ln_tgt", [P, GROUPS * PACK], F32)
+        nc.scalar.activation(out=ln_tgt[:], in_=tgt[:], func=ACT.Ln)
+        warm = kept("warm", [P, 1], F32)
+        nc.scalar.activation(out=warm[:], in_=ln_tgt[:, 0:1], func=ACT.Tanh)
+
         nc.vector.memset(tab2_sc[:], 0)
         nc.vector.memset(tab_sc[0:SC_ROW0, :], 0)
         nc.vector.memset(w4_sc_raw[0:SC_ROW0, :], 0)
@@ -99,7 +107,7 @@ def tile_list_transport_plan_lookup_kernel(tc, tab_words, tab_scales, tab2_words
         turned = bank(7, [P, P])
         nc.tensor.transpose(turned[:], src_rows[:], ident[:])
         src_cols = kept("src_cols", [P, S // P], F32)
-        nc.scalar.copy(out=src_cols[:], in_=turned[:, SRC_ROW0:P])
+        nc.vector.tensor_copy(out=src_cols[:], in_=turned[:, SRC_ROW0:P])
 
         def spread_src(h, b):
             spread = bank(b, [P, CHUNKS, CHUNK])
@@ -205,26 +213,36 @@ def tile_list_transport_plan_lookup_kernel(tc, tab_words, tab_scales, tab2_words
                 nc.tensor.matmul_mx(out=s_bank[:], lhsT=v2[g][:, t, :].bitcast(FP8X4), lhsT_scale=v2_sc[:, t, g, :],
                                     rhs=h_q[h][:].bitcast(FP8X4), rhs_scale=h_sc[h][:], start=True, stop=True)
                 kern = kern_buffer(F32)
-                nc.scalar.activation(out=kern[:], in_=s_bank[:], func=ACT.Exp, scale=0.5)
-                nc.vector.scalar_tensor_tensor(out=y[:, t, :], in0=kern[:], scalar=tgt[:, g, t:t + 1],
-                                               in1=src[h][:].rearrange("p c n -> p (c n)"), op0=ALU.mult, op1=ALU.mult)
+                nc.scalar.activation(out=kern[:], in_=s_bank[:], func=ACT.Exp, scale=0.5,
+                                     bias=ln_tgt[:, PACK * g + t:PACK * g + t + 1])
+                nc.vector.tensor_tensor(out=y[:, t, :], in0=kern[:], in1=src[h][:].rearrange("p c n -> p (c n)"),
+                                        op=ALU.mult)
                 nc.sync.dma_start(out=rows_out[:, t, :], in_=y[:, t, :])
             return y
 
         def planes(n, y, parts):
             h, g = UNITS[n]
-            cut = WEAVE_FIRST - WEAVE_STEP * n
-            y_bf = ring.tile([P, HALF, PACK], BF16, name="y_bf", bufs=3, align_bytes=64)
-            nc.scalar.copy(out=y_bf[:, 0:cut, :].rearrange("p (c i) t -> p c t i", i=2),
+            cut = HALF // 2
+            low = ring.tile([P, cut, PACK], BF16, name="y_bf_low", bufs=3, align_bytes=64)
+            high = ring.tile([P, cut, PACK], BF16, name="y_bf_high", bufs=1, align_bytes=64)
+            nc.scalar.copy(out=low[:].rearrange("p (c i) t -> p c t i", i=2),
                            in_=y[:, :, 0:cut].rearrange("p t (c i) -> p c t i", i=2))
-            nc.vector.tensor_copy(out=y_bf[:, cut:HALF, :].rearrange("p (c i) t -> p c t i", i=2),
-                                  in_=y[:, :, cut:HALF].rearrange("p t (c i) -> p c t i", i=2))
+            if n < len(UNITS) - 1:
+                nc.gpsimd.tensor_scalar(out=high[:], in0=y[:, :, cut:HALF].rearrange("p t i -> p i t"),
+                                        scalar1=1.0, scalar2=0.0, op0=ALU.mult, op1=ALU.add)
+            else:
+                nc.vector.tensor_copy(out=high[:].rearrange("p (c i) t -> p c t i", i=2),
+                                      in_=y[:, :, cut:HALF].rearrange("p t (c i) -> p c t i", i=2))
             y_q = ring.tile([P, HALF], U32, name="y_q", bufs=3, align_bytes=64)
             words_out = out_1[g].rearrange("p m t -> p (m t)").bitcast(I32)[:, h * HALF:(h + 1) * HALF]
             for part in parts:
+                y_bf = low if part.start == 0 else high
                 nc.vector.quantize_mx(out=y_q[:, part].bitcast(FP8X4), scales=y_sc[h][:, g, part],
-                                      in_=y_bf[:, part, :].rearrange("p i t -> p (i t)"))
-                nc.sync.dma_start(out=words_out[:, part], in_=y_q[:, part].bitcast(I32))
+                                      in_=y_bf[:].rearrange("p i t -> p (i t)"))
+                if n == len(UNITS) - 1:
+                    nc.sync.dma_start(out=words_out[:, part], in_=y_q[:, part].bitcast(I32))
+            if n < len(UNITS) - 1:
+                nc.sync.dma_start(out=words_out, in_=y_q[:].bitcast(I32))
 
         def store_scales(h, queue):
             word_cols = slice(h * HALF // 4, (h + 1) * HALF // 4)
@@ -246,14 +264,11 @@ def tile_list_transport_plan_lookup_kernel(tc, tab_words, tab_scales, tab2_words
         quantise_wg(1, P)
         gather_sources(1, 0, HALVES, "v1")
         wg_raw.append(load_wg(placed(wg_place, "wg_raw2", [P, PACK, H], F32, T // 2), last))
-        tgt_offset = S2 + 64
         tab2_offset = 2048
         tab2 = load_words(placed(tab1_place, "tab2", [P, T2], I32, tab2_offset), tab2_words[0])
         v2_sc = placed(tab1_place, "v2_sc", [P, PACK, GROUPS, P], U8, 0)
         for r in range(PACK):
             nc.sync.dma_start(out=v2_sc[r:P:QUAD].bitcast(I32), in_=dealt_sc[TGT_SC_STEP * r:P:QUAD].bitcast(I32))
-        tgt = placed(tab1_place, "tgt", [P, GROUPS, PACK], F32, tgt_offset)
-        nc.sync.dma_start(out=tgt[:], in_=tgt_scale.rearrange("(g p t) -> p g t", p=P, t=PACK))
         for c in range(CHUNKS):
             project_p(banks[c][0], 1, 0, c)
             project_g(banks[c][1], 1, 0, c)
@@ -278,7 +293,7 @@ def tile_list_transport_plan_lookup_kernel(tc, tab_words, tab_scales, tab2_words
                 project_p(p_bank, a, 1, c)
             gate(p_bank, g_bank, 1, c)
 
-        whole = [slice(0, HALF)]
+        whole = [slice(0, HALF // 2), slice(HALF // 2, HALF)]
         gather_targets(1, kept("picked", [P, PASS], U32))
         y_prev = plan(0)
         second_half_chunk(0)
@@ -296,4 +311,4 @@ def tile_list_transport_plan_lookup_kernel(tc, tab_words, tab_scales, tab2_words
             if n == GROUPS:
                 store_scales(0, nc.sync)
         planes(len(UNITS) - 1, y_now, [slice(HALF // 2, HALF), slice(0, HALF // 2)])
-        store_scales(1, nc.scalar)
+        store_scales(1, nc.sync)

@@ -191,12 +191,10 @@ def tile_list_transport_plan_lookup_kernel(tc, tab_words, tab_scales, tab2_words
             nc.vector.tensor_copy(out=dealt_sc[:].rearrange("p t g (c m) -> p (g c) t m", m=16),
                                   in_=picked[:].rearrange("p (c m t) -> p c t m", m=16, t=PACK))
 
-        def gather_targets(g, picked):
-            dealt = kept("tgt_words%d" % g, [P, PACK, P], U32)
-            nc.vector.tensor_copy(picked[:],
+        def gather_targets(g, flat):
+            dealt = flat[:].rearrange("p (t m) -> p t m", t=PACK)
+            nc.vector.tensor_copy(dealt.rearrange("p t m -> p m t"),
                                   tab2[:].bitcast(U32).indirect(tgt_list[:, g * LIST_COLS:(g + 1) * LIST_COLS]))
-            nc.vector.tensor_copy(out=dealt[:].rearrange("p t (c m) -> p c t m", m=4),
-                                  in_=picked[:].rearrange("p (c m t) -> p c t m", m=4, t=PACK))
             v2.append(dealt)
 
         def kern_buffer(dtype):
@@ -282,7 +280,7 @@ def tile_list_transport_plan_lookup_kernel(tc, tab_words, tab_scales, tab2_words
             project_g(banks[c][1], last, 0, c)
             gate(banks[c][0], banks[c][1], 0, c)
         src = [spread_src(0, 0)]
-        gather_targets(0, kept("picked", [P, PASS], U32))
+        gather_targets(0, kept("tgt_words0", [P, PASS], U32))
         quantise_h(0)
 
         def second_half_chunk(c):
@@ -294,12 +292,12 @@ def tile_list_transport_plan_lookup_kernel(tc, tab_words, tab_scales, tab2_words
             gate(p_bank, g_bank, 1, c)
 
         whole = [slice(0, HALF // 2), slice(HALF // 2, HALF)]
-        gather_targets(1, kept("picked", [P, PASS], U32))
+        gather_targets(1, kept("tgt_words1", [P, PASS], U32))
         y_prev = plan(0)
         second_half_chunk(0)
         second_half_chunk(1)
         y_now = plan(1)
-        gather_targets(2, kern_buffer(U32))
+        gather_targets(2, kept("tgt_words2", [P, PASS], U32))
         planes(0, y_prev, whole)
         second_half_chunk(2)
         second_half_chunk(3)

@@ -38,6 +38,8 @@ WEAVE_FIRST, WEAVE_STEP = 416, 32
 WG_CUT = 48
 PLAN_BANKS = (1, 6, 7)
 KERN_BUFS = 2 * PACK
+Y_BYTES = PACK * HALF * 4
+TURNS = 4
 
 
 def tile_list_transport_plan_lookup_kernel(tc, tab_words, tab_scales, tab2_words, tab2_scales, w4_words,
@@ -50,6 +52,7 @@ def tile_list_transport_plan_lookup_kernel(tc, tab_words, tab_scales, tab2_words
         ring = ctx.enter_context(tc.tile_pool(name="ring", bufs=2))
         tab1_place = ctx.enter_context(tc.tile_pool(name="tab1_place", bufs=1))
         wg_place = ctx.enter_context(tc.tile_pool(name="wg_place", bufs=1))
+        turns = ctx.enter_context(tc.tile_pool(name="turns", bufs=1))
         psum = ctx.enter_context(tc.psum_pool(name="psum", bufs=1))
 
         def kept(tag, shape, dtype):
@@ -115,6 +118,10 @@ def tile_list_transport_plan_lookup_kernel(tc, tab_words, tab_scales, tab2_words
                 col = h * CHUNKS + c
                 nc.tensor.transpose(spread[:, c, :], src_cols[:, col:col + 1].to_broadcast([P, P]), ident[:])
             return spread
+
+        src_sbuf = kept("src_sbuf", [P, HALVES, HALF], F32)
+        for h in range(HALVES):
+            nc.scalar.copy(out=src_sbuf[:, h, :], in_=spread_src(h, 5 + h)[:].rearrange("p c n -> p (c n)"))
 
         w4 = kept("w4", [P, PASSES, 2 * H], U8)
         nc.vector.tensor_copy(out=w4[:].bitcast(U16).rearrange("p a (t c m) -> p c a t m", t=PACK, c=2),
@@ -205,32 +212,38 @@ def tile_list_transport_plan_lookup_kernel(tc, tab_words, tab_scales, tab2_words
         def plan(n):
             h, g = UNITS[n]
             rows_out = out_0[g * PASS:(g + 1) * PASS, h * HALF:(h + 1) * HALF].rearrange("(p t) i -> p t i", t=PACK)
-            y = ring.tile([P, PACK, HALF], F32, name="y", bufs=4)
+            if n < 2:
+                y = placed(tab1_place, "y%d" % n, [P, PACK, HALF], F32, tab2_offset + n * Y_BYTES)
+            else:
+                y = placed(turns, "y%d" % n, [P, PACK, HALF], F32, (n - 1) % TURNS * Y_BYTES)
             for t in range(PACK):
                 s_bank = bank(PLAN_BANKS[(PACK * n + t) % len(PLAN_BANKS)], [P, HALF])
                 nc.tensor.matmul_mx(out=s_bank[:], lhsT=v2[g][:, t, :].bitcast(FP8X4), lhsT_scale=v2_sc[:, t, g, :],
                                     rhs=h_q[h][:].bitcast(FP8X4), rhs_scale=h_sc[h][:], start=True, stop=True)
-                kern = kern_buffer(F32)
+                if n and t == PACK - 1:
+                    kern = placed(turns, "kern%d" % n, [P, HALF], F32, n % TURNS * Y_BYTES)
+                else:
+                    kern = kern_buffer(F32)
                 nc.scalar.activation(out=kern[:], in_=s_bank[:], func=ACT.Exp, scale=0.5,
                                      bias=ln_tgt[:, PACK * g + t:PACK * g + t + 1])
-                nc.vector.tensor_tensor(out=y[:, t, :], in0=kern[:], in1=src[h][:].rearrange("p c n -> p (c n)"),
-                                        op=ALU.mult)
+                if t == 0:
+                    nc.gpsimd.tensor_tensor(out=y[:, t, :], in0=kern[:], in1=src_sbuf[:, h, :], op=ALU.mult)
+                else:
+                    nc.vector.tensor_tensor(out=y[:, t, :], in0=kern[:], in1=src[h][:].rearrange("p c n -> p (c n)"),
+                                            op=ALU.mult)
                 nc.sync.dma_start(out=rows_out[:, t, :], in_=y[:, t, :])
             return y
 
         def planes(n, y, parts):
             h, g = UNITS[n]
             cut = HALF // 2
-            low = ring.tile([P, cut, PACK], BF16, name="y_bf_low", bufs=3, align_bytes=64)
-            high = ring.tile([P, cut, PACK], BF16, name="y_bf_high", bufs=1, align_bytes=64)
+            turn = (n + 1) % TURNS * Y_BYTES
+            low = placed(turns, "y_bf_low%d" % n, [P, cut, PACK], BF16, turn + Y_BYTES // 2)
+            high = placed(turns, "y_bf_high%d" % n, [P, cut, PACK], BF16, turn)
             nc.scalar.copy(out=low[:].rearrange("p (c i) t -> p c t i", i=2),
                            in_=y[:, :, 0:cut].rearrange("p t (c i) -> p c t i", i=2))
-            if n < len(UNITS) - 1:
-                nc.gpsimd.tensor_scalar(out=high[:], in0=y[:, :, cut:HALF].rearrange("p t i -> p i t"),
-                                        scalar1=1.0, scalar2=0.0, op0=ALU.mult, op1=ALU.add)
-            else:
-                nc.vector.tensor_copy(out=high[:].rearrange("p (c i) t -> p c t i", i=2),
-                                      in_=y[:, :, cut:HALF].rearrange("p t (c i) -> p c t i", i=2))
+            nc.vector.tensor_copy(out=high[:].rearrange("p (c i) t -> p c t i", i=2),
+                                  in_=y[:, :, cut:HALF].rearrange("p t (c i) -> p c t i", i=2))
             y_q = ring.tile([P, HALF], U32, name="y_q", bufs=3, align_bytes=64)
             words_out = out_1[g].rearrange("p m t -> p (m t)").bitcast(I32)[:, h * HALF:(h + 1) * HALF]
             for part in parts:
@@ -293,11 +306,11 @@ def tile_list_transport_plan_lookup_kernel(tc, tab_words, tab_scales, tab2_words
 
         whole = [slice(0, HALF // 2), slice(HALF // 2, HALF)]
         gather_targets(1, kept("tgt_words1", [P, PASS], U32))
+        gather_targets(2, kept("tgt_words2", [P, PASS], U32))
         y_prev = plan(0)
         second_half_chunk(0)
         second_half_chunk(1)
         y_now = plan(1)
-        gather_targets(2, kept("tgt_words2", [P, PASS], U32))
         planes(0, y_prev, whole)
         second_half_chunk(2)
         second_half_chunk(3)

@@ -36,7 +36,7 @@ TGT_SC_STEP = P // BLOCKS
 SRC_ROW0 = P - S // P
 WEAVE_FIRST, WEAVE_STEP = 416, 32
 WG_CUT = 48
-PLAN_BANKS = (1, 6, 7)
+PLAN_BANKS = (2, 4, 6)
 KERN_BUFS = 2 * PACK
 Y_BYTES = PACK * HALF * 4
 TURNS = 4
@@ -179,9 +179,12 @@ def tile_list_transport_plan_lookup_kernel(tc, tab_words, tab_scales, tab2_words
         h_q = [kept("h_q%d" % h, [P, HALF], U32) for h in range(HALVES)]
         h_sc = [kept("h_sc%d" % h, [P, HALF], U8) for h in range(HALVES)]
 
-        def gate(p_bank, g_bank, h, c):
-            tanh = ring.tile([P, CHUNK, PACK], F32, name="tanh", bufs=3)
+        def squash(g_bank):
+            tanh = ring.tile([P, CHUNK, PACK], F32, name="tanh", bufs=6)
             nc.scalar.activation(out=tanh[:], in_=g_bank[:].rearrange("p t n -> p n t"), func=ACT.Tanh, scale=0.5)
+            return tanh
+
+        def gate(p_bank, tanh, h, c):
             nc.vector.scalar_tensor_tensor(out=h_bf[h][:, c * CHUNK:(c + 1) * CHUNK, :], in0=tanh[:], scalar=1.0,
                                            in1=p_bank[:].rearrange("p t n -> p n t"), op0=ALU.add, op1=ALU.mult)
 
@@ -209,27 +212,36 @@ def tile_list_transport_plan_lookup_kernel(tc, tab_words, tab_scales, tab2_words
 
         y_sc = [kept("y_sc%d" % h, [P, GROUPS, HALF], U8) for h in range(HALVES)]
 
-        def plan(n):
+        turn = [turns.tile([P, PACK * HALF], F32, name="turn%d" % r, align_bytes=64) for r in range(TURNS)]
+
+        def exponentials(n):
             h, g = UNITS[n]
-            rows_out = out_0[g * PASS:(g + 1) * PASS, h * HALF:(h + 1) * HALF].rearrange("(p t) i -> p t i", t=PACK)
-            if n < 2:
-                y = placed(tab1_place, "y%d" % n, [P, PACK, HALF], F32, tab2_offset + n * Y_BYTES)
-            else:
-                y = placed(turns, "y%d" % n, [P, PACK, HALF], F32, (n - 1) % TURNS * Y_BYTES)
+            kerns = []
             for t in range(PACK):
                 s_bank = bank(PLAN_BANKS[(PACK * n + t) % len(PLAN_BANKS)], [P, HALF])
                 nc.tensor.matmul_mx(out=s_bank[:], lhsT=v2[g][:, t, :].bitcast(FP8X4), lhsT_scale=v2_sc[:, t, g, :],
                                     rhs=h_q[h][:].bitcast(FP8X4), rhs_scale=h_sc[h][:], start=True, stop=True)
                 if n and t == PACK - 1:
-                    kern = placed(turns, "kern%d" % n, [P, HALF], F32, n % TURNS * Y_BYTES)
+                    kern = turn[n % TURNS][:, 0:HALF]
                 else:
-                    kern = kern_buffer(F32)
-                nc.scalar.activation(out=kern[:], in_=s_bank[:], func=ACT.Exp, scale=0.5,
+                    kern = kern_buffer(F32)[:]
+                nc.scalar.activation(out=kern, in_=s_bank[:], func=ACT.Exp, scale=0.5,
                                      bias=ln_tgt[:, PACK * g + t:PACK * g + t + 1])
-                if t == 0:
-                    nc.gpsimd.tensor_tensor(out=y[:, t, :], in0=kern[:], in1=src_sbuf[:, h, :], op=ALU.mult)
+                kerns.append(kern)
+            return kerns
+
+        def scale_and_store(n, kerns):
+            h, g = UNITS[n]
+            rows_out = out_0[g * PASS:(g + 1) * PASS, h * HALF:(h + 1) * HALF].rearrange("(p t) i -> p t i", t=PACK)
+            if n < 2:
+                y = placed(tab1_place, "y%d" % n, [P, PACK, HALF], F32, tab2_offset + n * Y_BYTES)[:]
+            else:
+                y = turn[(n - 1) % TURNS][:].rearrange("p (t i) -> p t i", t=PACK)
+            for t, kern in enumerate(kerns):
+                if t == 0 or (n, t) == (1, 1):
+                    nc.gpsimd.tensor_tensor(out=y[:, t, :], in0=kern, in1=src_sbuf[:, h, :], op=ALU.mult)
                 else:
-                    nc.vector.tensor_tensor(out=y[:, t, :], in0=kern[:], in1=src[h][:].rearrange("p c n -> p (c n)"),
+                    nc.vector.tensor_tensor(out=y[:, t, :], in0=kern, in1=src[h][:].rearrange("p c n -> p (c n)"),
                                             op=ALU.mult)
                 nc.sync.dma_start(out=rows_out[:, t, :], in_=y[:, t, :])
             return y
@@ -237,19 +249,18 @@ def tile_list_transport_plan_lookup_kernel(tc, tab_words, tab_scales, tab2_words
         def planes(n, y, parts):
             h, g = UNITS[n]
             cut = HALF // 2
-            turn = (n + 1) % TURNS * Y_BYTES
-            low = placed(turns, "y_bf_low%d" % n, [P, cut, PACK], BF16, turn + Y_BYTES // 2)
-            high = placed(turns, "y_bf_high%d" % n, [P, cut, PACK], BF16, turn)
-            nc.scalar.copy(out=low[:].rearrange("p (c i) t -> p c t i", i=2),
+            low = ring.tile([P, cut, PACK], BF16, name="y_bf_low", bufs=3, align_bytes=64)[:]
+            high = turn[(n + 1) % TURNS][:, 0:HALF].bitcast(BF16).rearrange("p (i t) -> p i t", t=PACK)
+            nc.scalar.copy(out=low.rearrange("p (c i) t -> p c t i", i=2),
                            in_=y[:, :, 0:cut].rearrange("p t (c i) -> p c t i", i=2))
-            nc.vector.tensor_copy(out=high[:].rearrange("p (c i) t -> p c t i", i=2),
+            nc.vector.tensor_copy(out=high.rearrange("p (c i) t -> p c t i", i=2),
                                   in_=y[:, :, cut:HALF].rearrange("p t (c i) -> p c t i", i=2))
             y_q = ring.tile([P, HALF], U32, name="y_q", bufs=3, align_bytes=64)
             words_out = out_1[g].rearrange("p m t -> p (m t)").bitcast(I32)[:, h * HALF:(h + 1) * HALF]
             for part in parts:
                 y_bf = low if part.start == 0 else high
                 nc.vector.quantize_mx(out=y_q[:, part].bitcast(FP8X4), scales=y_sc[h][:, g, part],
-                                      in_=y_bf[:].rearrange("p i t -> p (i t)"))
+                                      in_=y_bf.rearrange("p i t -> p (i t)"))
                 if n == len(UNITS) - 1:
                     nc.sync.dma_start(out=words_out[:, part], in_=y_q[:, part].bitcast(I32))
             if n < len(UNITS) - 1:
@@ -291,35 +302,49 @@ def tile_list_transport_plan_lookup_kernel(tc, tab_words, tab_scales, tab2_words
         gather_sources(last, 1, HALVES, "wg_bf")
         for c in range(CHUNKS):
             project_g(banks[c][1], last, 0, c)
-            gate(banks[c][0], banks[c][1], 0, c)
-        src = [spread_src(0, 0)]
+            gate(banks[c][0], squash(banks[c][1]), 0, c)
         gather_targets(0, kept("tgt_words0", [P, PASS], U32))
         quantise_h(0)
 
-        def second_half_chunk(c):
-            p_bank, g_bank = bank(2 + 2 * (c % 2), [P, PACK, CHUNK]), bank(3 + 2 * (c % 2), [P, PACK, CHUNK])
+        tanh_second = []
+
+        def second_half_g(c):
+            g_bank = bank(2 * c + 1, [P, PACK, CHUNK])
             for a in range(PASSES):
                 project_g(g_bank, a, 1, c)
+            tanh_second.append(squash(g_bank))
+
+        def second_half_p(c):
+            p_bank = bank(2 * c + 1, [P, PACK, CHUNK])
             for a in range(PASSES):
                 project_p(p_bank, a, 1, c)
-            gate(p_bank, g_bank, 1, c)
+            gate(p_bank, tanh_second[c], 1, c)
 
         whole = [slice(0, HALF // 2), slice(HALF // 2, HALF)]
-        gather_targets(1, kept("tgt_words1", [P, PASS], U32))
-        gather_targets(2, kept("tgt_words2", [P, PASS], U32))
-        y_prev = plan(0)
-        second_half_chunk(0)
-        second_half_chunk(1)
-        y_now = plan(1)
+        for g in range(1, GROUPS):
+            gather_targets(g, kept("tgt_words%d" % g, [P, PASS], U32))
+        for c in range(CHUNKS - 1):
+            second_half_g(c)
+        kerns = exponentials(0)
+        src = [spread_src(0, 0)]
+        y_prev = scale_and_store(0, kerns)
+        second_half_g(CHUNKS - 1)
+        kerns = exponentials(1)
+        second_half_p(0)
+        second_half_p(1)
+        y_now = scale_and_store(1, kerns)
         planes(0, y_prev, whole)
-        second_half_chunk(2)
-        second_half_chunk(3)
+        kerns = exponentials(2)
+        second_half_p(2)
+        second_half_p(3)
         quantise_h(1)
-        src.append(spread_src(1, 2))
+        src.append(spread_src(1, 1))
         for n in range(2, len(UNITS)):
-            y_prev, y_now = y_now, plan(n)
+            y_prev, y_now = y_now, scale_and_store(n, kerns)
             planes(n - 1, y_prev, whole)
             if n == GROUPS:
                 store_scales(0, nc.sync)
+            if n + 1 < len(UNITS):
+                kerns = exponentials(n + 1)
         planes(len(UNITS) - 1, y_now, [slice(HALF // 2, HALF), slice(0, HALF // 2)])
         store_scales(1, nc.sync)

@@ -31,7 +31,9 @@ CHUNKS = HALF // CHUNK
 LIST_COLS = HALF // 16
 UNITS = [(h, g) for h in range(HALVES) for g in range(GROUPS)]
 
-SC_ROW0 = P - BLOCKS * PASSES
+SC_ROW0 = 48
+SC_ROW1 = SC_ROW0 + BLOCKS * PASSES
+TGT_SC_ROW0 = 4
 TGT_SC_STEP = P // BLOCKS
 SRC_ROW0 = P - S // P
 WEAVE_FIRST, WEAVE_STEP = 416, 32
@@ -81,8 +83,8 @@ def tile_list_transport_plan_lookup_kernel(tc, tab_words, tab_scales, tab2_words
 
         nc.sync.dma_start(src_list[:], offs)
         nc.sync.dma_start(out=w4_raw[:], in_=w4_words.bitcast(I32).rearrange("a p b -> p a b"))
-        nc.sync.dma_start(out=tab_sc[SC_ROW0:P, :], in_=tab_scales.bitcast(I32).rearrange("a q c -> q a c"))
-        nc.sync.dma_start(out=w4_sc_raw[SC_ROW0:P, :], in_=w4_scales.bitcast(I32).rearrange("a q c -> q a c"))
+        nc.sync.dma_start(out=tab_sc[SC_ROW0:SC_ROW1, :], in_=tab_scales.bitcast(I32).rearrange("a q c -> q a c"))
+        nc.scalar.dma_start(out=w4_sc_raw[SC_ROW0:SC_ROW1, :], in_=w4_scales.bitcast(I32).rearrange("a q c -> q a c"))
         wg_raw = [load_wg(kept("wg_raw0", [P, PACK, H], F32), 0)]
         nc.sync.dma_start(tgt_list[:], offs2)
         tab = [load_words(kept("tab0", [P, T], I32), tab_words[0])]
@@ -95,11 +97,12 @@ def tile_list_transport_plan_lookup_kernel(tc, tab_words, tab_scales, tab2_words
         warm = kept("warm", [P, 1], F32)
         nc.scalar.activation(out=warm[:], in_=ln_tgt[:, 0:1], func=ACT.Tanh)
 
-        nc.vector.memset(tab2_sc[:], 0)
-        nc.vector.memset(tab_sc[0:SC_ROW0, :], 0)
-        nc.vector.memset(w4_sc_raw[0:SC_ROW0, :], 0)
-        nc.scalar.dma_start(out=tab2_sc[0:P:TGT_SC_STEP, :], in_=tab2_scales.bitcast(I32)[0])
-        sc = kept("sc", [P, PASSES, S + H], U8)
+        nc.gpsimd.memset(tab2_sc[:], 0)
+        for rows in (slice(0, SC_ROW0), slice(SC_ROW1, P)):
+            nc.vector.memset(tab_sc[rows, :], 0)
+            nc.vector.memset(w4_sc_raw[rows, :], 0)
+        nc.scalar.dma_start(out=tab2_sc[TGT_SC_ROW0:P:TGT_SC_STEP, :], in_=tab2_scales.bitcast(I32)[0])
+        sc = kept("sc", [P, PASSES, HALF + H], U8)
 
         ident = kept("ident", [P, P], F32)
         make_identity(nc, ident[:])
@@ -128,16 +131,23 @@ def tile_list_transport_plan_lookup_kernel(tc, tab_words, tab_scales, tab2_words
                               in_=w4_raw[:].bitcast(U16).rearrange("p a (c m t) -> p c a t m", t=PACK, c=2))
         picked_src_sc = placed(tab1_place, "picked_src_sc", [P, S], U8, 0)
         nc.vector.tensor_copy(picked_src_sc[:], tab_sc[:].bitcast(U8).indirect(src_list[:]))
-        sc_rows = kept("tab_last", [P, S + H], U8)
-        nc.vector.tensor_copy(out=sc_rows[:, S:S + H].rearrange("p (t m) -> p t m", t=PACK),
+        sc_rows = kept("tab_last", [P, HALF + H], U8)
+        sc_rows_second = kept("sc_rows_second", [P, HALF], U8)
+        nc.vector.tensor_copy(out=sc_rows[:, HALF:HALF + H].rearrange("p (t m) -> p t m", t=PACK),
                               in_=w4_sc_raw[:].bitcast(U8).rearrange("p (m t) -> p t m", t=PACK))
         wg_raw.append(load_wg(placed(wg_place, "wg_raw1", [P, PACK, H], F32, T // 2), 1))
-        nc.vector.tensor_copy(out=sc_rows[:, 0:S].bitcast(I32), in_=picked_src_sc[:].bitcast(I32))
+        nc.vector.tensor_copy(out=sc_rows_second[:].bitcast(I32), in_=picked_src_sc[:, HALF:S].bitcast(I32))
+        nc.vector.tensor_copy(out=sc_rows[:, 0:HALF].bitcast(I32), in_=picked_src_sc[:, 0:HALF].bitcast(I32))
         rows_a_quad = PACK * PASSES
-        for quad in (0, 2, 1, 3):
-            first = SC_ROW0 + rows_a_quad * quad
-            nc.sync.dma_start(out=sc[QUAD * quad:QUAD * quad + PACK, :, :].bitcast(I32),
-                              in_=sc_rows[first:first + rows_a_quad, :].bitcast(I32))
+
+        def spread_planes(planes_out, rows):
+            for quad in (0, 2, 1, 3):
+                first = SC_ROW0 + rows_a_quad * quad
+                nc.sync.dma_start(out=planes_out[QUAD * quad:QUAD * quad + PACK, :, :].bitcast(I32),
+                                  in_=rows[first:first + rows_a_quad, :].bitcast(I32))
+
+        spread_planes(sc, sc_rows)
+        src_sc = [sc]
         tab.append(load_words(placed(tab1_place, "tab1", [P, T], I32, 0), tab_words[1]))
 
         v = {}
@@ -161,10 +171,10 @@ def tile_list_transport_plan_lookup_kernel(tc, tab_words, tab_scales, tab2_words
             nc.vector.quantize_mx(out=wg_q[a][:].bitcast(FP8X4), scales=wg_sc[a][:], in_=rounded[:])
 
         def project(out_bank, words, scales, a, h, c):
-            sc_cols = slice(h * HALF + c * CHUNK, h * HALF + (c + 1) * CHUNK)
+            sc_cols = slice(c * CHUNK, (c + 1) * CHUNK)
             for t in range(PACK):
                 nc.tensor.matmul_mx(out=out_bank[:, t, :], lhsT=words(a, t), lhsT_scale=scales(a, t),
-                                    rhs=v[a, h][:, c * CHUNK:(c + 1) * CHUNK].bitcast(FP8X4), rhs_scale=sc[:, a, sc_cols],
+                                    rhs=v[a, h][:, c * CHUNK:(c + 1) * CHUNK].bitcast(FP8X4), rhs_scale=src_sc[h][:, a, sc_cols],
                                     start=(a == 0 and t == 0), stop=(a == PASSES - 1 and t == PACK - 1))
 
         def project_g(g_bank, a, h, c):
@@ -173,7 +183,7 @@ def tile_list_transport_plan_lookup_kernel(tc, tab_words, tab_scales, tab2_words
 
         def project_p(p_bank, a, h, c):
             project(p_bank, lambda a, t: w4[:, a, 2 * t * P:2 * (t + 1) * P].bitcast(FP4X4),
-                    lambda a, t: sc[:, a, S + t * P:S + (t + 1) * P], a, h, c)
+                    lambda a, t: sc[:, a, HALF + t * P:HALF + (t + 1) * P], a, h, c)
 
         h_bf = [kept("h_bf%d" % h, [P, HALF, PACK], BF16) for h in range(HALVES)]
         h_q = [kept("h_q%d" % h, [P, HALF], U32) for h in range(HALVES)]
@@ -286,11 +296,13 @@ def tile_list_transport_plan_lookup_kernel(tc, tab_words, tab_scales, tab2_words
         quantise_wg(1, P)
         gather_sources(1, 0, HALVES, "v1")
         wg_raw.append(load_wg(placed(wg_place, "wg_raw2", [P, PACK, H], F32, T // 2), last))
-        tab2_offset = 2048
+        tab2_offset = 4096
         tab2 = load_words(placed(tab1_place, "tab2", [P, T2], I32, tab2_offset), tab2_words[0])
+        src_sc.append(placed(tab1_place, "sc_second", [P, PASSES, HALF], U8, 2048))
+        spread_planes(src_sc[1], sc_rows_second)
         v2_sc = placed(tab1_place, "v2_sc", [P, PACK, GROUPS, P], U8, 0)
         for r in range(PACK):
-            nc.sync.dma_start(out=v2_sc[r:P:QUAD].bitcast(I32), in_=dealt_sc[TGT_SC_STEP * r:P:QUAD].bitcast(I32))
+            nc.sync.dma_start(out=v2_sc[r:P:QUAD].bitcast(I32), in_=dealt_sc[TGT_SC_ROW0 + TGT_SC_STEP * r:P:QUAD].bitcast(I32))
         for c in range(CHUNKS):
             project_p(banks[c][0], 1, 0, c)
             project_g(banks[c][1], 1, 0, c)

@@ -39,7 +39,9 @@ SRC_ROW0 = P - S // P
 WEAVE_FIRST, WEAVE_STEP = 416, 32
 WG_CUT = 48
 PLAN_BANKS = (2, 4, 6)
-KERN_BUFS = 2 * PACK
+KERN_BUFS = 3
+SCALAR_COLS = (256, 256, 256, 256, 256, 256)
+GPSIMD_COLS = (512, 1024, 1024, 640, 640, 640)
 Y_BYTES = PACK * HALF * 4
 TURNS = 4
 
@@ -122,9 +124,11 @@ def tile_list_transport_plan_lookup_kernel(tc, tab_words, tab_scales, tab2_words
                 nc.tensor.transpose(spread[:, c, :], src_cols[:, col:col + 1].to_broadcast([P, P]), ident[:])
             return spread
 
-        src_sbuf = kept("src_sbuf", [P, HALVES, HALF], F32)
+        src_sbuf = kept("src_sbuf", [P, HALVES, 2, HALF], F32)
         for h in range(HALVES):
-            nc.scalar.copy(out=src_sbuf[:, h, :], in_=spread_src(h, 5 + h)[:].rearrange("p c n -> p (c n)"))
+            spread = spread_src(h, 5 + h)
+            for twice in range(2):
+                nc.scalar.copy(out=src_sbuf[:, h, twice, :], in_=spread[:].rearrange("p c n -> p (c n)"))
 
         w4 = kept("w4", [P, PASSES, 2 * H], U8)
         nc.vector.tensor_copy(out=w4[:].bitcast(U16).rearrange("p a (t c m) -> p c a t m", t=PACK, c=2),
@@ -185,7 +189,9 @@ def tile_list_transport_plan_lookup_kernel(tc, tab_words, tab_scales, tab2_words
             project(p_bank, lambda a, t: w4[:, a, 2 * t * P:2 * (t + 1) * P].bitcast(FP4X4),
                     lambda a, t: sc[:, a, HALF + t * P:HALF + (t + 1) * P], a, h, c)
 
-        h_bf = [kept("h_bf%d" % h, [P, HALF, PACK], BF16) for h in range(HALVES)]
+        turn = [turns.tile([P, PACK * HALF], F32, name="turn%d" % r, align_bytes=64) for r in range(TURNS)]
+        h_bf = [kept("h_bf0", [P, HALF, PACK], BF16)[:],
+                turn[1][:, HALF:3 * HALF].bitcast(BF16).rearrange("p (i t) -> p i t", t=PACK)]
         h_q = [kept("h_q%d" % h, [P, HALF], U32) for h in range(HALVES)]
         h_sc = [kept("h_sc%d" % h, [P, HALF], U8) for h in range(HALVES)]
 
@@ -200,7 +206,7 @@ def tile_list_transport_plan_lookup_kernel(tc, tab_words, tab_scales, tab2_words
 
         def quantise_h(h):
             nc.vector.quantize_mx(out=h_q[h][:].bitcast(FP8X4), scales=h_sc[h][:],
-                                  in_=h_bf[h][:].rearrange("p i t -> p (i t)"))
+                                  in_=h_bf[h].rearrange("p i t -> p (i t)"))
 
         v2 = []
         dealt_sc = kept("dealt_sc", [P, PACK, GROUPS, P], U8)
@@ -222,23 +228,24 @@ def tile_list_transport_plan_lookup_kernel(tc, tab_words, tab_scales, tab2_words
 
         y_sc = [kept("y_sc%d" % h, [P, GROUPS, HALF], U8) for h in range(HALVES)]
 
-        turn = [turns.tile([P, PACK * HALF], F32, name="turn%d" % r, align_bytes=64) for r in range(TURNS)]
-
         def exponentials(n):
             h, g = UNITS[n]
             kerns = []
+            pair = ring.tile([P, 2 * HALF], F32, name="kern_pair", bufs=3, align_bytes=64)
             for t in range(PACK):
                 s_bank = bank(PLAN_BANKS[(PACK * n + t) % len(PLAN_BANKS)], [P, HALF])
                 nc.tensor.matmul_mx(out=s_bank[:], lhsT=v2[g][:, t, :].bitcast(FP8X4), lhsT_scale=v2_sc[:, t, g, :],
                                     rhs=h_q[h][:].bitcast(FP8X4), rhs_scale=h_sc[h][:], start=True, stop=True)
-                if n and t == PACK - 1:
+                if t < 2:
+                    kern = pair[:, t * HALF:(t + 1) * HALF]
+                elif n and t == PACK - 1:
                     kern = turn[n % TURNS][:, 0:HALF]
                 else:
                     kern = kern_buffer(F32)[:]
                 nc.scalar.activation(out=kern, in_=s_bank[:], func=ACT.Exp, scale=0.5,
                                      bias=ln_tgt[:, PACK * g + t:PACK * g + t + 1])
                 kerns.append(kern)
-            return kerns
+            return pair, kerns
 
         def scale_and_store(n, kerns):
             h, g = UNITS[n]
@@ -247,20 +254,28 @@ def tile_list_transport_plan_lookup_kernel(tc, tab_words, tab_scales, tab2_words
                 y = placed(tab1_place, "y%d" % n, [P, PACK, HALF], F32, tab2_offset + n * Y_BYTES)[:]
             else:
                 y = turn[(n - 1) % TURNS][:].rearrange("p (t i) -> p t i", t=PACK)
+            pair, kerns = kerns
+            cols = GPSIMD_COLS[n]
+            for run in ([slice(0, HALF), slice(HALF, cols)] if n == 2 else [slice(0, cols)]):
+                nc.gpsimd.tensor_tensor(out=y.rearrange("p t i -> p (t i)")[:, run], in0=pair[:, run],
+                                        in1=src_sbuf[:, h].rearrange("p t i -> p (t i)")[:, run], op=ALU.mult)
             for t, kern in enumerate(kerns):
-                if t == 0 or (n, t) == (1, 1):
-                    nc.gpsimd.tensor_tensor(out=y[:, t, :], in0=kern, in1=src_sbuf[:, h, :], op=ALU.mult)
-                else:
-                    nc.vector.tensor_tensor(out=y[:, t, :], in0=kern, in1=src[h][:].rearrange("p c n -> p (c n)"),
-                                            op=ALU.mult)
+                rest = slice(min(max(cols - t * HALF, 0), HALF), HALF)
+                if rest.start < HALF:
+                    nc.vector.tensor_tensor(out=y[:, t, rest], in0=kern[:, rest],
+                                            in1=src[h][:].rearrange("p c n -> p (c n)")[:, rest], op=ALU.mult)
+            for t in (2, 3, 0, 1):
                 nc.sync.dma_start(out=rows_out[:, t, :], in_=y[:, t, :])
             return y
 
-        def planes(n, y, parts):
+        def planes(n, y):
             h, g = UNITS[n]
-            cut = HALF // 2
+            cut = SCALAR_COLS[n]
             low = ring.tile([P, cut, PACK], BF16, name="y_bf_low", bufs=3, align_bytes=64)[:]
-            high = turn[(n + 1) % TURNS][:, 0:HALF].bitcast(BF16).rearrange("p (i t) -> p i t", t=PACK)
+            parts = [slice(0, cut), slice(cut, HALF)]
+            if n == len(UNITS) - 1:
+                parts = parts[::-1]
+            high = turn[(n + 1) % TURNS][:, 0:2 * (HALF - cut)].bitcast(BF16).rearrange("p (i t) -> p i t", t=PACK)
             nc.scalar.copy(out=low.rearrange("p (c i) t -> p c t i", i=2),
                            in_=y[:, :, 0:cut].rearrange("p t (c i) -> p c t i", i=2))
             nc.vector.tensor_copy(out=high.rearrange("p (c i) t -> p c t i", i=2),
@@ -297,9 +312,12 @@ def tile_list_transport_plan_lookup_kernel(tc, tab_words, tab_scales, tab2_words
         gather_sources(1, 0, HALVES, "v1")
         wg_raw.append(load_wg(placed(wg_place, "wg_raw2", [P, PACK, H], F32, T // 2), last))
         tab2_offset = 4096
-        tab2 = load_words(placed(tab1_place, "tab2", [P, T2], I32, tab2_offset), tab2_words[0])
+        tab2 = placed(tab1_place, "tab2", [P, T2], I32, tab2_offset)
+        tab2_in = tab2_words[0].rearrange("p t i -> p (t i)").bitcast(I32)
+        nc.sync.dma_start(out=tab2[:, 0:T2 // 2], in_=tab2_in[:, 0:T2 // 2])
         src_sc.append(placed(tab1_place, "sc_second", [P, PASSES, HALF], U8, 2048))
         spread_planes(src_sc[1], sc_rows_second)
+        nc.sync.dma_start(out=tab2[:, T2 // 2:T2], in_=tab2_in[:, T2 // 2:T2])
         v2_sc = placed(tab1_place, "v2_sc", [P, PACK, GROUPS, P], U8, 0)
         for r in range(PACK):
             nc.sync.dma_start(out=v2_sc[r:P:QUAD].bitcast(I32), in_=dealt_sc[TGT_SC_ROW0 + TGT_SC_STEP * r:P:QUAD].bitcast(I32))
@@ -332,7 +350,6 @@ def tile_list_transport_plan_lookup_kernel(tc, tab_words, tab_scales, tab2_words
                 project_p(p_bank, a, 1, c)
             gate(p_bank, tanh_second[c], 1, c)
 
-        whole = [slice(0, HALF // 2), slice(HALF // 2, HALF)]
         for g in range(1, GROUPS):
             gather_targets(g, kept("tgt_words%d" % g, [P, PASS], U32))
         for c in range(CHUNKS - 1):
@@ -345,7 +362,7 @@ def tile_list_transport_plan_lookup_kernel(tc, tab_words, tab_scales, tab2_words
         second_half_p(0)
         second_half_p(1)
         y_now = scale_and_store(1, kerns)
-        planes(0, y_prev, whole)
+        planes(0, y_prev)
         kerns = exponentials(2)
         second_half_p(2)
         second_half_p(3)
@@ -353,10 +370,10 @@ def tile_list_transport_plan_lookup_kernel(tc, tab_words, tab_scales, tab2_words
         src.append(spread_src(1, 1))
         for n in range(2, len(UNITS)):
             y_prev, y_now = y_now, scale_and_store(n, kerns)
-            planes(n - 1, y_prev, whole)
+            planes(n - 1, y_prev)
             if n == GROUPS:
                 store_scales(0, nc.sync)
             if n + 1 < len(UNITS):
                 kerns = exponentials(n + 1)
-        planes(len(UNITS) - 1, y_now, [slice(HALF // 2, HALF), slice(0, HALF // 2)])
+        planes(len(UNITS) - 1, y_now)
         store_scales(1, nc.sync)

@@ -56,6 +56,7 @@ def tile_list_transport_plan_lookup_kernel(tc, tab_words, tab_scales, tab2_words
         ring = ctx.enter_context(tc.tile_pool(name="ring", bufs=2))
         tab1_place = ctx.enter_context(tc.tile_pool(name="tab1_place", bufs=1))
         wg_place = ctx.enter_context(tc.tile_pool(name="wg_place", bufs=1))
+        late_place = ctx.enter_context(tc.tile_pool(name="late_place", bufs=1))
         turns = ctx.enter_context(tc.tile_pool(name="turns", bufs=1))
         psum = ctx.enter_context(tc.psum_pool(name="psum", bufs=1))
 
@@ -87,7 +88,7 @@ def tile_list_transport_plan_lookup_kernel(tc, tab_words, tab_scales, tab2_words
         nc.sync.dma_start(out=w4_raw[:], in_=w4_words.bitcast(I32).rearrange("a p b -> p a b"))
         nc.sync.dma_start(out=tab_sc[SC_ROW0:SC_ROW1, :], in_=tab_scales.bitcast(I32).rearrange("a q c -> q a c"))
         nc.scalar.dma_start(out=w4_sc_raw[SC_ROW0:SC_ROW1, :], in_=w4_scales.bitcast(I32).rearrange("a q c -> q a c"))
-        wg_raw = [load_wg(kept("wg_raw0", [P, PACK, H], F32), 0)]
+        wg_raw = {0: load_wg(kept("wg_raw0", [P, PACK, H], F32), 0)}
         nc.sync.dma_start(tgt_list[:], offs2)
         tab = [load_words(kept("tab0", [P, T], I32), tab_words[0])]
 
@@ -135,11 +136,11 @@ def tile_list_transport_plan_lookup_kernel(tc, tab_words, tab_scales, tab2_words
                               in_=w4_raw[:].bitcast(U16).rearrange("p a (c m t) -> p c a t m", t=PACK, c=2))
         picked_src_sc = placed(tab1_place, "picked_src_sc", [P, S], U8, 0)
         nc.vector.tensor_copy(picked_src_sc[:], tab_sc[:].bitcast(U8).indirect(src_list[:]))
-        sc_rows = kept("tab_last", [P, HALF + H], U8)
+        sc_rows = placed(late_place, "sc_rows", [P, HALF + H], U8, 2 * T - HALF)
         sc_rows_second = kept("sc_rows_second", [P, HALF], U8)
         nc.vector.tensor_copy(out=sc_rows[:, HALF:HALF + H].rearrange("p (t m) -> p t m", t=PACK),
                               in_=w4_sc_raw[:].bitcast(U8).rearrange("p (m t) -> p t m", t=PACK))
-        wg_raw.append(load_wg(placed(wg_place, "wg_raw1", [P, PACK, H], F32, T // 2), 1))
+        wg_raw[2] = load_wg(placed(wg_place, "wg_raw2", [P, PACK, H], F32, T // 2), 2)
         nc.vector.tensor_copy(out=sc_rows_second[:].bitcast(I32), in_=picked_src_sc[:, HALF:S].bitcast(I32))
         nc.vector.tensor_copy(out=sc_rows[:, 0:HALF].bitcast(I32), in_=picked_src_sc[:, 0:HALF].bitcast(I32))
         rows_a_quad = PACK * PASSES
@@ -299,7 +300,6 @@ def tile_list_transport_plan_lookup_kernel(tc, tab_words, tab_scales, tab2_words
 
         banks = [(bank(2 * c, [P, PACK, CHUNK]), bank(2 * c + 1, [P, PACK, CHUNK])) for c in range(CHUNKS)]
         last = PASSES - 1
-        tab.append(load_words(kept("tab_last", [P, T], I32), tab_words[last]))
 
         quantise_wg(0, P)
         gather_sources(0, 0, HALVES, "v0")
@@ -308,9 +308,10 @@ def tile_list_transport_plan_lookup_kernel(tc, tab_words, tab_scales, tab2_words
             project_p(banks[c][0], 0, 0, c)
             project_g(banks[c][1], 0, 0, c)
 
-        quantise_wg(1, P)
+        quantise_wg(last, P)
+        wg_raw[1] = load_wg(placed(late_place, "wg_raw1", [P, PACK, H], F32, 0), 1)
+        tab.append(load_words(placed(late_place, "tab_last", [P, T], I32, 2 * T), tab_words[last]))
         gather_sources(1, 0, HALVES, "v1")
-        wg_raw.append(load_wg(placed(wg_place, "wg_raw2", [P, PACK, H], F32, T // 2), last))
         tab2_offset = 4096
         tab2 = placed(tab1_place, "tab2", [P, T2], I32, tab2_offset)
         tab2_in = tab2_words[0].rearrange("p t i -> p (t i)").bitcast(I32)
@@ -323,15 +324,17 @@ def tile_list_transport_plan_lookup_kernel(tc, tab_words, tab_scales, tab2_words
             nc.sync.dma_start(out=v2_sc[r:P:QUAD].bitcast(I32), in_=dealt_sc[TGT_SC_ROW0 + TGT_SC_STEP * r:P:QUAD].bitcast(I32))
         for c in range(CHUNKS):
             project_p(banks[c][0], 1, 0, c)
+        quantise_wg(1, P)
+        for c in range(CHUNKS):
             project_g(banks[c][1], 1, 0, c)
 
         gather_sources(last, 0, 1, "v2_first")
+        gather_sources(last, 1, HALVES, "v2_second")
+        project_g(banks[0][1], last, 0, 0)
         for c in range(CHUNKS):
+            if c + 1 < CHUNKS:
+                project_g(banks[c + 1][1], last, 0, c + 1)
             project_p(banks[c][0], last, 0, c)
-        quantise_wg(last, WG_CUT)
-        gather_sources(last, 1, HALVES, "wg_bf")
-        for c in range(CHUNKS):
-            project_g(banks[c][1], last, 0, c)
             gate(banks[c][0], squash(banks[c][1]), 0, c)
         gather_targets(0, kept("tgt_words0", [P, PASS], U32))
         quantise_h(0)
@@ -352,12 +355,11 @@ def tile_list_transport_plan_lookup_kernel(tc, tab_words, tab_scales, tab2_words
 
         for g in range(1, GROUPS):
             gather_targets(g, kept("tgt_words%d" % g, [P, PASS], U32))
-        for c in range(CHUNKS - 1):
+        for c in range(CHUNKS):
             second_half_g(c)
         kerns = exponentials(0)
         src = [spread_src(0, 0)]
         y_prev = scale_and_store(0, kerns)
-        second_half_g(CHUNKS - 1)
         kerns = exponentials(1)
         second_half_p(0)
         second_half_p(1)

@@ -240,7 +240,8 @@ def tile_list_transport_plan_lookup_kernel(tc, tab_words, tab_scales, tab2_words
                 if t < 2:
                     kern = pair[:, t * HALF:(t + 1) * HALF]
                 elif n and t == PACK - 1:
-                    kern = turn[n % TURNS][:, 0:HALF]
+                    first = HALF if n == len(UNITS) - 1 else 0
+                    kern = turn[n % TURNS][:, first:first + HALF]
                 else:
                     kern = kern_buffer(F32)[:]
                 nc.scalar.activation(out=kern, in_=s_bank[:], func=ACT.Exp, scale=0.5,
@@ -276,7 +277,16 @@ def tile_list_transport_plan_lookup_kernel(tc, tab_words, tab_scales, tab2_words
             parts = [slice(0, cut), slice(cut, HALF)]
             if n == len(UNITS) - 1:
                 parts = parts[::-1]
-            high = turn[(n + 1) % TURNS][:, 0:2 * (HALF - cut)].bitcast(BF16).rearrange("p (i t) -> p i t", t=PACK)
+            words = 2 * (HALF - cut)
+            if n < GROUPS:
+                high = turn[(n + 1) % TURNS][:, 0:words]
+            elif n == GROUPS:
+                high = turn[1][:, HALF + 16 - words:HALF + 16]
+            elif n == GROUPS + 1:
+                high = turn[1][:, 2 * HALF - 16:2 * HALF - 16 + words]
+            else:
+                high = kept("y_bf_last", [P, words], F32)[:]
+            high = high.bitcast(BF16).rearrange("p (i t) -> p i t", t=PACK)
             nc.scalar.copy(out=low.rearrange("p (c i) t -> p c t i", i=2),
                            in_=y[:, :, 0:cut].rearrange("p t (c i) -> p c t i", i=2))
             nc.vector.tensor_copy(out=high.rearrange("p (c i) t -> p c t i", i=2),
@@ -370,12 +380,15 @@ def tile_list_transport_plan_lookup_kernel(tc, tab_words, tab_scales, tab2_words
         second_half_p(3)
         quantise_h(1)
         src.append(spread_src(1, 1))
+        ys = [y_prev, y_now]
         for n in range(2, len(UNITS)):
-            y_prev, y_now = y_now, scale_and_store(n, kerns)
-            planes(n - 1, y_prev)
+            ys.append(scale_and_store(n, kerns))
+            if n <= GROUPS:
+                planes(n - 1, ys[n - 1])
             if n == GROUPS:
                 store_scales(0, nc.sync)
             if n + 1 < len(UNITS):
                 kerns = exponentials(n + 1)
-        planes(len(UNITS) - 1, y_now)
+        for n in range(GROUPS, len(UNITS)):
+            planes(n, ys[n])
         store_scales(1, nc.sync)

@@ -97,8 +97,6 @@ def tile_list_transport_plan_lookup_kernel(tc, tab_words, tab_scales, tab2_words
                             in_=tgt_scale.rearrange("(g p t) -> p g t", p=P, t=PACK))
         ln_tgt = kept("ln_tgt", [P, GROUPS * PACK], F32)
         nc.scalar.activation(out=ln_tgt[:], in_=tgt[:], func=ACT.Ln)
-        warm = kept("warm", [P, 1], F32)
-        nc.scalar.activation(out=warm[:], in_=ln_tgt[:, 0:1], func=ACT.Tanh)
 
         nc.gpsimd.memset(tab2_sc[:], 0)
         for rows in (slice(0, SC_ROW0), slice(SC_ROW1, P)):

@@ -36,14 +36,11 @@ SC_ROW1 = SC_ROW0 + BLOCKS * PASSES
 TGT_SC_ROW0 = 4
 TGT_SC_STEP = P // BLOCKS
 SRC_ROW0 = P - S // P
-WEAVE_FIRST, WEAVE_STEP = 416, 32
-WG_CUT = 48
-PLAN_BANKS = (2, 4, 6)
-KERN_BUFS = 3
-SCALAR_COLS = (256, 256, 256, 256, 256, 256)
-GPSIMD_COLS = (512, 1024, 1024, 640, 640, 640)
+SCALAR_COLS = 224
+SCALAR_COLS_LAST = 168
+GPSIMD_SLICES = (2, 1)
+Z_BUFS = 6
 Y_BYTES = PACK * HALF * 4
-TURNS = 4
 
 
 def tile_list_transport_plan_lookup_kernel(tc, tab_words, tab_scales, tab2_words, tab2_scales, w4_words,
@@ -57,7 +54,6 @@ def tile_list_transport_plan_lookup_kernel(tc, tab_words, tab_scales, tab2_words
         tab1_place = ctx.enter_context(tc.tile_pool(name="tab1_place", bufs=1))
         wg_place = ctx.enter_context(tc.tile_pool(name="wg_place", bufs=1))
         late_place = ctx.enter_context(tc.tile_pool(name="late_place", bufs=1))
-        turns = ctx.enter_context(tc.tile_pool(name="turns", bufs=1))
         psum = ctx.enter_context(tc.psum_pool(name="psum", bufs=1))
 
         def kept(tag, shape, dtype):
@@ -116,18 +112,16 @@ def tile_list_transport_plan_lookup_kernel(tc, tab_words, tab_scales, tab2_words
         src_cols = kept("src_cols", [P, S // P], F32)
         nc.vector.tensor_copy(out=src_cols[:], in_=turned[:, SRC_ROW0:P])
 
-        def spread_src(h, b):
-            spread = bank(b, [P, CHUNKS, CHUNK])
+        ln_src = kept("ln_src", [P, HALVES, HALF], F32)
+        src_first = kept("src_first", [P, HALF], F32)
+        for h in range(HALVES):
+            spread = bank(5 + h, [P, CHUNKS, CHUNK])
             for c in range(CHUNKS):
                 col = h * CHUNKS + c
                 nc.tensor.transpose(spread[:, c, :], src_cols[:, col:col + 1].to_broadcast([P, P]), ident[:])
-            return spread
-
-        src_sbuf = kept("src_sbuf", [P, HALVES, 2, HALF], F32)
-        for h in range(HALVES):
-            spread = spread_src(h, 5 + h)
-            for twice in range(2):
-                nc.scalar.copy(out=src_sbuf[:, h, twice, :], in_=spread[:].rearrange("p c n -> p (c n)"))
+            nc.scalar.activation(out=ln_src[:, h, :], in_=spread[:].rearrange("p c n -> p (c n)"), func=ACT.Ln)
+            if h == 0:
+                nc.scalar.copy(out=src_first[:], in_=spread[:].rearrange("p c n -> p (c n)"))
 
         w4 = kept("w4", [P, PASSES, 2 * H], U8)
         nc.vector.tensor_copy(out=w4[:].bitcast(U16).rearrange("p a (t c m) -> p c a t m", t=PACK, c=2),
@@ -188,9 +182,7 @@ def tile_list_transport_plan_lookup_kernel(tc, tab_words, tab_scales, tab2_words
             project(p_bank, lambda a, t: w4[:, a, 2 * t * P:2 * (t + 1) * P].bitcast(FP4X4),
                     lambda a, t: sc[:, a, HALF + t * P:HALF + (t + 1) * P], a, h, c)
 
-        turn = [turns.tile([P, PACK * HALF], F32, name="turn%d" % r, align_bytes=64) for r in range(TURNS)]
-        h_bf = [kept("h_bf0", [P, HALF, PACK], BF16)[:],
-                turn[1][:, HALF:3 * HALF].bitcast(BF16).rearrange("p (i t) -> p i t", t=PACK)]
+        h_bf = [kept("h_bf%d" % h, [P, HALF, PACK], BF16)[:] for h in range(HALVES)]
         h_q = [kept("h_q%d" % h, [P, HALF], U32) for h in range(HALVES)]
         h_sc = [kept("h_sc%d" % h, [P, HALF], U8) for h in range(HALVES)]
 
@@ -222,83 +214,67 @@ def tile_list_transport_plan_lookup_kernel(tc, tab_words, tab_scales, tab2_words
                                   tab2[:].bitcast(U32).indirect(tgt_list[:, g * LIST_COLS:(g + 1) * LIST_COLS]))
             v2.append(dealt)
 
-        def kern_buffer(dtype):
-            return ring.tile([P, HALF], dtype, name="kern", bufs=KERN_BUFS, align_bytes=64)
-
         y_sc = [kept("y_sc%d" % h, [P, GROUPS, HALF], U8) for h in range(HALVES)]
+        woven = kept("woven", [P, PACK * (HALF + SCALAR_COLS)], BF16)
 
-        def exponentials(n):
-            h, g = UNITS[n]
-            kerns = []
-            pair = ring.tile([P, 2 * HALF], F32, name="kern_pair", bufs=3, align_bytes=64)
-            for t in range(PACK):
-                s_bank = bank(PLAN_BANKS[(PACK * n + t) % len(PLAN_BANKS)], [P, HALF])
-                nc.tensor.matmul_mx(out=s_bank[:], lhsT=v2[g][:, t, :].bitcast(FP8X4), lhsT_scale=v2_sc[:, t, g, :],
-                                    rhs=h_q[h][:].bitcast(FP8X4), rhs_scale=h_sc[h][:], start=True, stop=True)
-                if t < 2:
-                    kern = pair[:, t * HALF:(t + 1) * HALF]
-                elif n and t == PACK - 1:
-                    first = HALF if n == len(UNITS) - 1 else 0
-                    kern = turn[n % TURNS][:, first:first + HALF]
-                else:
-                    kern = kern_buffer(F32)[:]
-                nc.scalar.activation(out=kern, in_=s_bank[:], func=ACT.Exp, scale=0.5,
-                                     bias=ln_tgt[:, PACK * g + t:PACK * g + t + 1])
-                kerns.append(kern)
-            return pair, kerns
-
-        def scale_and_store(n, kerns):
+        def plan(n):
             h, g = UNITS[n]
             rows_out = out_0[g * PASS:(g + 1) * PASS, h * HALF:(h + 1) * HALF].rearrange("(p t) i -> p t i", t=PACK)
-            if n < 2:
-                y = placed(tab1_place, "y%d" % n, [P, PACK, HALF], F32, tab2_offset + n * Y_BYTES)[:]
+            if n == 0:
+                y = placed(tab1_place, "y0", [P, PACK, HALF], F32, tab2_offset)[:]
             else:
-                y = turn[(n - 1) % TURNS][:].rearrange("p (t i) -> p t i", t=PACK)
-            pair, kerns = kerns
-            cols = GPSIMD_COLS[n]
-            for run in ([slice(0, HALF), slice(HALF, cols)] if n == 2 else [slice(0, cols)]):
-                nc.gpsimd.tensor_tensor(out=y.rearrange("p t i -> p (t i)")[:, run], in0=pair[:, run],
-                                        in1=src_sbuf[:, h].rearrange("p t i -> p (t i)")[:, run], op=ALU.mult)
-            for t, kern in enumerate(kerns):
-                rest = slice(min(max(cols - t * HALF, 0), HALF), HALF)
-                if rest.start < HALF:
-                    nc.vector.tensor_tensor(out=y[:, t, rest], in0=kern[:, rest],
-                                            in1=src[h][:].rearrange("p c n -> p (c n)")[:, rest], op=ALU.mult)
-            for t in (2, 3, 0, 1):
+                y = kept("y%d" % n, [P, PACK, HALF], F32)[:]
+            direct = GPSIMD_SLICES[n] if n < len(GPSIMD_SLICES) else 0
+            if direct:
+                kern = kept("kern%d" % n, [P, direct, HALF], F32)
+            for t in range(PACK):
+                s_bank = bank(plan_bank(n, t), [P, HALF])
+                nc.tensor.matmul_mx(out=s_bank[:], lhsT=v2[g][:, t, :].bitcast(FP8X4), lhsT_scale=v2_sc[:, t, g, :],
+                                    rhs=h_q[h][:].bitcast(FP8X4), rhs_scale=h_sc[h][:], start=True, stop=True)
+                bias = ln_tgt[:, PACK * g + t:PACK * g + t + 1]
+                if t < direct:
+                    nc.scalar.activation(out=kern[:, t, :], in_=s_bank[:], func=ACT.Exp, scale=0.5, bias=bias)
+                    continue
+                z = ring.tile([P, HALF], F32, name="z", bufs=Z_BUFS, align_bytes=64)
+                nc.vector.scalar_tensor_tensor(out=z[:], in0=s_bank[:], scalar=0.5, in1=ln_src[:, h, :],
+                                               op0=ALU.mult, op1=ALU.add)
+                nc.scalar.activation(out=y[:, t, :], in_=z[:], func=ACT.Exp, bias=bias)
+            if direct:
+                nc.gpsimd.tensor_tensor(out=y[:, 0:direct, :], in0=kern[:],
+                                        in1=src_first[:].unsqueeze(1).to_broadcast([P, direct, HALF]), op=ALU.mult)
+            for t in list(range(direct, PACK)) + list(range(direct)):
                 nc.sync.dma_start(out=rows_out[:, t, :], in_=y[:, t, :])
             return y
 
-        def planes(n, y):
-            h, g = UNITS[n]
-            cut = SCALAR_COLS[n]
-            low = ring.tile([P, cut, PACK], BF16, name="y_bf_low", bufs=3, align_bytes=64)[:]
-            parts = [slice(0, cut), slice(cut, HALF)]
-            if n == len(UNITS) - 1:
-                parts = parts[::-1]
-            words = 2 * (HALF - cut)
-            if n < GROUPS:
-                high = turn[(n + 1) % TURNS][:, 0:words]
-            elif n == GROUPS:
-                high = turn[1][:, HALF + 16 - words:HALF + 16]
-            elif n == GROUPS + 1:
-                high = turn[1][:, 2 * HALF - 16:2 * HALF - 16 + words]
+        def plan_bank(n, t):
+            if n < 2:
+                return 2 * t + 1
+            return ((0, 2, 1, 3), (5, 7, 4, 6))[n % 2][t]
+
+        def woven_unit(n):
+            first = PACK * SCALAR_COLS * (n % 2)
+            return woven[:, first:first + PACK * HALF]
+
+        def weave(n, y):
+            final = n == len(UNITS) - 1
+            cols = SCALAR_COLS_LAST if final else SCALAR_COLS
+            outer, middle = (slice(HALF - cols, HALF), slice(0, HALF - cols)) if n % 2 else (slice(0, cols), slice(cols, HALF))
+            y_bf = woven_unit(n).rearrange("p (i t) -> p i t", t=PACK)
+            nc.scalar.copy(out=y_bf[:, outer, :].rearrange("p (c i) t -> p c t i", i=2),
+                           in_=y[:, :, outer].rearrange("p t (c i) -> p c t i", i=2))
+            if final:
+                nc.vector.tensor_copy(out=y_bf[:, middle, :].rearrange("p (c i) t -> p c t i", i=2),
+                                      in_=y[:, :, middle].rearrange("p t (c i) -> p c t i", i=2))
             else:
-                high = kept("y_bf_last", [P, words], F32)[:]
-            high = high.bitcast(BF16).rearrange("p (i t) -> p i t", t=PACK)
-            nc.scalar.copy(out=low.rearrange("p (c i) t -> p c t i", i=2),
-                           in_=y[:, :, 0:cut].rearrange("p t (c i) -> p c t i", i=2))
-            nc.vector.tensor_copy(out=high.rearrange("p (c i) t -> p c t i", i=2),
-                                  in_=y[:, :, cut:HALF].rearrange("p t (c i) -> p c t i", i=2))
-            y_q = ring.tile([P, HALF], U32, name="y_q", bufs=3, align_bytes=64)
+                nc.gpsimd.tensor_scalar(out=y_bf[:, middle, :], in0=y[:, :, middle].rearrange("p t i -> p i t"),
+                                        scalar1=1.0, scalar2=0.0, op0=ALU.mult, op1=ALU.add)
+
+        def quantise_y(n):
+            h, g = UNITS[n]
+            y_q = kept("y_q%d" % n, [P, HALF], U32)
+            nc.vector.quantize_mx(out=y_q[:].bitcast(FP8X4), scales=y_sc[h][:, g, :], in_=woven_unit(n))
             words_out = out_1[g].rearrange("p m t -> p (m t)").bitcast(I32)[:, h * HALF:(h + 1) * HALF]
-            for part in parts:
-                y_bf = low if part.start == 0 else high
-                nc.vector.quantize_mx(out=y_q[:, part].bitcast(FP8X4), scales=y_sc[h][:, g, part],
-                                      in_=y_bf.rearrange("p i t -> p (i t)"))
-                if n == len(UNITS) - 1:
-                    nc.sync.dma_start(out=words_out[:, part], in_=y_q[:, part].bitcast(I32))
-            if n < len(UNITS) - 1:
-                nc.sync.dma_start(out=words_out, in_=y_q[:].bitcast(I32))
+            nc.sync.dma_start(out=words_out, in_=y_q[:].bitcast(I32))
 
         def store_scales(h, queue):
             word_cols = slice(h * HALF // 4, (h + 1) * HALF // 4)
@@ -356,7 +332,7 @@ def tile_list_transport_plan_lookup_kernel(tc, tab_words, tab_scales, tab2_words
             tanh_second.append(squash(g_bank))
 
         def second_half_p(c):
-            p_bank = bank(2 * c + 1, [P, PACK, CHUNK])
+            p_bank = bank(2 * c, [P, PACK, CHUNK])
             for a in range(PASSES):
                 project_p(p_bank, a, 1, c)
             gate(p_bank, tanh_second[c], 1, c)
@@ -365,28 +341,21 @@ def tile_list_transport_plan_lookup_kernel(tc, tab_words, tab_scales, tab2_words
             gather_targets(g, kept("tgt_words%d" % g, [P, PASS], U32))
         for c in range(CHUNKS):
             second_half_g(c)
-        kerns = exponentials(0)
-        src = [spread_src(0, 0)]
-        y_prev = scale_and_store(0, kerns)
-        kerns = exponentials(1)
+        ys = [plan(0)]
         second_half_p(0)
         second_half_p(1)
-        y_now = scale_and_store(1, kerns)
-        planes(0, y_prev)
-        kerns = exponentials(2)
+        ys.append(plan(1))
+        weave(0, ys[0])
         second_half_p(2)
         second_half_p(3)
+        quantise_y(0)
         quantise_h(1)
-        src.append(spread_src(1, 1))
-        ys = [y_prev, y_now]
         for n in range(2, len(UNITS)):
-            ys.append(scale_and_store(n, kerns))
-            if n <= GROUPS:
-                planes(n - 1, ys[n - 1])
+            weave(n - 1, ys[n - 1])
+            ys.append(plan(n))
+            quantise_y(n - 1)
             if n == GROUPS:
                 store_scales(0, nc.sync)
-            if n + 1 < len(UNITS):
-                kerns = exponentials(n + 1)
-        for n in range(GROUPS, len(UNITS)):
-            planes(n, ys[n])
+        weave(len(UNITS) - 1, ys[-1])
+        quantise_y(len(UNITS) - 1)
         store_scales(1, nc.sync)

@@ -36,8 +36,8 @@ SC_ROW1 = SC_ROW0 + BLOCKS * PASSES
 TGT_SC_ROW0 = 4
 TGT_SC_STEP = P // BLOCKS
 SRC_ROW0 = P - S // P
-SCALAR_COLS = 224
-SCALAR_COLS_LAST = 168
+SCALAR_COLS = (352, 256, 160, 160, 160, 168)
+WOVEN_SHIFT = PACK * max(SCALAR_COLS[1:])
 GPSIMD_SLICES = (2, 1)
 Z_BUFS = 6
 Y_BYTES = PACK * HALF * 4
@@ -215,7 +215,7 @@ def tile_list_transport_plan_lookup_kernel(tc, tab_words, tab_scales, tab2_words
             v2.append(dealt)
 
         y_sc = [kept("y_sc%d" % h, [P, GROUPS, HALF], U8) for h in range(HALVES)]
-        woven = kept("woven", [P, PACK * (HALF + SCALAR_COLS)], BF16)
+        woven = kept("woven", [P, PACK * HALF + WOVEN_SHIFT], BF16)
 
         def plan(n):
             h, g = UNITS[n]
@@ -252,12 +252,12 @@ def tile_list_transport_plan_lookup_kernel(tc, tab_words, tab_scales, tab2_words
             return ((0, 2, 1, 3), (5, 7, 4, 6))[n % 2][t]
 
         def woven_unit(n):
-            first = PACK * SCALAR_COLS * (n % 2)
+            first = WOVEN_SHIFT * (n % 2)
             return woven[:, first:first + PACK * HALF]
 
         def weave(n, y):
             final = n == len(UNITS) - 1
-            cols = SCALAR_COLS_LAST if final else SCALAR_COLS
+            cols = SCALAR_COLS[n]
             outer, middle = (slice(HALF - cols, HALF), slice(0, HALF - cols)) if n % 2 else (slice(0, cols), slice(cols, HALF))
             y_bf = woven_unit(n).rearrange("p (i t) -> p i t", t=PACK)
             nc.scalar.copy(out=y_bf[:, outer, :].rearrange("p (c i) t -> p c t i", i=2),

@@ -272,9 +272,12 @@ def tile_list_transport_plan_lookup_kernel(tc, tab_words, tab_scales, tab2_words
         def quantise_y(n):
             h, g = UNITS[n]
             y_q = kept("y_q%d" % n, [P, HALF], U32)
-            nc.vector.quantize_mx(out=y_q[:].bitcast(FP8X4), scales=y_sc[h][:, g, :], in_=woven_unit(n))
             words_out = out_1[g].rearrange("p m t -> p (m t)").bitcast(I32)[:, h * HALF:(h + 1) * HALF]
-            nc.sync.dma_start(out=words_out, in_=y_q[:].bitcast(I32))
+            parts = [slice(0, HALF // 2), slice(HALF // 2, HALF)] if n == len(UNITS) - 1 else [slice(0, HALF)]
+            for cols in parts:
+                nc.vector.quantize_mx(out=y_q[:, cols].bitcast(FP8X4), scales=y_sc[h][:, g, cols],
+                                      in_=woven_unit(n)[:, PACK * cols.start:PACK * cols.stop])
+                nc.sync.dma_start(out=words_out[:, cols], in_=y_q[:, cols].bitcast(I32))
 
         def store_scales(h, queue):
             word_cols = slice(h * HALF // 4, (h + 1) * HALF // 4)
@@ -312,7 +315,11 @@ def tile_list_transport_plan_lookup_kernel(tc, tab_words, tab_scales, tab2_words
         for c in range(CHUNKS):
             project_g(banks[c][1], 1, 0, c)
 
-        gather_sources(last, 0, 1, "v2_first")
+        picked = kept("v2_first", [P, HALF], U32)
+        for piece in range(2):
+            nc.vector.tensor_copy(picked[:, piece * HALF // 2:(piece + 1) * HALF // 2],
+                                  tab[last][:].bitcast(U32).indirect(src_list[:, piece * LIST_COLS // 2:(piece + 1) * LIST_COLS // 2]))
+        v[last, 0] = picked[:]
         gather_sources(last, 1, HALVES, "v2_second")
         project_g(banks[0][1], last, 0, 0)
         for c in range(CHUNKS):

@@ -36,7 +36,7 @@ SC_ROW1 = SC_ROW0 + BLOCKS * PASSES
 TGT_SC_ROW0 = 4
 TGT_SC_STEP = P // BLOCKS
 SRC_ROW0 = P - S // P
-SCALAR_COLS = (352, 256, 160, 160, 160, 168)
+SCALAR_COLS = (352, 256, 144, 144, 144, 168)
 WOVEN_SHIFT = PACK * max(SCALAR_COLS[1:])
 GPSIMD_SLICES = (2, 1)
 Z_BUFS = 6
@@ -263,8 +263,9 @@ def tile_list_transport_plan_lookup_kernel(tc, tab_words, tab_scales, tab2_words
             nc.scalar.copy(out=y_bf[:, outer, :].rearrange("p (c i) t -> p c t i", i=2),
                            in_=y[:, :, outer].rearrange("p t (c i) -> p c t i", i=2))
             if final:
-                nc.vector.tensor_copy(out=y_bf[:, middle, :].rearrange("p (c i) t -> p c t i", i=2),
-                                      in_=y[:, :, middle].rearrange("p t (c i) -> p c t i", i=2))
+                for run in (slice(0, HALF // 2), slice(HALF // 2, middle.stop)):
+                    nc.vector.tensor_copy(out=y_bf[:, run, :].rearrange("p (c i) t -> p c t i", i=2),
+                                          in_=y[:, :, run].rearrange("p t (c i) -> p c t i", i=2))
             else:
                 nc.gpsimd.tensor_scalar(out=y_bf[:, middle, :], in0=y[:, :, middle].rearrange("p t i -> p i t"),
                                         scalar1=1.0, scalar2=0.0, op0=ALU.mult, op1=ALU.add)
@@ -344,8 +345,10 @@ def tile_list_transport_plan_lookup_kernel(tc, tab_words, tab_scales, tab2_words
                 project_p(p_bank, a, 1, c)
             gate(p_bank, tanh_second[c], 1, c)
 
-        for g in range(1, GROUPS):
-            gather_targets(g, kept("tgt_words%d" % g, [P, PASS], U32))
+        rest = kept("tgt_words_rest", [P, GROUPS - 1, PACK, P], U32)
+        nc.vector.tensor_copy(rest[:].rearrange("p g t m -> p g m t"),
+                              tab2[:].bitcast(U32).indirect(tgt_list[:, LIST_COLS:GROUPS * LIST_COLS]))
+        v2.extend(rest[:, g] for g in range(GROUPS - 1))
         for c in range(CHUNKS):
             second_half_g(c)
         ys = [plan(0)]

@@ -36,7 +36,7 @@ SC_ROW1 = SC_ROW0 + BLOCKS * PASSES
 TGT_SC_ROW0 = 4
 TGT_SC_STEP = P // BLOCKS
 SRC_ROW0 = P - S // P
-SCALAR_COLS = (352, 256, 144, 144, 144, 168)
+SCALAR_COLS = (352, 256, 160, 160, 160, 168)
 WOVEN_SHIFT = PACK * max(SCALAR_COLS[1:])
 GPSIMD_SLICES = (2, 1)
 Z_BUFS = 6

from contextlib import ExitStack

import concourse.mybir as mybir
from concourse.masks import make_identity

K, H, T, S, T2, S2 = 1536, 512, 4096, 1024, 4096, 1536
FLOPS = 2 * (2 * K * H * S + H * S2 * S)

F32 = mybir.dt.float32
BF16 = mybir.dt.bfloat16
I32 = mybir.dt.int32
U32 = mybir.dt.uint32
U16 = mybir.dt.uint16
U8 = mybir.dt.uint8
FP8X4 = mybir.dt.float8_e4m3fn_x4
FP4X4 = mybir.dt.float4_e2m1fn_x4
ACT = mybir.ActivationFunctionType
ALU = mybir.AluOpType

P = 128
PACK = 4
PASS = P * PACK
PASSES = K // PASS
BLOCKS = PASS // 32
QUAD = 32
GROUPS = S2 // PASS
HALF = 512
HALVES = S // HALF
CHUNK = 128
CHUNKS = HALF // CHUNK
LIST_COLS = HALF // 16
UNITS = [(h, g) for h in range(HALVES) for g in range(GROUPS)]

SC_ROW0 = 48
SC_ROW1 = SC_ROW0 + BLOCKS * PASSES
TGT_SC_ROW0 = 4
TGT_SC_STEP = P // BLOCKS
SRC_ROW0 = P - S // P
SCALAR_COLS = (352, 256, 160, 160, 160, 168)
WOVEN_SHIFT = PACK * max(SCALAR_COLS[1:])
GPSIMD_SLICES = (2, 1)
Z_BUFS = 6
Y_BYTES = PACK * HALF * 4


def tile_list_transport_plan_lookup_kernel(tc, tab_words, tab_scales, tab2_words, tab2_scales, w4_words,
                                                       w4_scales, wg, src_scale, tgt_scale, offs, offs2,
                                                       out_0, out_1, out_2):
    nc = tc.nc
    with ExitStack() as ctx:
        lists = ctx.enter_context(tc.tile_pool(name="lists", bufs=1))
        keep = ctx.enter_context(tc.tile_pool(name="keep", bufs=1))
        ring = ctx.enter_context(tc.tile_pool(name="ring", bufs=2))
        tab1_place = ctx.enter_context(tc.tile_pool(name="tab1_place", bufs=1))
        wg_place = ctx.enter_context(tc.tile_pool(name="wg_place", bufs=1))
        late_place = ctx.enter_context(tc.tile_pool(name="late_place", bufs=1))
        psum = ctx.enter_context(tc.psum_pool(name="psum", bufs=1))

        def kept(tag, shape, dtype):
            return keep.tile(shape, dtype, name=tag, align_bytes=64)

        def placed(pool, name, shape, dtype, offset):
            return pool.tile(shape, dtype, name=name, align_bytes=64, offset=offset)

        def bank(b, shape):
            return psum.tile(shape, F32, name="bank%d" % b)

        def load_words(window, words):
            nc.sync.dma_start(out=window[:], in_=words.rearrange("p t i -> p (t i)").bitcast(I32))
            return window

        def load_wg(raw, a):
            nc.sync.dma_start(out=raw[:], in_=wg[a * PASS:(a + 1) * PASS, :].rearrange("(p j) c -> p j c", j=PACK))
            return raw

        src_list = lists.tile([P, S // 16], U16, name="src_list")
        tgt_list = lists.tile([P, S2 // 16], U16, name="tgt_list")
        w4_raw = kept("w4_raw", [P, PASSES, 2 * H // 4], I32)
        tab_sc = placed(wg_place, "tab_sc", [P, T // 4], I32, 0)
        w4_sc_raw = placed(tab1_place, "w4_sc_raw", [P, H // 4], I32, S)
        tab2_sc = kept("tab2_sc", [P, T2 // 4], I32)

        nc.sync.dma_start(src_list[:], offs)
        nc.sync.dma_start(out=w4_raw[:], in_=w4_words.bitcast(I32).rearrange("a p b -> p a b"))
        nc.sync.dma_start(out=tab_sc[SC_ROW0:SC_ROW1, :], in_=tab_scales.bitcast(I32).rearrange("a q c -> q a c"))
        nc.scalar.dma_start(out=w4_sc_raw[SC_ROW0:SC_ROW1, :], in_=w4_scales.bitcast(I32).rearrange("a q c -> q a c"))
        wg_raw = {0: load_wg(kept("wg_raw0", [P, PACK, H], F32), 0)}
        nc.sync.dma_start(tgt_list[:], offs2)
        tab = [load_words(kept("tab0", [P, T], I32), tab_words[0])]

        tgt = kept("tgt", [P, GROUPS * PACK], F32)
        nc.scalar.dma_start(out=tgt[:].rearrange("p (g t) -> p g t", t=PACK),
                            in_=tgt_scale.rearrange("(g p t) -> p g t", p=P, t=PACK))
        ln_tgt = kept("ln_tgt", [P, GROUPS * PACK], F32)
        nc.scalar.activation(out=ln_tgt[:], in_=tgt[:], func=ACT.Ln)

        nc.gpsimd.memset(tab2_sc[:], 0)
        for rows in (slice(0, SC_ROW0), slice(SC_ROW1, P)):
            nc.vector.memset(tab_sc[rows, :], 0)
            nc.vector.memset(w4_sc_raw[rows, :], 0)
        nc.scalar.dma_start(out=tab2_sc[TGT_SC_ROW0:P:TGT_SC_STEP, :], in_=tab2_scales.bitcast(I32)[0])
        sc = kept("sc", [P, PASSES, HALF + H], U8)

        ident = kept("ident", [P, P], F32)
        make_identity(nc, ident[:])
        src_rows = kept("src_rows", [P, P], F32)
        nc.gpsimd.memset(src_rows[0:P - QUAD, :], 0.0)
        nc.gpsimd.memset(src_rows[P - QUAD:SRC_ROW0, :], 0.0)
        nc.scalar.dma_start(out=src_rows[SRC_ROW0:P, :], in_=src_scale.rearrange("(c p) -> c p", p=P))
        turned = bank(7, [P, P])
        nc.tensor.transpose(turned[:], src_rows[:], ident[:])
        src_cols = kept("src_cols", [P, S // P], F32)
        nc.vector.tensor_copy(out=src_cols[:], in_=turned[:, SRC_ROW0:P])

        ln_src = kept("ln_src", [P, HALVES, HALF], F32)
        src_first = kept("src_first", [P, HALF], F32)
        for h in range(HALVES):
            spread = bank(5 + h, [P, CHUNKS, CHUNK])
            for c in range(CHUNKS):
                col = h * CHUNKS + c
                nc.tensor.transpose(spread[:, c, :], src_cols[:, col:col + 1].to_broadcast([P, P]), ident[:])
            nc.scalar.activation(out=ln_src[:, h, :], in_=spread[:].rearrange("p c n -> p (c n)"), func=ACT.Ln)
            if h == 0:
                nc.scalar.copy(out=src_first[:], in_=spread[:].rearrange("p c n -> p (c n)"))

        w4 = kept("w4", [P, PASSES, 2 * H], U8)
        nc.vector.tensor_copy(out=w4[:].bitcast(U16).rearrange("p a (t c m) -> p c a t m", t=PACK, c=2),
                              in_=w4_raw[:].bitcast(U16).rearrange("p a (c m t) -> p c a t m", t=PACK, c=2))
        picked_src_sc = placed(tab1_place, "picked_src_sc", [P, S], U8, 0)
        nc.vector.tensor_copy(picked_src_sc[:], tab_sc[:].bitcast(U8).indirect(src_list[:]))
        sc_rows = placed(late_place, "sc_rows", [P, HALF + H], U8, 2 * T - HALF)
        sc_rows_second = kept("sc_rows_second", [P, HALF], U8)
        nc.vector.tensor_copy(out=sc_rows[:, HALF:HALF + H].rearrange("p (t m) -> p t m", t=PACK),
                              in_=w4_sc_raw[:].bitcast(U8).rearrange("p (m t) -> p t m", t=PACK))
        wg_raw[2] = load_wg(placed(wg_place, "wg_raw2", [P, PACK, H], F32, T // 2), 2)
        nc.vector.tensor_copy(out=sc_rows_second[:].bitcast(I32), in_=picked_src_sc[:, HALF:S].bitcast(I32))
        nc.vector.tensor_copy(out=sc_rows[:, 0:HALF].bitcast(I32), in_=picked_src_sc[:, 0:HALF].bitcast(I32))
        rows_a_quad = PACK * PASSES

        def spread_planes(planes_out, rows):
            for quad in (0, 2, 1, 3):
                first = SC_ROW0 + rows_a_quad * quad
                nc.sync.dma_start(out=planes_out[QUAD * quad:QUAD * quad + PACK, :, :].bitcast(I32),
                                  in_=rows[first:first + rows_a_quad, :].bitcast(I32))

        spread_planes(sc, sc_rows)
        src_sc = [sc]
        tab.append(load_words(placed(tab1_place, "tab1", [P, T], I32, 0), tab_words[1]))

        v = {}
        wg_q = [kept("wg_q%d" % a, [P, H], U32) for a in range(PASSES)]
        wg_sc = [kept("wg_sc%d" % a, [P, H], U8) for a in range(PASSES)]

        def gather_sources(a, h0, h1, tag):
            picked = kept(tag, [P, (h1 - h0) * HALF], U32)
            nc.vector.tensor_copy(picked[:],
                                  tab[a][:].bitcast(U32).indirect(src_list[:, h0 * LIST_COLS:h1 * LIST_COLS]))
            for h in range(h0, h1):
                v[a, h] = picked[:, (h - h0) * HALF:(h - h0 + 1) * HALF]

        def quantise_wg(a, cut):
            rounded = kept("wg_bf", [P, PACK * H], BF16)
            dst = rounded[:].rearrange("p (u t m j) -> p u m j t", u=2, t=2, j=PACK)
            raw = wg_raw[a][:].rearrange("p j (m u t) -> p u m j t", u=2, t=2)
            nc.scalar.copy(out=dst[:, :, 0:cut], in_=raw[:, :, 0:cut])
            if cut < P:
                nc.vector.tensor_copy(out=dst[:, :, cut:P], in_=raw[:, :, cut:P])
            nc.vector.quantize_mx(out=wg_q[a][:].bitcast(FP8X4), scales=wg_sc[a][:], in_=rounded[:])

        def project(out_bank, words, scales, a, h, c):
            sc_cols = slice(c * CHUNK, (c + 1) * CHUNK)
            for t in range(PACK):
                nc.tensor.matmul_mx(out=out_bank[:, t, :], lhsT=words(a, t), lhsT_scale=scales(a, t),
                                    rhs=v[a, h][:, c * CHUNK:(c + 1) * CHUNK].bitcast(FP8X4), rhs_scale=src_sc[h][:, a, sc_cols],
                                    start=(a == 0 and t == 0), stop=(a == PASSES - 1 and t == PACK - 1))

        def project_g(g_bank, a, h, c):
            project(g_bank, lambda a, t: wg_q[a][:, t * P:(t + 1) * P].bitcast(FP8X4),
                    lambda a, t: wg_sc[a][:, t * P:(t + 1) * P], a, h, c)

        def project_p(p_bank, a, h, c):
            project(p_bank, lambda a, t: w4[:, a, 2 * t * P:2 * (t + 1) * P].bitcast(FP4X4),
                    lambda a, t: sc[:, a, HALF + t * P:HALF + (t + 1) * P], a, h, c)

        h_bf = [kept("h_bf%d" % h, [P, HALF, PACK], BF16)[:] for h in range(HALVES)]
        h_q = [kept("h_q%d" % h, [P, HALF], U32) for h in range(HALVES)]
        h_sc = [kept("h_sc%d" % h, [P, HALF], U8) for h in range(HALVES)]

        def squash(g_bank):
            tanh = ring.tile([P, CHUNK, PACK], F32, name="tanh", bufs=6)
            nc.scalar.activation(out=tanh[:], in_=g_bank[:].rearrange("p t n -> p n t"), func=ACT.Tanh, scale=0.5)
            return tanh

        def gate(p_bank, tanh, h, c):
            nc.vector.scalar_tensor_tensor(out=h_bf[h][:, c * CHUNK:(c + 1) * CHUNK, :], in0=tanh[:], scalar=1.0,
                                           in1=p_bank[:].rearrange("p t n -> p n t"), op0=ALU.add, op1=ALU.mult)

        def quantise_h(h):
            nc.vector.quantize_mx(out=h_q[h][:].bitcast(FP8X4), scales=h_sc[h][:],
                                  in_=h_bf[h].rearrange("p i t -> p (i t)"))

        v2 = []
        dealt_sc = kept("dealt_sc", [P, PACK, GROUPS, P], U8)

        def gather_target_scales():
            picked = placed(wg_place, "picked_tgt_sc", [P, S2], U8, 0)
            nc.vector.tensor_copy(picked[:], tab2_sc[:].bitcast(U8).indirect(tgt_list[:]))
            nc.vector.tensor_copy(out=dealt_sc[:].rearrange("p t g (c m) -> p (g c) t m", m=16),
                                  in_=picked[:].rearrange("p (c m t) -> p c t m", m=16, t=PACK))

        def gather_targets(g, flat):
            dealt = flat[:].rearrange("p (t m) -> p t m", t=PACK)
            nc.vector.tensor_copy(dealt.rearrange("p t m -> p m t"),
                                  tab2[:].bitcast(U32).indirect(tgt_list[:, g * LIST_COLS:(g + 1) * LIST_COLS]))
            v2.append(dealt)

        y_sc = [kept("y_sc%d" % h, [P, GROUPS, HALF], U8) for h in range(HALVES)]
        woven = kept("woven", [P, PACK * HALF + WOVEN_SHIFT], BF16)

        def plan(n):
            h, g = UNITS[n]
            rows_out = out_0[g * PASS:(g + 1) * PASS, h * HALF:(h + 1) * HALF].rearrange("(p t) i -> p t i", t=PACK)
            if n == 0:
                y = placed(tab1_place, "y0", [P, PACK, HALF], F32, tab2_offset)[:]
            else:
                y = kept("y%d" % n, [P, PACK, HALF], F32)[:]
            direct = GPSIMD_SLICES[n] if n < len(GPSIMD_SLICES) else 0
            if direct:
                kern = kept("kern%d" % n, [P, direct, HALF], F32)
            for t in range(PACK):
                s_bank = bank(plan_bank(n, t), [P, HALF])
                nc.tensor.matmul_mx(out=s_bank[:], lhsT=v2[g][:, t, :].bitcast(FP8X4), lhsT_scale=v2_sc[:, t, g, :],
                                    rhs=h_q[h][:].bitcast(FP8X4), rhs_scale=h_sc[h][:], start=True, stop=True)
                bias = ln_tgt[:, PACK * g + t:PACK * g + t + 1]
                if t < direct:
                    nc.scalar.activation(out=kern[:, t, :], in_=s_bank[:], func=ACT.Exp, scale=0.5, bias=bias)
                    continue
                z = ring.tile([P, HALF], F32, name="z", bufs=Z_BUFS, align_bytes=64)
                nc.vector.scalar_tensor_tensor(out=z[:], in0=s_bank[:], scalar=0.5, in1=ln_src[:, h, :],
                                               op0=ALU.mult, op1=ALU.add)
                nc.scalar.activation(out=y[:, t, :], in_=z[:], func=ACT.Exp, bias=bias)
            if direct:
                nc.gpsimd.tensor_tensor(out=y[:, 0:direct, :], in0=kern[:],
                                        in1=src_first[:].unsqueeze(1).to_broadcast([P, direct, HALF]), op=ALU.mult)
            for t in list(range(direct, PACK)) + list(range(direct)):
                nc.sync.dma_start(out=rows_out[:, t, :], in_=y[:, t, :])
            return y

        def plan_bank(n, t):
            if n < 2:
                return 2 * t + 1
            return ((0, 2, 1, 3), (5, 7, 4, 6))[n % 2][t]

        def woven_unit(n):
            first = WOVEN_SHIFT * (n % 2)
            return woven[:, first:first + PACK * HALF]

        def weave(n, y):
            final = n == len(UNITS) - 1
            cols = SCALAR_COLS[n]
            outer, middle = (slice(HALF - cols, HALF), slice(0, HALF - cols)) if n % 2 else (slice(0, cols), slice(cols, HALF))
            y_bf = woven_unit(n).rearrange("p (i t) -> p i t", t=PACK)
            nc.scalar.copy(out=y_bf[:, outer, :].rearrange("p (c i) t -> p c t i", i=2),
                           in_=y[:, :, outer].rearrange("p t (c i) -> p c t i", i=2))
            if final:
                for run in (slice(0, HALF // 2), slice(HALF // 2, middle.stop)):
                    nc.vector.tensor_copy(out=y_bf[:, run, :].rearrange("p (c i) t -> p c t i", i=2),
                                          in_=y[:, :, run].rearrange("p t (c i) -> p c t i", i=2))
            else:
                nc.gpsimd.tensor_scalar(out=y_bf[:, middle, :], in0=y[:, :, middle].rearrange("p t i -> p i t"),
                                        scalar1=1.0, scalar2=0.0, op0=ALU.mult, op1=ALU.add)

        def quantise_y(n):
            h, g = UNITS[n]
            y_q = kept("y_q%d" % n, [P, HALF], U32)
            words_out = out_1[g].rearrange("p m t -> p (m t)").bitcast(I32)[:, h * HALF:(h + 1) * HALF]
            parts = [slice(0, HALF // 2), slice(HALF // 2, HALF)] if n == len(UNITS) - 1 else [slice(0, HALF)]
            for cols in parts:
                nc.vector.quantize_mx(out=y_q[:, cols].bitcast(FP8X4), scales=y_sc[h][:, g, cols],
                                      in_=woven_unit(n)[:, PACK * cols.start:PACK * cols.stop])
                nc.sync.dma_start(out=words_out[:, cols], in_=y_q[:, cols].bitcast(I32))

        def store_scales(h, queue):
            word_cols = slice(h * HALF // 4, (h + 1) * HALF // 4)
            for r in range(PACK):
                queue.dma_start(out=out_2.bitcast(I32)[:, r:BLOCKS:PACK, word_cols].rearrange("g q m -> q g m"),
                                in_=y_sc[h][r:P:QUAD, :, :].bitcast(I32))

        banks = [(bank(2 * c, [P, PACK, CHUNK]), bank(2 * c + 1, [P, PACK, CHUNK])) for c in range(CHUNKS)]
        last = PASSES - 1

        quantise_wg(0, P)
        gather_sources(0, 0, HALVES, "v0")
        gather_target_scales()
        for c in range(CHUNKS):
            project_p(banks[c][0], 0, 0, c)
            project_g(banks[c][1], 0, 0, c)

        quantise_wg(last, P)
        wg_raw[1] = load_wg(placed(late_place, "wg_raw1", [P, PACK, H], F32, 0), 1)
        tab.append(load_words(placed(late_place, "tab_last", [P, T], I32, 2 * T), tab_words[last]))
        gather_sources(1, 0, HALVES, "v1")
        tab2_offset = 4096
        tab2 = placed(tab1_place, "tab2", [P, T2], I32, tab2_offset)
        tab2_in = tab2_words[0].rearrange("p t i -> p (t i)").bitcast(I32)
        nc.sync.dma_start(out=tab2[:, 0:T2 // 2], in_=tab2_in[:, 0:T2 // 2])
        src_sc.append(placed(tab1_place, "sc_second", [P, PASSES, HALF], U8, 2048))
        spread_planes(src_sc[1], sc_rows_second)
        nc.sync.dma_start(out=tab2[:, T2 // 2:T2], in_=tab2_in[:, T2 // 2:T2])
        v2_sc = placed(tab1_place, "v2_sc", [P, PACK, GROUPS, P], U8, 0)
        for r in range(PACK):
            nc.sync.dma_start(out=v2_sc[r:P:QUAD].bitcast(I32), in_=dealt_sc[TGT_SC_ROW0 + TGT_SC_STEP * r:P:QUAD].bitcast(I32))
        for c in range(CHUNKS):
            project_p(banks[c][0], 1, 0, c)
        quantise_wg(1, P)
        for c in range(CHUNKS):
            project_g(banks[c][1], 1, 0, c)

        picked = kept("v2_first", [P, HALF], U32)
        for piece in range(2):
            nc.vector.tensor_copy(picked[:, piece * HALF // 2:(piece + 1) * HALF // 2],
                                  tab[last][:].bitcast(U32).indirect(src_list[:, piece * LIST_COLS // 2:(piece + 1) * LIST_COLS // 2]))
        v[last, 0] = picked[:]
        gather_sources(last, 1, HALVES, "v2_second")
        project_g(banks[0][1], last, 0, 0)
        for c in range(CHUNKS):
            if c + 1 < CHUNKS:
                project_g(banks[c + 1][1], last, 0, c + 1)
            project_p(banks[c][0], last, 0, c)
            gate(banks[c][0], squash(banks[c][1]), 0, c)
        gather_targets(0, kept("tgt_words0", [P, PASS], U32))
        quantise_h(0)

        tanh_second = []

        def second_half_g(c):
            g_bank = bank(2 * c + 1, [P, PACK, CHUNK])
            for a in range(PASSES):
                project_g(g_bank, a, 1, c)
            tanh_second.append(squash(g_bank))

        def second_half_p(c):
            p_bank = bank(2 * c, [P, PACK, CHUNK])
            for a in range(PASSES):
                project_p(p_bank, a, 1, c)
            gate(p_bank, tanh_second[c], 1, c)

        rest = kept("tgt_words_rest", [P, GROUPS - 1, PACK, P], U32)
        nc.vector.tensor_copy(rest[:].rearrange("p g t m -> p g m t"),
                              tab2[:].bitcast(U32).indirect(tgt_list[:, LIST_COLS:GROUPS * LIST_COLS]))
        v2.extend(rest[:, g] for g in range(GROUPS - 1))
        for c in range(CHUNKS):
            second_half_g(c)
        ys = [plan(0)]
        second_half_p(0)
        second_half_p(1)
        ys.append(plan(1))
        weave(0, ys[0])
        second_half_p(2)
        second_half_p(3)
        quantise_y(0)
        quantise_h(1)
        for n in range(2, len(UNITS)):
            weave(n - 1, ys[n - 1])
            ys.append(plan(n))
            quantise_y(n - 1)
            if n == GROUPS:
                store_scales(0, nc.sync)
        weave(len(UNITS) - 1, ys[-1])
        quantise_y(len(UNITS) - 1)
        store_scales(1, nc.sync)
